import numpy as np
import ml_dtypes


def mxq(x, axis, fmt="e4m3"):
    dtype, down = {"e4m3": (ml_dtypes.float8_e4m3fn, 7), "e5m2": (ml_dtypes.float8_e5m2, 14)}[fmt]
    v = np.moveaxis(np.asarray(x, np.float32).astype(ml_dtypes.bfloat16).astype(np.float64), axis, -1)
    blocks = v.reshape(v.shape[:-1] + (-1, 32))
    amax = np.abs(blocks).max(-1, keepdims=True)
    byte = np.maximum(np.where(amax > 0, np.frexp(amax)[1] - 1 + 127, 0) - down, 1)
    scale = np.exp2(byte - 127.0)
    codes = (blocks / scale).astype(np.float32).astype(dtype).astype(np.float64)
    return np.moveaxis((codes * scale).reshape(v.shape), -1, axis)


WIDE = False


def mx_kscale(k):
    if not WIDE:
        return np.ones(k)
    levels = np.array([10, -10, 5, -5, 0])
    if k % 512:
        return np.exp2(np.random.permutation(np.resize(levels, k // 32))).repeat(32)
    a = np.empty((k // 512, 16))
    for p in range(k // 512):
        a[p, :8] = np.random.permutation(np.resize(levels, 8))
        for g in range(8):
            far = levels[np.abs(levels - a[p, g]) >= 10]
            a[p, g + 8] = far[np.random.randint(len(far))]
    return np.exp2(a.ravel()).repeat(32)


def f64(x):
    return np.asarray(x).astype(np.float64)


def striped(idx):
    return np.tile(idx.reshape(-1, 16).T, (8, 1)).astype(np.uint16)


def unstriped(offs):
    return offs[:16].T.reshape(-1).astype(np.int64)


E2M1 = np.array([0.0, 0.5, 1.0, 1.5, 2.0, 3.0, 4.0, 6.0, -0.0, -0.5, -1.0, -1.5, -2.0, -3.0, -4.0, -6.0])


def pack_weight(w, fmt):
    k, n = w.shape
    w = f64(np.asarray(w, np.float32).astype(ml_dtypes.bfloat16)).reshape(k // 32, 32, n)
    amax = np.abs(w).max(1)
    if fmt == "e4m3":
        byte = np.frexp(amax)[1] - 1 + 127 - 7
    else:
        mant, ex = np.frexp(amax / 6.0)
        byte = np.where(mant > 0.5, ex, ex - 1) + 127
    byte = np.clip(np.where(amax > 0, byte, 1), 1, 254)
    scaled = (w * np.exp2(127.0 - byte)[:, None, :]).reshape(k, n).astype(np.float32)
    by_word = np.ascontiguousarray(scaled.reshape(k // 512, 128, 4, n).transpose(0, 1, 3, 2))
    if fmt == "e4m3":
        words = by_word.astype(ml_dtypes.float8_e4m3fn).view(np.uint8)
    else:
        c = by_word.astype(ml_dtypes.float4_e2m1fn).view(np.uint8) & 0xF
        words = (c[..., 0::2] | (c[..., 1::2] << 4)).reshape(k // 512, 128, 2 * n)
    return np.ascontiguousarray(words), np.ascontiguousarray(byte.astype(np.uint8).reshape(k // 512, 16, n))


def unpack_weight(words, scales, fmt):
    g, _, n = scales.shape
    words = np.ascontiguousarray(words).reshape(g, 128, n, -1)
    if fmt == "e4m3":
        vals = words.view(ml_dtypes.float8_e4m3fn).astype(np.float64)
    else:
        nib = np.empty((g, 128, n, 4), np.uint8)
        nib[..., 0::2] = words & 0xF
        nib[..., 1::2] = words >> 4
        vals = E2M1[nib]
    vals = vals * np.repeat(np.exp2(scales.astype(np.float64) - 127.0), 8, axis=1)[..., None]
    return vals.transpose(0, 1, 3, 2).reshape(g * 512, n)


def gelu(v):
    return 0.5 * v * (1.0 + np.tanh(np.sqrt(2.0 / np.pi) * (v + 0.044715 * v**3)))


K, H, N, T, S, T2, P = 1024, 1024, 512, 2048, 1024, 2048, 1024


def setup_inputs():
    n = np.random.standard_normal
    s = mx_kscale(K)[:, None]
    u = mx_kscale(H)[:, None]
    tab_words, tab_scales = pack_weight(n((K, T)) * s, "e4m3")
    w2_words, w2_scales = pack_weight(n((H, N)) / np.sqrt(H) / u, "e2m1")
    return {
        "tab_words": tab_words,
        "tab_scales": tab_scales,
        "offs": striped(np.random.permutation(T)[:S]),
        "offs2": striped(np.random.permutation(T2)[:S]),
        "offs3": striped(np.random.permutation(T2)[:P]),
        "offs4": striped(np.random.permutation(T2)[:P]),
        "w1": (0.45 * n((K, H)) / np.sqrt(K) / s).astype(np.float32),
        "wgs": np.exp(0.3 * n((128, S))).astype(np.float32),
        "gain": (3.5 * np.exp(0.3 * n(H)) * u[:, 0]).astype(np.float32),
        "aniso": (0.7 * n((H, P)) * u).astype(np.float32),
        "w2_words": w2_words,
        "w2_scales": w2_scales,
        "w3": (n((H, N)) / np.sqrt(H) / u).astype(np.float32),
    }


def reference(tab_words, tab_scales, offs, offs2, offs3, offs4, w1, wgs, gain, aniso, w2_words, w2_scales, w3):
    v = unpack_weight(tab_words, tab_scales, "e4m3")[:, unstriped(offs)]
    h = np.sin(mxq(f64(w1), 0, "e4m3").T @ v)
    page = np.zeros((H, T2))
    page[:, unstriped(offs2)] = np.tile(f64(wgs), (H // 128, 1)) * h
    x1 = page[:, unstriped(offs3)]
    x2 = page[:, unstriped(offs4)]
    z = f64(gain)[:, None] * (x1 * x2) + f64(aniso)
    zq = mxq(z, 0, "e4m3")
    y2 = unpack_weight(w2_words, w2_scales, "e2m1").T @ zq
    y3 = mxq(f64(w3), 0, "e4m3").T @ zq
    return np.maximum(y2, y3)

@@ -1,0 +1,253 @@
+from contextlib import ExitStack
+
+import concourse.mybir as mybir
+from concourse.masks import make_identity
+
+K, H, N, T, S, T2, M = 1024, 1024, 512, 2048, 1024, 2048, 1024
+FLOPS = 2 * K * H * S + 2 * 2 * H * N * M
+
+F32 = mybir.dt.float32
+BF16 = mybir.dt.bfloat16
+I32 = mybir.dt.int32
+U32 = mybir.dt.uint32
+U16 = mybir.dt.uint16
+U8 = mybir.dt.uint8
+FP8X4 = mybir.dt.float8_e4m3fn_x4
+FP4X4 = mybir.dt.float4_e2m1fn_x4
+MULT = mybir.AluOpType.mult
+MAX = mybir.AluOpType.max
+SIN = mybir.ActivationFunctionType.Sin
+
+P = 128
+PACK = 4
+K_PASS = P * PACK
+PASSES = 2
+BANK = 512
+ROW_TILES = H // P
+OUT_TILES = N // P
+W1_WIDTHS = (128, 128, 256, 512)
+BOND_WIDTHS = (256, 256, 256, 128, 128)
+VECTOR_PAGES = 2
+
+
+def tile_list_garnet_bond_maximum_kernel(
+    tc, tab_words, tab_scales, offs, offs2, offs3, offs4, w1, wgs, gain, aniso, w2_words, w2_scales, w3, out
+):
+    nc = tc.nc
+    with ExitStack() as ctx:
+        held = ctx.enter_context(tc.tile_pool(name="held", bufs=1))
+        ring = ctx.enter_context(tc.tile_pool(name="ring", bufs=2))
+        psum = ctx.enter_context(tc.psum_pool(name="psum", bufs=2))
+
+        def load_list(name, dram):
+            tile = held.tile([P, S // 16], U16, name=name)
+            nc.sync.dma_start(tile[:], dram)
+            return tile
+
+        def entries(tile, start, count):
+            return tile[:, start // 16 : (start + count) // 16]
+
+        def load_rows(w, a, c0, width, name, pool, tag, bufs):
+            raw = pool.tile([P, PACK, width], F32, name=name, tag=tag, bufs=bufs)
+            nc.sync.dma_start(
+                raw[:], w[a * K_PASS : (a + 1) * K_PASS, c0 : c0 + width].rearrange("(p i) c -> p i c", i=PACK)
+            )
+            return raw
+
+        def quantize_weight(raws, width, name):
+            grouped = ring.tile([P, PASSES, width, PACK], BF16, name=name + "_bf16", tag="grouped", align_bytes=64)
+            for a in range(PASSES):
+                nc.scalar.copy(
+                    grouped[:, a].rearrange("p (c q) i -> p c i q", q=4),
+                    raws[a][:].rearrange("p i (c q) -> p c i q", q=4),
+                )
+            codes = held.tile([P, PASSES * width], U32, name=name + "_codes", align_bytes=64)
+            scales = held.tile([P, PASSES * width], U8, name=name + "_scales", align_bytes=64)
+            nc.vector.quantize_mx(
+                out=codes[:].bitcast(FP8X4), scales=scales[:], in_=grouped[:].rearrange("p a c i -> p (a c i)")
+            )
+            return codes, scales
+
+        tab_plane = held.tile([P, T], U8, name="tab_plane")
+        nc.vector.memset(tab_plane[:].bitcast(I32), 0)
+        spin_list = load_list("spin_list", offs)
+        tab = [held.tile([P, T], I32, name="tab%d" % a) for a in range(PASSES)]
+        nc.sync.dma_start(tab[0][:], tab_words[0].rearrange("p t i -> p (t i)").bitcast(I32))
+        for q in range(4):
+            nc.sync.dma_start(
+                tab_plane[32 * q : 32 * q + 4 * PASSES, :].bitcast(I32),
+                tab_scales[:, 4 * q : 4 * q + 4, :].bitcast(I32),
+            )
+        w1_starts = [sum(W1_WIDTHS[:c]) for c in range(len(W1_WIDTHS))]
+        w1_raw = {}
+
+        def load_w1(c):
+            big = W1_WIDTHS[c] == BANK
+            w1_raw[c] = [
+                load_rows(
+                    w1, a, w1_starts[c], W1_WIDTHS[c], "w1_raw%d_%d" % (c, a),
+                    ring if big else held, "staged" if big else "w1_raw%d_%d" % (c, a), 3 if big else 1,
+                )
+                for a in range(PASSES)
+            ]
+
+        load_w1(0)
+        nc.sync.dma_start(tab[1][:], tab_words[1].rearrange("p t i -> p (t i)").bitcast(I32))
+        site_list = load_list("site_list", offs2)
+        wgs_sb = held.tile([P, S], F32, name="wgs_sb")
+        nc.sync.dma_start(wgs_sb[:], wgs)
+        for c in range(1, len(W1_WIDTHS)):
+            load_w1(c)
+
+        identity = held.tile([P, P], F32, name="identity")
+        make_identity(nc, identity[:])
+        gain_rows = held.tile([P, P], F32, name="gain_rows")
+        nc.gpsimd.memset(gain_rows[:], 0.0)
+        w2_plane = held.tile([P, PASSES, N], U8, name="w2_plane", align_bytes=64)
+        nc.gpsimd.memset(w2_plane[:].rearrange("p a n -> p (a n)").bitcast(I32), 0)
+        pages = [held.tile([P, T2], F32, name="page%d" % t) for t in range(ROW_TILES)]
+        for t in range(ROW_TILES):
+            if t < VECTOR_PAGES:
+                nc.vector.memset(pages[t][:], 0.0)
+            else:
+                for half in range(2):
+                    nc.gpsimd.memset(pages[t][:, half * (T2 // 2) : (half + 1) * (T2 // 2)], 0.0)
+
+        v_scales = held.tile([P, S], U8, name="v_scales", align_bytes=64)
+        nc.vector.tensor_copy(v_scales[:], tab_plane[:].indirect(spin_list[:]))
+        v_codes = [held.tile([P, S], U32, name="v_codes%d" % a, align_bytes=64) for a in range(PASSES)]
+        nc.vector.tensor_copy(v_codes[0][:], tab[0][:].bitcast(U32).indirect(spin_list[:]))
+        w1_q = {0: quantize_weight(w1_raw[0], W1_WIDTHS[0], "w1_0")}
+        for j0 in range(0, S, BANK):
+            nc.vector.tensor_copy(
+                v_codes[1][:, j0 : j0 + BANK], tab[1][:].bitcast(U32).indirect(entries(spin_list, j0, BANK))
+            )
+
+        later = {}
+        for t in range(ROW_TILES):
+            c = max(i for i in range(len(W1_WIDTHS)) if w1_starts[i] <= t * P)
+            codes, scales = w1_q[c]
+            h = ring.tile([P, S], F32, name="h", bufs=3)
+            for j0 in range(0, S, BANK):
+                acc = psum.tile([P, BANK], F32, name="angles", tag="sums", bufs=4)
+                for a in range(PASSES):
+                    col = a * W1_WIDTHS[c] + t * P - w1_starts[c]
+                    nc.tensor.matmul_mx(
+                        out=acc[:],
+                        lhsT=codes[:, col : col + P].bitcast(FP8X4),
+                        lhsT_scale=scales[:, col : col + P],
+                        rhs=v_codes[a][:, j0 : j0 + BANK].bitcast(FP8X4),
+                        rhs_scale=v_scales[4 * a :, j0 : j0 + BANK],
+                        start=(a == 0),
+                        stop=(a == PASSES - 1),
+                    )
+                nc.scalar.activation(h[:, j0 : j0 + BANK], acc[:], SIN)
+            step = BANK if t == 0 else S
+            for j0 in range(0, S, step):
+                nc.vector.tensor_tensor(
+                    pages[t][:].indirect(entries(site_list, j0, step)),
+                    h[:, j0 : j0 + step],
+                    wgs_sb[:, j0 : j0 + step],
+                    MULT,
+                )
+            if t + 1 < len(W1_WIDTHS):
+                w1_q[t + 1] = quantize_weight(w1_raw[t + 1], W1_WIDTHS[t + 1], "w1_%d" % (t + 1))
+            if t == 3:
+                w3_raw = [load_rows(w3, a, 0, N, "w3_raw%d" % a, ring, "staged", 3) for a in range(PASSES)]
+                later["w3"] = quantize_weight(w3_raw, N, "w3")
+
+        w3_codes, w3_scales = later["w3"]
+        end1_list = load_list("end1_list", offs3)
+        end2_list = load_list("end2_list", offs4)
+        w2_codes = held.tile([P, PASSES, 2 * N], U8, name="w2_codes", align_bytes=64)
+        nc.sync.dma_start(w2_codes[:].bitcast(I32), w2_words.rearrange("a p b -> p a b").bitcast(I32))
+        for q in range(4):
+            nc.sync.dma_start(
+                w2_plane[32 * q : 32 * q + 4].bitcast(I32),
+                w2_scales[:, 4 * q : 4 * q + 4, :].rearrange("a r n -> r a n").bitcast(I32),
+            )
+        nc.sync.dma_start(gain_rows[0:ROW_TILES, :], gain.rearrange("(t p) -> t p", p=P))
+        gain_cols = psum.tile([P, P], F32, name="gain_cols", tag="words")
+        nc.tensor.transpose(gain_cols[:], gain_rows[:], identity[:])
+        widest = max(BOND_WIDTHS)
+        gain_wide = held.tile([P, ROW_TILES, widest], F32, name="gain_wide")
+        nc.scalar.copy(gain_wide[:], gain_cols[:, 0:ROW_TILES].unsqueeze(2).to_broadcast([P, ROW_TILES, widest]))
+
+        out_view = out.rearrange("(t p) m -> p t m", p=P)
+        m0 = 0
+        for width in BOND_WIDTHS:
+            blocks = width // P
+            an = ring.tile([P, ROW_TILES, width], F32, name="an", tag="staged", bufs=3)
+            nc.sync.dma_start(an[:], aniso[:, m0 : m0 + width].rearrange("(t p) m -> p t m", p=P))
+            x1 = []
+            for t in range(ROW_TILES):
+                x = held.tile([P, width], F32, name="x1_%d" % t)
+                nc.vector.tensor_tensor(
+                    x[:], pages[t][:].indirect(entries(end1_list, m0, width)), gain_wide[:, t, 0:width], MULT
+                )
+                x1.append(x)
+            prod = []
+            for t in range(ROW_TILES):
+                x = held.tile([P, width], F32, name="prod_%d" % t)
+                nc.vector.tensor_tensor(x[:], pages[t][:].indirect(entries(end2_list, m0, width)), x1[t][:], MULT)
+                prod.append(x)
+            z_q = []
+            for a in range(PASSES):
+                words = psum.tile([P, blocks, 2, P], F32, name="words", tag="words")
+                for b in range(blocks):
+                    cols = slice(b * P, (b + 1) * P)
+                    zt = psum.tile([P, PACK, P], F32, name="zt")
+                    terms = [an[:, PACK * a + i, cols] for i in range(PACK)]
+                    terms = terms + [prod[PACK * a + i][:, cols] for i in range(PACK)]
+                    for n, term in enumerate(terms):
+                        nc.tensor.matmul(
+                            zt[:, n % PACK, :], term, identity[:],
+                            start=(n == 0), stop=(n == len(terms) - 1), is_transpose=True,
+                        )
+                    zt_bf = ring.tile([P, K_PASS], BF16, name="zt_bf", bufs=3)
+                    nc.scalar.copy(
+                        zt_bf[:].rearrange("m (u p e) -> m u p e", u=2, e=2),
+                        zt[:].rearrange("m i r -> m (i r)").rearrange("m (p u e) -> m u p e", u=2, e=2),
+                    )
+                    for u in range(2):
+                        nc.tensor.transpose(
+                            words[:, b, u, :], zt_bf[:].bitcast(F32)[:, u * P : (u + 1) * P], identity[:]
+                        )
+                z_bf = ring.tile([P, width * PACK], BF16, name="z_bf", align_bytes=64)
+                nc.scalar.copy(
+                    z_bf[:].bitcast(F32).rearrange("p (b m u) -> p b m u", b=blocks, u=2),
+                    words[:].rearrange("p b u m -> p b m u"),
+                )
+                z_codes = ring.tile([P, width], U32, name="z_codes", bufs=4, align_bytes=64)
+                z_scales = ring.tile([P, width], U8, name="z_scales", bufs=4, align_bytes=64)
+                nc.vector.quantize_mx(out=z_codes[:].bitcast(FP8X4), scales=z_scales[:], in_=z_bf[:])
+                z_q.append((z_codes, z_scales))
+            for b in range(blocks):
+                cols = slice(b * P, (b + 1) * P)
+                y2 = psum.tile([P, OUT_TILES, P], F32, name="y2", tag="sums", bufs=4)
+                y3 = psum.tile([P, OUT_TILES, P], F32, name="y3", tag="sums", bufs=4)
+                for a in range(PASSES):
+                    z_codes, z_scales = z_q[a]
+                    for y in (y2, y3):
+                        for n in range(OUT_TILES):
+                            if y is y2:
+                                lhs = w2_codes[:, a, 2 * n * P : 2 * (n + 1) * P].bitcast(FP4X4)
+                                lhs_scale = w2_plane[:, a, n * P : (n + 1) * P]
+                            else:
+                                lhs = w3_codes[:, a * N + n * P : a * N + (n + 1) * P].bitcast(FP8X4)
+                                lhs_scale = w3_scales[:, a * N + n * P : a * N + (n + 1) * P]
+                            nc.tensor.matmul_mx(
+                                out=y[:, n, :],
+                                lhsT=lhs,
+                                lhsT_scale=lhs_scale,
+                                rhs=z_codes[:, cols].bitcast(FP8X4),
+                                rhs_scale=z_scales[:, cols],
+                                start=(a == 0 and n == 0),
+                                stop=(a == PASSES - 1 and n == OUT_TILES - 1),
+                            )
+                y2_sb = ring.tile([P, OUT_TILES, P], F32, name="y2_sb")
+                nc.scalar.copy(y2_sb[:], y2[:])
+                best = ring.tile([P, OUT_TILES, P], F32, name="best")
+                nc.vector.tensor_tensor(best[:], y3[:], y2_sb[:], MAX)
+                nc.sync.dma_start(out_view[:, :, m0 + b * P : m0 + (b + 1) * P], best[:])
+            m0 = m0 + width

@@ -16,6 +16,7 @@ FP8X4 = mybir.dt.float8_e4m3fn_x4
 FP4X4 = mybir.dt.float4_e2m1fn_x4
 MULT = mybir.AluOpType.mult
 MAX = mybir.AluOpType.max
+COPY = mybir.ActivationFunctionType.Copy
 SIN = mybir.ActivationFunctionType.Sin
 
 P = 128
@@ -26,8 +27,8 @@ BANK = 512
 ROW_TILES = H // P
 OUT_TILES = N // P
 W1_WIDTHS = (128, 128, 256, 512)
-BOND_WIDTHS = (256, 256, 256, 128, 128)
-VECTOR_PAGES = 2
+END1_WIDTH = 256
+PAGES = 4
 
 
 def tile_list_garnet_bond_maximum_kernel(
@@ -54,8 +55,8 @@ def tile_list_garnet_bond_maximum_kernel(
             )
             return raw
 
-        def quantize_weight(raws, width, name):
-            grouped = ring.tile([P, PASSES, width, PACK], BF16, name=name + "_bf16", tag="grouped", align_bytes=64)
+        def quantize_weight(raws, width, name, tag):
+            grouped = held.tile([P, PASSES, width, PACK], BF16, name=name + "_bf16", tag=tag, align_bytes=64)
             for a in range(PASSES):
                 nc.scalar.copy(
                     grouped[:, a].rearrange("p (c q) i -> p c i q", q=4),
@@ -93,10 +94,11 @@ def tile_list_garnet_bond_maximum_kernel(
 
         load_w1(0)
         nc.sync.dma_start(tab[1][:], tab_words[1].rearrange("p t i -> p (t i)").bitcast(I32))
+        load_w1(1)
         site_list = load_list("site_list", offs2)
         wgs_sb = held.tile([P, S], F32, name="wgs_sb")
         nc.sync.dma_start(wgs_sb[:], wgs)
-        for c in range(1, len(W1_WIDTHS)):
+        for c in range(2, len(W1_WIDTHS)):
             load_w1(c)
 
         identity = held.tile([P, P], F32, name="identity")
@@ -105,26 +107,30 @@ def tile_list_garnet_bond_maximum_kernel(
         nc.gpsimd.memset(gain_rows[:], 0.0)
         w2_plane = held.tile([P, PASSES, N], U8, name="w2_plane", align_bytes=64)
         nc.gpsimd.memset(w2_plane[:].rearrange("p a n -> p (a n)").bitcast(I32), 0)
-        pages = [held.tile([P, T2], F32, name="page%d" % t) for t in range(ROW_TILES)]
-        for t in range(ROW_TILES):
-            if t < VECTOR_PAGES:
-                nc.vector.memset(pages[t][:], 0.0)
-            else:
-                for half in range(2):
-                    nc.gpsimd.memset(pages[t][:, half * (T2 // 2) : (half + 1) * (T2 // 2)], 0.0)
+        pages = [held.tile([P, T2], F32, name="page%d" % t) for t in range(PAGES)]
+        for page in pages:
+            nc.vector.memset(page[:].bitcast(I32), 0)
 
         v_scales = held.tile([P, S], U8, name="v_scales", align_bytes=64)
         nc.vector.tensor_copy(v_scales[:], tab_plane[:].indirect(spin_list[:]))
         v_codes = [held.tile([P, S], U32, name="v_codes%d" % a, align_bytes=64) for a in range(PASSES)]
         nc.vector.tensor_copy(v_codes[0][:], tab[0][:].bitcast(U32).indirect(spin_list[:]))
-        w1_q = {0: quantize_weight(w1_raw[0], W1_WIDTHS[0], "w1_0")}
+        w1_q = {0: quantize_weight(w1_raw[0], W1_WIDTHS[0], "w1_0", "w1_0")}
         for j0 in range(0, S, BANK):
             nc.vector.tensor_copy(
                 v_codes[1][:, j0 : j0 + BANK], tab[1][:].bitcast(U32).indirect(entries(spin_list, j0, BANK))
             )
 
-        later = {}
-        for t in range(ROW_TILES):
+        w1_q[1] = quantize_weight(w1_raw[1], W1_WIDTHS[1], "w1_1", "x1_0")
+        end1_list = load_list("end1_list", offs3)
+        end2_list = load_list("end2_list", offs4)
+        nc.sync.dma_start(gain_rows[0:ROW_TILES, :], gain.rearrange("(t p) -> t p", p=P))
+        gain_psum = psum.tile([P, P], F32, name="gain_psum", tag="words")
+        nc.tensor.transpose(gain_psum[:], gain_rows[:], identity[:])
+        gain_cols = held.tile([P, ROW_TILES], F32, name="gain_cols")
+        nc.scalar.copy(gain_cols[:], gain_psum[:, 0:ROW_TILES])
+
+        def sines_to_page(t):
             c = max(i for i in range(len(W1_WIDTHS)) if w1_starts[i] <= t * P)
             codes, scales = w1_q[c]
             h = ring.tile([P, S], F32, name="h", bufs=3)
@@ -145,20 +151,77 @@ def tile_list_garnet_bond_maximum_kernel(
             step = BANK if t == 0 else S
             for j0 in range(0, S, step):
                 nc.vector.tensor_tensor(
-                    pages[t][:].indirect(entries(site_list, j0, step)),
+                    pages[t % PAGES][:].indirect(entries(site_list, j0, step)),
                     h[:, j0 : j0 + step],
                     wgs_sb[:, j0 : j0 + step],
                     MULT,
                 )
-            if t + 1 < len(W1_WIDTHS):
-                w1_q[t + 1] = quantize_weight(w1_raw[t + 1], W1_WIDTHS[t + 1], "w1_%d" % (t + 1))
-            if t == 3:
-                w3_raw = [load_rows(w3, a, 0, N, "w3_raw%d" % a, ring, "staged", 3) for a in range(PASSES)]
-                later["w3"] = quantize_weight(w3_raw, N, "w3")
 
-        w3_codes, w3_scales = later["w3"]
-        end1_list = load_list("end1_list", offs3)
-        end2_list = load_list("end2_list", offs4)
+        def first_end(x1, t, m0, width):
+            nc.vector.tensor_copy(x1, pages[t % PAGES][:].indirect(entries(end1_list, m0, width)))
+            nc.scalar.activation(x1, x1, COPY, scale=gain_cols[:, t : t + 1])
+
+        def second_end(prod, x1, t, m0, width):
+            nc.vector.tensor_tensor(prod, pages[t % PAGES][:].indirect(entries(end2_list, m0, width)), x1, MULT)
+
+        def load_aniso(a, m0, width):
+            an = ring.tile([P, PACK, width], F32, name="an", tag="staged", bufs=3)
+            nc.sync.dma_start(
+                an[:], aniso[a * K_PASS : (a + 1) * K_PASS, m0 : m0 + width].rearrange("(i p) m -> p i m", p=P)
+            )
+            return an
+
+        def round_z(z_bf, an, prod, width):
+            blocks = width // P
+            words = psum.tile([P, blocks, 2, P], F32, name="words", tag="words")
+            for b in range(blocks):
+                cols = slice(b * P, (b + 1) * P)
+                zt = psum.tile([P, PACK, P], F32, name="zt")
+                terms = [an[:, i, cols] for i in range(PACK)] + [prod[i][:, cols] for i in range(PACK)]
+                for n, term in enumerate(terms):
+                    nc.tensor.matmul(
+                        zt[:, n % PACK, :], term, identity[:],
+                        start=(n == 0), stop=(n == len(terms) - 1), is_transpose=True,
+                    )
+                zt_bf = ring.tile([P, K_PASS], BF16, name="zt_bf", bufs=3)
+                nc.scalar.copy(
+                    zt_bf[:].rearrange("m (u p e) -> m u p e", u=2, e=2),
+                    zt[:].rearrange("m i r -> m (i r)").rearrange("m (p u e) -> m u p e", u=2, e=2),
+                )
+                for u in range(2):
+                    nc.tensor.transpose(words[:, b, u, :], zt_bf[:].bitcast(F32)[:, u * P : (u + 1) * P], identity[:])
+            nc.scalar.copy(
+                z_bf.bitcast(F32).rearrange("p (b m u) -> p b m u", b=blocks, u=2),
+                words[:].rearrange("p b u m -> p b m u"),
+            )
+
+        x1 = {}
+        prod = [held.tile([P, M], F32, name="prod_%d" % i) for i in range(PACK)]
+
+        def whole_first_end(t):
+            x1[t] = held.tile([P, M], F32, name="x1_%d" % t, align_bytes=64)
+            first_end(x1[t][:], t, 0, M)
+
+        def whole_second_end(t):
+            second_end(prod[t][:], x1[t][:], t, 0, M)
+
+        sines_to_page(0)
+        w1_q[2] = quantize_weight(w1_raw[2], W1_WIDTHS[2], "w1_2", "x1_0")
+        sines_to_page(1)
+        whole_first_end(0)
+        whole_first_end(1)
+        sines_to_page(2)
+        w1_q[3] = quantize_weight(w1_raw[3], W1_WIDTHS[3], "w1_3", "x1_2")
+        whole_second_end(0)
+        sines_to_page(3)
+        whole_first_end(2)
+        whole_second_end(1)
+        whole_first_end(3)
+        whole_second_end(2)
+        sines_to_page(4)
+        whole_second_end(3)
+        w3_raw = [load_rows(w3, a, 0, N, "w3_raw%d" % a, ring, "staged", 3) for a in range(PASSES)]
+        w3_codes, w3_scales = quantize_weight(w3_raw, N, "w3", "w3_bf16")
         w2_codes = held.tile([P, PASSES, 2 * N], U8, name="w2_codes", align_bytes=64)
         nc.sync.dma_start(w2_codes[:].bitcast(I32), w2_words.rearrange("a p b -> p a b").bitcast(I32))
         for q in range(4):
@@ -166,68 +229,66 @@ def tile_list_garnet_bond_maximum_kernel(
                 w2_plane[32 * q : 32 * q + 4].bitcast(I32),
                 w2_scales[:, 4 * q : 4 * q + 4, :].rearrange("a r n -> r a n").bitcast(I32),
             )
-        nc.sync.dma_start(gain_rows[0:ROW_TILES, :], gain.rearrange("(t p) -> t p", p=P))
-        gain_cols = psum.tile([P, P], F32, name="gain_cols", tag="words")
-        nc.tensor.transpose(gain_cols[:], gain_rows[:], identity[:])
-        widest = max(BOND_WIDTHS)
-        gain_wide = held.tile([P, ROW_TILES, widest], F32, name="gain_wide")
-        nc.scalar.copy(gain_wide[:], gain_cols[:, 0:ROW_TILES].unsqueeze(2).to_broadcast([P, ROW_TILES, widest]))
+        for t in range(PACK + 1, ROW_TILES - 1):
+            sines_to_page(t)
+        z0_bf = held.tile([P, M * PACK], BF16, name="z0_bf", align_bytes=64)
+        for m0 in range(0, M, BANK):
+            an = load_aniso(0, m0, BANK)
+            for d in range(0, BANK, 2 * P):
+                round_z(
+                    z0_bf[:, (m0 + d) * PACK : (m0 + d + 2 * P) * PACK],
+                    an[:, :, d : d + 2 * P],
+                    [x[:, m0 + d : m0 + d + 2 * P] for x in prod],
+                    2 * P,
+                )
+        sines_to_page(ROW_TILES - 1)
+        z0_codes = held.tile([P, M], U32, name="z0_codes", align_bytes=64)
+        z0_scales = held.tile([P, M], U8, name="z0_scales", align_bytes=64)
+        nc.vector.quantize_mx(out=z0_codes[:].bitcast(FP8X4), scales=z0_scales[:], in_=z0_bf[:])
 
         out_view = out.rearrange("(t p) m -> p t m", p=P)
-        m0 = 0
-        for width in BOND_WIDTHS:
-            blocks = width // P
-            an = ring.tile([P, ROW_TILES, width], F32, name="an", tag="staged", bufs=3)
-            nc.sync.dma_start(an[:], aniso[:, m0 : m0 + width].rearrange("(t p) m -> p t m", p=P))
-            x1 = []
-            for t in range(ROW_TILES):
-                x = held.tile([P, width], F32, name="x1_%d" % t)
-                nc.vector.tensor_tensor(
-                    x[:], pages[t][:].indirect(entries(end1_list, m0, width)), gain_wide[:, t, 0:width], MULT
-                )
-                x1.append(x)
-            prod = []
-            for t in range(ROW_TILES):
-                x = held.tile([P, width], F32, name="prod_%d" % t)
-                nc.vector.tensor_tensor(x[:], pages[t][:].indirect(entries(end2_list, m0, width)), x1[t][:], MULT)
-                prod.append(x)
-            z_q = []
-            for a in range(PASSES):
-                words = psum.tile([P, blocks, 2, P], F32, name="words", tag="words")
-                for b in range(blocks):
-                    cols = slice(b * P, (b + 1) * P)
-                    zt = psum.tile([P, PACK, P], F32, name="zt")
-                    terms = [an[:, PACK * a + i, cols] for i in range(PACK)]
-                    terms = terms + [prod[PACK * a + i][:, cols] for i in range(PACK)]
-                    for n, term in enumerate(terms):
-                        nc.tensor.matmul(
-                            zt[:, n % PACK, :], term, identity[:],
-                            start=(n == 0), stop=(n == len(terms) - 1), is_transpose=True,
-                        )
-                    zt_bf = ring.tile([P, K_PASS], BF16, name="zt_bf", bufs=3)
-                    nc.scalar.copy(
-                        zt_bf[:].rearrange("m (u p e) -> m u p e", u=2, e=2),
-                        zt[:].rearrange("m i r -> m (i r)").rearrange("m (p u e) -> m u p e", u=2, e=2),
-                    )
-                    for u in range(2):
-                        nc.tensor.transpose(
-                            words[:, b, u, :], zt_bf[:].bitcast(F32)[:, u * P : (u + 1) * P], identity[:]
-                        )
-                z_bf = ring.tile([P, width * PACK], BF16, name="z_bf", align_bytes=64)
-                nc.scalar.copy(
-                    z_bf[:].bitcast(F32).rearrange("p (b m u) -> p b m u", b=blocks, u=2),
-                    words[:].rearrange("p b u m -> p b m u"),
-                )
-                z_codes = ring.tile([P, width], U32, name="z_codes", bufs=4, align_bytes=64)
-                z_scales = ring.tile([P, width], U8, name="z_scales", bufs=4, align_bytes=64)
-                nc.vector.quantize_mx(out=z_codes[:].bitcast(FP8X4), scales=z_scales[:], in_=z_bf[:])
-                z_q.append((z_codes, z_scales))
-            for b in range(blocks):
-                cols = slice(b * P, (b + 1) * P)
+        an1 = [load_aniso(1, m0, BANK) for m0 in range(0, M, BANK)]
+        ends1 = {}
+        prods = {}
+
+        def first_ends(pair, tiles):
+            for i in tiles:
+                x = ring.tile([P, END1_WIDTH], F32, name="end1_%d" % i)
+                first_end(x[:], PACK + i, pair * END1_WIDTH, END1_WIDTH)
+                ends1[pair, i] = x
+
+        def second_ends(c):
+            tiles = []
+            for i in range(PACK):
+                tag = "paced%d" % (c % 2) if i == 0 else "bond%d_%d" % (i, c % 2)
+                x = held.tile([P, P], F32, name="bond%d" % i, tag=tag, align_bytes=64)
+                d = (c % 2) * P
+                second_end(x[:], ends1[c // 2, i][:, d : d + P], PACK + i, c * P, P)
+                tiles.append(x[:])
+            prods[c] = tiles
+
+        rounded = {}
+
+        def round_block(c):
+            m0, width = c * P, P
+            z_bf = held.tile([P, width * PACK], BF16, name="z_bf", tag="paced%d" % (c % 2), align_bytes=64)
+            round_z(z_bf[:], an1[m0 // BANK][:, :, m0 % BANK : m0 % BANK + width], prods[c], width)
+            rounded[c] = z_bf
+
+        def readouts(c):
+            m0, width = c * P, P
+            z_bf = rounded[c]
+            z_codes = ring.tile([P, width], U32, name="z_codes", align_bytes=64)
+            z_scales = ring.tile([P, width], U8, name="z_scales", align_bytes=64)
+            nc.vector.quantize_mx(out=z_codes[:].bitcast(FP8X4), scales=z_scales[:], in_=z_bf[:])
+            for b0 in range(0, width, P):
+                moving = [
+                    (z0_codes[:, m0 + b0 : m0 + b0 + P], z0_scales[:, m0 + b0 : m0 + b0 + P]),
+                    (z_codes[:, b0 : b0 + P], z_scales[:, b0 : b0 + P]),
+                ]
                 y2 = psum.tile([P, OUT_TILES, P], F32, name="y2", tag="sums", bufs=4)
                 y3 = psum.tile([P, OUT_TILES, P], F32, name="y3", tag="sums", bufs=4)
                 for a in range(PASSES):
-                    z_codes, z_scales = z_q[a]
                     for y in (y2, y3):
                         for n in range(OUT_TILES):
                             if y is y2:
@@ -240,8 +301,8 @@ def tile_list_garnet_bond_maximum_kernel(
                                 out=y[:, n, :],
                                 lhsT=lhs,
                                 lhsT_scale=lhs_scale,
-                                rhs=z_codes[:, cols].bitcast(FP8X4),
-                                rhs_scale=z_scales[:, cols],
+                                rhs=moving[a][0].bitcast(FP8X4),
+                                rhs_scale=moving[a][1],
                                 start=(a == 0 and n == 0),
                                 stop=(a == PASSES - 1 and n == OUT_TILES - 1),
                             )
@@ -249,5 +310,15 @@ def tile_list_garnet_bond_maximum_kernel(
                 nc.scalar.copy(y2_sb[:], y2[:])
                 best = ring.tile([P, OUT_TILES, P], F32, name="best")
                 nc.vector.tensor_tensor(best[:], y3[:], y2_sb[:], MAX)
-                nc.sync.dma_start(out_view[:, :, m0 + b * P : m0 + (b + 1) * P], best[:])
-            m0 = m0 + width
+                nc.sync.dma_start(out_view[:, :, m0 + b0 : m0 + b0 + P], best[:])
+
+        blocks = M // P
+        first_ends(0, range(PACK))
+        for c in range(blocks):
+            if c // 2 + 1 < blocks // 2:
+                first_ends(c // 2 + 1, range(2 * (c % 2), 2 * (c % 2) + 2))
+            second_ends(c)
+            round_block(c)
+            if c >= 1:
+                readouts(c - 1)
+        readouts(blocks - 1)

@@ -26,7 +26,7 @@ PASSES = 2
 BANK = 512
 ROW_TILES = H // P
 OUT_TILES = N // P
-W1_WIDTHS = (128, 128, 256, 512)
+W1_WIDTHS = (256, 256, 512)
 END1_WIDTH = 256
 PAGES = 4
 
@@ -94,11 +94,10 @@ def tile_list_garnet_bond_maximum_kernel(
 
         load_w1(0)
         nc.sync.dma_start(tab[1][:], tab_words[1].rearrange("p t i -> p (t i)").bitcast(I32))
-        load_w1(1)
         site_list = load_list("site_list", offs2)
         wgs_sb = held.tile([P, S], F32, name="wgs_sb")
         nc.sync.dma_start(wgs_sb[:], wgs)
-        for c in range(2, len(W1_WIDTHS)):
+        for c in range(1, len(W1_WIDTHS)):
             load_w1(c)
 
         identity = held.tile([P, P], F32, name="identity")
@@ -112,16 +111,15 @@ def tile_list_garnet_bond_maximum_kernel(
             nc.vector.memset(page[:].bitcast(I32), 0)
 
         v_scales = held.tile([P, S], U8, name="v_scales", align_bytes=64)
-        nc.vector.tensor_copy(v_scales[:], tab_plane[:].indirect(spin_list[:]))
         v_codes = [held.tile([P, S], U32, name="v_codes%d" % a, align_bytes=64) for a in range(PASSES)]
         nc.vector.tensor_copy(v_codes[0][:], tab[0][:].bitcast(U32).indirect(spin_list[:]))
+        nc.vector.tensor_copy(v_scales[:], tab_plane[:].indirect(spin_list[:]))
         w1_q = {0: quantize_weight(w1_raw[0], W1_WIDTHS[0], "w1_0", "w1_0")}
         for j0 in range(0, S, BANK):
             nc.vector.tensor_copy(
                 v_codes[1][:, j0 : j0 + BANK], tab[1][:].bitcast(U32).indirect(entries(spin_list, j0, BANK))
             )
 
-        w1_q[1] = quantize_weight(w1_raw[1], W1_WIDTHS[1], "w1_1", "x1_0")
         end1_list = load_list("end1_list", offs3)
         end2_list = load_list("end2_list", offs4)
         nc.sync.dma_start(gain_rows[0:ROW_TILES, :], gain.rearrange("(t p) -> t p", p=P))
@@ -133,7 +131,10 @@ def tile_list_garnet_bond_maximum_kernel(
         def sines_to_page(t):
             c = max(i for i in range(len(W1_WIDTHS)) if w1_starts[i] <= t * P)
             codes, scales = w1_q[c]
-            h = ring.tile([P, S], F32, name="h", bufs=3)
+            if t == 0:
+                h = held.tile([P, S], F32, name="h", tag="x1_0", align_bytes=64)
+            else:
+                h = ring.tile([P, S], F32, name="h", bufs=4)
             for j0 in range(0, S, BANK):
                 acc = psum.tile([P, BANK], F32, name="angles", tag="sums", bufs=4)
                 for a in range(PASSES):
@@ -206,20 +207,18 @@ def tile_list_garnet_bond_maximum_kernel(
             second_end(prod[t][:], x1[t][:], t, 0, M)
 
         sines_to_page(0)
-        w1_q[2] = quantize_weight(w1_raw[2], W1_WIDTHS[2], "w1_2", "x1_0")
         sines_to_page(1)
+        w1_q[1] = quantize_weight(w1_raw[1], W1_WIDTHS[1], "w1_1", "x1_0")
         whole_first_end(0)
         whole_first_end(1)
         sines_to_page(2)
-        w1_q[3] = quantize_weight(w1_raw[3], W1_WIDTHS[3], "w1_3", "x1_2")
-        whole_second_end(0)
         sines_to_page(3)
+        w1_q[2] = quantize_weight(w1_raw[2], W1_WIDTHS[2], "w1_2", "x1_2")
         whole_first_end(2)
-        whole_second_end(1)
         whole_first_end(3)
-        whole_second_end(2)
+        for t in range(PACK):
+            whole_second_end(t)
         sines_to_page(4)
-        whole_second_end(3)
         w3_raw = [load_rows(w3, a, 0, N, "w3_raw%d" % a, ring, "staged", 3) for a in range(PASSES)]
         w3_codes, w3_scales = quantize_weight(w3_raw, N, "w3", "w3_bf16")
         w2_codes = held.tile([P, PASSES, 2 * N], U8, name="w2_codes", align_bytes=64)
@@ -231,7 +230,7 @@ def tile_list_garnet_bond_maximum_kernel(
             )
         for t in range(PACK + 1, ROW_TILES - 1):
             sines_to_page(t)
-        z0_bf = held.tile([P, M * PACK], BF16, name="z0_bf", align_bytes=64)
+        z0_bf = held.tile([P, M * PACK], BF16, name="z0_bf", tag="ends", align_bytes=64)
         for m0 in range(0, M, BANK):
             an = load_aniso(0, m0, BANK)
             for d in range(0, BANK, 2 * P):
@@ -251,11 +250,10 @@ def tile_list_garnet_bond_maximum_kernel(
         ends1 = {}
         prods = {}
 
-        def first_ends(pair, tiles):
-            for i in tiles:
-                x = ring.tile([P, END1_WIDTH], F32, name="end1_%d" % i)
-                first_end(x[:], PACK + i, pair * END1_WIDTH, END1_WIDTH)
-                ends1[pair, i] = x
+        def first_ends(pair):
+            ends1[pair] = held.tile([P, PACK, END1_WIDTH], F32, name="ends", align_bytes=64)
+            for i in range(PACK):
+                first_end(ends1[pair][:, i, :], PACK + i, pair * END1_WIDTH, END1_WIDTH)
 
         def second_ends(c):
             tiles = []
@@ -263,7 +261,7 @@ def tile_list_garnet_bond_maximum_kernel(
                 tag = "paced%d" % (c % 2) if i == 0 else "bond%d_%d" % (i, c % 2)
                 x = held.tile([P, P], F32, name="bond%d" % i, tag=tag, align_bytes=64)
                 d = (c % 2) * P
-                second_end(x[:], ends1[c // 2, i][:, d : d + P], PACK + i, c * P, P)
+                second_end(x[:], ends1[c // 2][:, i, d : d + P], PACK + i, c * P, P)
                 tiles.append(x[:])
             prods[c] = tiles
 
@@ -313,10 +311,9 @@ def tile_list_garnet_bond_maximum_kernel(
                 nc.sync.dma_start(out_view[:, :, m0 + b0 : m0 + b0 + P], best[:])
 
         blocks = M // P
-        first_ends(0, range(PACK))
         for c in range(blocks):
-            if c // 2 + 1 < blocks // 2:
-                first_ends(c // 2 + 1, range(2 * (c % 2), 2 * (c % 2) + 2))
+            if c % 2 == 0:
+                first_ends(c // 2)
             second_ends(c)
             round_block(c)
             if c >= 1:

@@ -17,6 +17,7 @@ FP4X4 = mybir.dt.float4_e2m1fn_x4
 MULT = mybir.AluOpType.mult
 MAX = mybir.AluOpType.max
 COPY = mybir.ActivationFunctionType.Copy
+IDENTITY = mybir.ActivationFunctionType.Identity
 SIN = mybir.ActivationFunctionType.Sin
 
 P = 128
@@ -27,8 +28,9 @@ BANK = 512
 ROW_TILES = H // P
 OUT_TILES = N // P
 W1_WIDTHS = (256, 256, 512)
-END1_WIDTH = 256
+END1_BLOCKS = ((2, 2, 2, 1, 1), (3, 2, 2, 1))
 PAGES = 4
+LATE = (4, 5)
 
 
 def tile_list_garnet_bond_maximum_kernel(
@@ -49,7 +51,7 @@ def tile_list_garnet_bond_maximum_kernel(
             return tile[:, start // 16 : (start + count) // 16]
 
         def load_rows(w, a, c0, width, name, pool, tag, bufs):
-            raw = pool.tile([P, PACK, width], F32, name=name, tag=tag, bufs=bufs)
+            raw = pool.tile([P, PACK, width], F32, name=name, tag=tag, bufs=bufs, align_bytes=64)
             nc.sync.dma_start(
                 raw[:], w[a * K_PASS : (a + 1) * K_PASS, c0 : c0 + width].rearrange("(p i) c -> p i c", i=PACK)
             )
@@ -83,12 +85,8 @@ def tile_list_garnet_bond_maximum_kernel(
         w1_raw = {}
 
         def load_w1(c):
-            big = W1_WIDTHS[c] == BANK
             w1_raw[c] = [
-                load_rows(
-                    w1, a, w1_starts[c], W1_WIDTHS[c], "w1_raw%d_%d" % (c, a),
-                    ring if big else held, "staged" if big else "w1_raw%d_%d" % (c, a), 3 if big else 1,
-                )
+                load_rows(w1, a, w1_starts[c], W1_WIDTHS[c], "w1_raw%d_%d" % (c, a), held, "w1_raw%d_%d" % (c, a), 1)
                 for a in range(PASSES)
             ]
 
@@ -123,40 +121,46 @@ def tile_list_garnet_bond_maximum_kernel(
         end1_list = load_list("end1_list", offs3)
         end2_list = load_list("end2_list", offs4)
         nc.sync.dma_start(gain_rows[0:ROW_TILES, :], gain.rearrange("(t p) -> t p", p=P))
-        gain_psum = psum.tile([P, P], F32, name="gain_psum", tag="words")
+        gain_psum = psum.tile([P, P], F32, name="gain_psum", tag="words", bufs=1)
         nc.tensor.transpose(gain_psum[:], gain_rows[:], identity[:])
         gain_cols = held.tile([P, ROW_TILES], F32, name="gain_cols")
         nc.scalar.copy(gain_cols[:], gain_psum[:, 0:ROW_TILES])
+        gain_wide = held.tile([P, PACK, P], F32, name="gain_wide")
+        for i in range(PACK):
+            nc.scalar.activation(
+                gain_wide[:, i, :], identity[:], IDENTITY, bias=gain_cols[:, PACK + i : PACK + i + 1], scale=0.0
+            )
 
-        def sines_to_page(t):
+        def sines(h, t, j0):
             c = max(i for i in range(len(W1_WIDTHS)) if w1_starts[i] <= t * P)
             codes, scales = w1_q[c]
-            if t == 0:
-                h = held.tile([P, S], F32, name="h", tag="x1_0", align_bytes=64)
-            else:
-                h = ring.tile([P, S], F32, name="h", bufs=4)
-            for j0 in range(0, S, BANK):
-                acc = psum.tile([P, BANK], F32, name="angles", tag="sums", bufs=4)
-                for a in range(PASSES):
-                    col = a * W1_WIDTHS[c] + t * P - w1_starts[c]
-                    nc.tensor.matmul_mx(
-                        out=acc[:],
-                        lhsT=codes[:, col : col + P].bitcast(FP8X4),
-                        lhsT_scale=scales[:, col : col + P],
-                        rhs=v_codes[a][:, j0 : j0 + BANK].bitcast(FP8X4),
-                        rhs_scale=v_scales[4 * a :, j0 : j0 + BANK],
-                        start=(a == 0),
-                        stop=(a == PASSES - 1),
-                    )
-                nc.scalar.activation(h[:, j0 : j0 + BANK], acc[:], SIN)
-            step = BANK if t == 0 else S
-            for j0 in range(0, S, step):
-                nc.vector.tensor_tensor(
-                    pages[t % PAGES][:].indirect(entries(site_list, j0, step)),
-                    h[:, j0 : j0 + step],
-                    wgs_sb[:, j0 : j0 + step],
-                    MULT,
+            acc = psum.tile([P, BANK], F32, name="angles", tag="y3", bufs=3)
+            for a in range(PASSES):
+                col = a * W1_WIDTHS[c] + t * P - w1_starts[c]
+                nc.tensor.matmul_mx(
+                    out=acc[:],
+                    lhsT=codes[:, col : col + P].bitcast(FP8X4),
+                    lhsT_scale=scales[:, col : col + P],
+                    rhs=v_codes[a][:, j0 : j0 + BANK].bitcast(FP8X4),
+                    rhs_scale=v_scales[4 * a :, j0 : j0 + BANK],
+                    start=(a == 0),
+                    stop=(a == PASSES - 1),
                 )
+            nc.scalar.activation(h[:, j0 : j0 + BANK], acc[:], SIN)
+
+        def scatter(h, t, j0, width):
+            nc.vector.tensor_tensor(
+                pages[t % PAGES][:].indirect(entries(site_list, j0, width)),
+                h[:, j0 : j0 + width],
+                wgs_sb[:, j0 : j0 + width],
+                MULT,
+            )
+
+        def sines_to_page(t):
+            h = ring.tile([P, S], F32, name="h", bufs=4)
+            for j0 in range(0, S, BANK):
+                sines(h, t, j0)
+            scatter(h, t, 0, S)
 
         def first_end(x1, t, m0, width):
             nc.vector.tensor_copy(x1, pages[t % PAGES][:].indirect(entries(end1_list, m0, width)))
@@ -166,29 +170,33 @@ def tile_list_garnet_bond_maximum_kernel(
             nc.vector.tensor_tensor(prod, pages[t % PAGES][:].indirect(entries(end2_list, m0, width)), x1, MULT)
 
         def load_aniso(a, m0, width):
-            an = ring.tile([P, PACK, width], F32, name="an", tag="staged", bufs=3)
+            an = ring.tile([P, PACK, width], F32, name="an", tag="staged", bufs=3, align_bytes=64)
             nc.sync.dma_start(
                 an[:], aniso[a * K_PASS : (a + 1) * K_PASS, m0 : m0 + width].rearrange("(i p) m -> p i m", p=P)
             )
             return an
 
-        def round_z(z_bf, an, prod, width):
+        def round_z(z_bf, an, prod, width, rounded_tile, banks, groups=((0, 1, 2, 3),)):
             blocks = width // P
-            words = psum.tile([P, blocks, 2, P], F32, name="words", tag="words")
+            words = psum.tile([P, blocks, 2, P], F32, name="words", tag="words", bufs=1)
             for b in range(blocks):
                 cols = slice(b * P, (b + 1) * P)
-                zt = psum.tile([P, PACK, P], F32, name="zt")
-                terms = [an[:, i, cols] for i in range(PACK)] + [prod[i][:, cols] for i in range(PACK)]
-                for n, term in enumerate(terms):
-                    nc.tensor.matmul(
-                        zt[:, n % PACK, :], term, identity[:],
-                        start=(n == 0), stop=(n == len(terms) - 1), is_transpose=True,
+                zt_bf = None
+                for g, tiles in enumerate(groups):
+                    zt = psum.tile([P, PACK, P], F32, name="zt", tag="zt%d" % ((b + g) % banks), bufs=1)
+                    terms = [(i, an[:, i, cols]) for i in tiles] + [(i, prod[i][:, cols]) for i in tiles]
+                    for n, (i, term) in enumerate(terms):
+                        nc.tensor.matmul(
+                            zt[:, i, :], term, identity[:],
+                            start=(n == 0), stop=(n == len(terms) - 1), is_transpose=True,
+                        )
+                    if zt_bf is None:
+                        zt_bf = rounded_tile()
+                    words_of = slice(32 * tiles[0], 32 * (tiles[-1] + 1))
+                    nc.scalar.copy(
+                        zt_bf[:].rearrange("m (u p e) -> m u p e", u=2, e=2)[:, :, words_of, :],
+                        zt[:].rearrange("m i r -> m (i r)").rearrange("m (p u e) -> m u p e", u=2, e=2)[:, :, words_of, :],
                     )
-                zt_bf = ring.tile([P, K_PASS], BF16, name="zt_bf", bufs=3)
-                nc.scalar.copy(
-                    zt_bf[:].rearrange("m (u p e) -> m u p e", u=2, e=2),
-                    zt[:].rearrange("m i r -> m (i r)").rearrange("m (p u e) -> m u p e", u=2, e=2),
-                )
                 for u in range(2):
                     nc.tensor.transpose(words[:, b, u, :], zt_bf[:].bitcast(F32)[:, u * P : (u + 1) * P], identity[:])
             nc.scalar.copy(
@@ -197,30 +205,33 @@ def tile_list_garnet_bond_maximum_kernel(
             )
 
         x1 = {}
-        prod = [held.tile([P, M], F32, name="prod_%d" % i) for i in range(PACK)]
+        prod = [held.tile([P, M], F32, name="prod_%d" % i, align_bytes=64) for i in range(PACK)]
 
         def whole_first_end(t):
-            x1[t] = held.tile([P, M], F32, name="x1_%d" % t, align_bytes=64)
+            x1[t] = held.tile([P, M], F32, name="x1_%d" % t, tag="w1_raw%d_%d" % (1 + t // 2, t % 2), align_bytes=64)
             first_end(x1[t][:], t, 0, M)
 
         def whole_second_end(t):
             second_end(prod[t][:], x1[t][:], t, 0, M)
 
-        sines_to_page(0)
-        sines_to_page(1)
-        w1_q[1] = quantize_weight(w1_raw[1], W1_WIDTHS[1], "w1_1", "x1_0")
-        whole_first_end(0)
-        whole_first_end(1)
-        sines_to_page(2)
-        sines_to_page(3)
-        w1_q[2] = quantize_weight(w1_raw[2], W1_WIDTHS[2], "w1_2", "x1_2")
-        whole_first_end(2)
-        whole_first_end(3)
-        for t in range(PACK):
+        first_h = [ring.tile([P, S], F32, name="h", bufs=4) for t in range(2)]
+        for j0 in range(0, S, BANK):
+            for t in range(2):
+                sines(first_h[t], t, j0)
+                scatter(first_h[t], t, j0, BANK)
+        for c in (1, 2):
+            t = 2 * (c - 1)
+            if c > 1:
+                sines_to_page(t)
+                sines_to_page(t + 1)
+            whole_first_end(t)
+            w1_q[c] = quantize_weight(w1_raw[c], W1_WIDTHS[c], "w1_%d" % c, "w1_%d" % c)
+            whole_first_end(t + 1)
             whole_second_end(t)
+            whole_second_end(t + 1)
         sines_to_page(4)
         w3_raw = [load_rows(w3, a, 0, N, "w3_raw%d" % a, ring, "staged", 3) for a in range(PASSES)]
-        w3_codes, w3_scales = quantize_weight(w3_raw, N, "w3", "w3_bf16")
+        w3_codes, w3_scales = quantize_weight(w3_raw, N, "w3", "w1_2")
         w2_codes = held.tile([P, PASSES, 2 * N], U8, name="w2_codes", align_bytes=64)
         nc.sync.dma_start(w2_codes[:].bitcast(I32), w2_words.rearrange("a p b -> p a b").bitcast(I32))
         for q in range(4):
@@ -230,7 +241,7 @@ def tile_list_garnet_bond_maximum_kernel(
             )
         for t in range(PACK + 1, ROW_TILES - 1):
             sines_to_page(t)
-        z0_bf = held.tile([P, M * PACK], BF16, name="z0_bf", tag="ends", align_bytes=64)
+        z0_bf = held.tile([P, M * PACK], BF16, name="z0_bf", align_bytes=64)
         for m0 in range(0, M, BANK):
             an = load_aniso(0, m0, BANK)
             for d in range(0, BANK, 2 * P):
@@ -239,6 +250,8 @@ def tile_list_garnet_bond_maximum_kernel(
                     an[:, :, d : d + 2 * P],
                     [x[:, m0 + d : m0 + d + 2 * P] for x in prod],
                     2 * P,
+                    lambda: ring.tile([P, K_PASS], BF16, name="zt_bf", bufs=3),
+                    2,
                 )
         sines_to_page(ROW_TILES - 1)
         z0_codes = held.tile([P, M], U32, name="z0_codes", align_bytes=64)
@@ -248,29 +261,60 @@ def tile_list_garnet_bond_maximum_kernel(
         out_view = out.rearrange("(t p) m -> p t m", p=P)
         an1 = [load_aniso(1, m0, BANK) for m0 in range(0, M, BANK)]
         ends1 = {}
-        prods = {}
 
-        def first_ends(pair):
-            ends1[pair] = held.tile([P, PACK, END1_WIDTH], F32, name="ends", align_bytes=64)
+        blocks = M // P
+        last = blocks - 1
+
+        run_at = [
+            {sum(END1_BLOCKS[i // 2][:j]): n for j, n in enumerate(END1_BLOCKS[i // 2])} for i in range(PACK)
+        ]
+        scaled = {}
+        rounded = {}
+        sums = {}
+
+        def first_ends(c):
             for i in range(PACK):
-                first_end(ends1[pair][:, i, :], PACK + i, pair * END1_WIDTH, END1_WIDTH)
+                count = run_at[i].get(c, 0)
+                if count > 1:
+                    x = held.tile([P, count * P], F32, name="ends", tag="prod_%d" % i, align_bytes=64)
+                    nc.vector.tensor_copy(x[:], pages[i][:].indirect(entries(end1_list, c * P, count * P)))
+                    for d in range(count):
+                        ends1[c + d, i] = x[:, d * P : (d + 1) * P]
+
+        def scale_ends(c):
+            scaled[c] = held.tile([P, PACK, P], F32, name="scaled", tag="paced%d" % (c % 2), align_bytes=64)
+            for i in sorted(range(PACK), key=lambda i: c + 1 not in run_at[i]):
+                if run_at[i].get(c) == 1:
+                    nc.vector.tensor_tensor(
+                        scaled[c][:, i, :],
+                        pages[i][:].indirect(entries(end1_list, c * P, P)),
+                        gain_wide[:, i, :],
+                        MULT,
+                    )
+                else:
+                    nc.scalar.activation(
+                        scaled[c][:, i, :], ends1[c, i], COPY, scale=gain_cols[:, PACK + i : PACK + i + 1]
+                    )
 
         def second_ends(c):
-            tiles = []
+            m0 = c * P
+            bonds = ring.tile([P, PACK, P], F32, name="bonds", align_bytes=64)
             for i in range(PACK):
-                tag = "paced%d" % (c % 2) if i == 0 else "bond%d_%d" % (i, c % 2)
-                x = held.tile([P, P], F32, name="bond%d" % i, tag=tag, align_bytes=64)
-                d = (c % 2) * P
-                second_end(x[:], ends1[c // 2][:, i, d : d + P], PACK + i, c * P, P)
-                tiles.append(x[:])
-            prods[c] = tiles
-
-        rounded = {}
-
-        def round_block(c):
-            m0, width = c * P, P
-            z_bf = held.tile([P, width * PACK], BF16, name="z_bf", tag="paced%d" % (c % 2), align_bytes=64)
-            round_z(z_bf[:], an1[m0 // BANK][:, :, m0 % BANK : m0 % BANK + width], prods[c], width)
+                second_end(bonds[:, i, :], scaled[c][:, i, :], PACK + i, m0, P)
+            if c == last - 1:
+                z_bf = held.tile([P, P * PACK], BF16, name="z_bf_late", tag="late0", align_bytes=64)
+            else:
+                z_bf = ring.tile([P, P * PACK], BF16, name="z_bf", align_bytes=64)
+            tag = "paced%d" % (c % 2) if c < last else "zt_last"
+            round_z(
+                z_bf[:],
+                an1[m0 // BANK][:, :, m0 % BANK : m0 % BANK + P],
+                [bonds[:, i, :] for i in range(PACK)],
+                P,
+                lambda: held.tile([P, K_PASS], BF16, name="zt_bf", tag=tag, align_bytes=64),
+                2 if c == last else 1,
+                ((0, 1, 2), (3,)) if c == last else ((0, 1, 2, 3),),
+            )
             rounded[c] = z_bf
 
         def readouts(c):
@@ -284,8 +328,8 @@ def tile_list_garnet_bond_maximum_kernel(
                     (z0_codes[:, m0 + b0 : m0 + b0 + P], z0_scales[:, m0 + b0 : m0 + b0 + P]),
                     (z_codes[:, b0 : b0 + P], z_scales[:, b0 : b0 + P]),
                 ]
-                y2 = psum.tile([P, OUT_TILES, P], F32, name="y2", tag="sums", bufs=4)
-                y3 = psum.tile([P, OUT_TILES, P], F32, name="y3", tag="sums", bufs=4)
+                y2 = psum.tile([P, OUT_TILES, P], F32, name="y2", bufs=2)
+                y3 = psum.tile([P, OUT_TILES, P], F32, name="y3", bufs=3)
                 for a in range(PASSES):
                     for y in (y2, y3):
                         for n in range(OUT_TILES):
@@ -304,18 +348,34 @@ def tile_list_garnet_bond_maximum_kernel(
                                 start=(a == 0 and n == 0),
                                 stop=(a == PASSES - 1 and n == OUT_TILES - 1),
                             )
-                y2_sb = ring.tile([P, OUT_TILES, P], F32, name="y2_sb")
+                if c == LATE[0]:
+                    y2_sb = held.tile([P, OUT_TILES, P], F32, name="y2_late", tag="late1", align_bytes=64)
+                else:
+                    y2_sb = ring.tile([P, OUT_TILES, P], F32, name="y2_sb", bufs=3)
                 nc.scalar.copy(y2_sb[:], y2[:])
-                best = ring.tile([P, OUT_TILES, P], F32, name="best")
-                nc.vector.tensor_tensor(best[:], y3[:], y2_sb[:], MAX)
-                nc.sync.dma_start(out_view[:, :, m0 + b0 : m0 + b0 + P], best[:])
+                sums[c] = (y2_sb, y3)
 
-        blocks = M // P
+        def store_maximum(c):
+            y2_sb, y3 = sums[c]
+            if c in LATE:
+                best = held.tile([P, OUT_TILES, P], F32, name="best_late", tag="late%d" % LATE.index(c), align_bytes=64)
+            else:
+                best = ring.tile([P, OUT_TILES, P], F32, name="best")
+            nc.vector.tensor_tensor(best[:], y3[:], y2_sb[:], MAX)
+            nc.sync.dma_start(out_view[:, :, c * P : (c + 1) * P], best[:])
+
+        first_ends(0)
         for c in range(blocks):
-            if c % 2 == 0:
-                first_ends(c // 2)
+            if c >= 3 and c - 3 not in LATE:
+                store_maximum(c - 3)
+            if c >= 2:
+                readouts(c - 2)
+            scale_ends(c)
+            first_ends(c + 1)
             second_ends(c)
-            round_block(c)
-            if c >= 1:
-                readouts(c - 1)
-        readouts(blocks - 1)
+        readouts(last - 1)
+        for c in LATE:
+            store_maximum(c)
+        readouts(last)
+        store_maximum(last - 1)
+        store_maximum(last)

@@ -27,8 +27,8 @@ PASSES = 2
 BANK = 512
 ROW_TILES = H // P
 OUT_TILES = N // P
-W1_WIDTHS = (256, 256, 512)
-END1_BLOCKS = ((2, 2, 2, 1, 1), (3, 2, 2, 1))
+W1_WIDTHS = (128, 128, 256, 512)
+END1_BLOCKS = ((2, 2, 2, 2), (2, 2, 2, 1, 1), (3, 2, 2, 1), (3, 2, 2, 1))
 PAGES = 4
 LATE = (4, 5)
 
@@ -40,6 +40,7 @@ def tile_list_garnet_bond_maximum_kernel(
     with ExitStack() as ctx:
         held = ctx.enter_context(tc.tile_pool(name="held", bufs=1))
         ring = ctx.enter_context(tc.tile_pool(name="ring", bufs=2))
+        paced = ctx.enter_context(tc.tile_pool(name="paced", bufs=1))
         psum = ctx.enter_context(tc.psum_pool(name="psum", bufs=2))
 
         def load_list(name, dram):
@@ -100,11 +101,7 @@ def tile_list_garnet_bond_maximum_kernel(
 
         identity = held.tile([P, P], F32, name="identity")
         make_identity(nc, identity[:])
-        gain_rows = held.tile([P, P], F32, name="gain_rows")
-        nc.gpsimd.memset(gain_rows[:], 0.0)
-        w2_plane = held.tile([P, PASSES, N], U8, name="w2_plane", align_bytes=64)
-        nc.gpsimd.memset(w2_plane[:].rearrange("p a n -> p (a n)").bitcast(I32), 0)
-        pages = [held.tile([P, T2], F32, name="page%d" % t) for t in range(PAGES)]
+        pages = [held.tile([P, T2], F32, name="page%d" % t) for t in range(PAGES - 1)]
         for page in pages:
             nc.vector.memset(page[:].bitcast(I32), 0)
 
@@ -118,11 +115,15 @@ def tile_list_garnet_bond_maximum_kernel(
                 v_codes[1][:, j0 : j0 + BANK], tab[1][:].bitcast(U32).indirect(entries(spin_list, j0, BANK))
             )
 
+        pages.append(held.tile([P, T2], F32, name="page_last", tag="tab1"))
+        nc.vector.memset(pages[-1][:].bitcast(I32), 0)
+
         end1_list = load_list("end1_list", offs3)
         end2_list = load_list("end2_list", offs4)
+        gain_rows = w1_raw[0][0][:, 0, :]
         nc.sync.dma_start(gain_rows[0:ROW_TILES, :], gain.rearrange("(t p) -> t p", p=P))
         gain_psum = psum.tile([P, P], F32, name="gain_psum", tag="words", bufs=1)
-        nc.tensor.transpose(gain_psum[:], gain_rows[:], identity[:])
+        nc.tensor.transpose(gain_psum[:], gain_rows, identity[:])
         gain_cols = held.tile([P, ROW_TILES], F32, name="gain_cols")
         nc.scalar.copy(gain_cols[:], gain_psum[:, 0:ROW_TILES])
         gain_wide = held.tile([P, PACK, P], F32, name="gain_wide")
@@ -146,12 +147,12 @@ def tile_list_garnet_bond_maximum_kernel(
                     start=(a == 0),
                     stop=(a == PASSES - 1),
                 )
-            nc.scalar.activation(h[:, j0 : j0 + BANK], acc[:], SIN)
+            nc.scalar.activation(h, acc[:], SIN)
 
         def scatter(h, t, j0, width):
             nc.vector.tensor_tensor(
                 pages[t % PAGES][:].indirect(entries(site_list, j0, width)),
-                h[:, j0 : j0 + width],
+                h,
                 wgs_sb[:, j0 : j0 + width],
                 MULT,
             )
@@ -159,8 +160,8 @@ def tile_list_garnet_bond_maximum_kernel(
         def sines_to_page(t):
             h = ring.tile([P, S], F32, name="h", bufs=4)
             for j0 in range(0, S, BANK):
-                sines(h, t, j0)
-            scatter(h, t, 0, S)
+                sines(h[:, j0 : j0 + BANK], t, j0)
+            scatter(h[:], t, 0, S)
 
         def first_end(x1, t, m0, width):
             nc.vector.tensor_copy(x1, pages[t % PAGES][:].indirect(entries(end1_list, m0, width)))
@@ -208,20 +209,25 @@ def tile_list_garnet_bond_maximum_kernel(
         prod = [held.tile([P, M], F32, name="prod_%d" % i, align_bytes=64) for i in range(PACK)]
 
         def whole_first_end(t):
-            x1[t] = held.tile([P, M], F32, name="x1_%d" % t, tag="w1_raw%d_%d" % (1 + t // 2, t % 2), align_bytes=64)
+            x1[t] = held.tile([P, M], F32, name="x1_%d" % t, tag="w1_raw%d_%d" % (2 + t // 2, t % 2), align_bytes=64)
             first_end(x1[t][:], t, 0, M)
 
         def whole_second_end(t):
             second_end(prod[t][:], x1[t][:], t, 0, M)
 
-        first_h = [ring.tile([P, S], F32, name="h", bufs=4) for t in range(2)]
-        for j0 in range(0, S, BANK):
-            for t in range(2):
-                sines(first_h[t], t, j0)
-                scatter(first_h[t], t, j0, BANK)
-        for c in (1, 2):
-            t = 2 * (c - 1)
-            if c > 1:
+        halves = [
+            held.tile([P, BANK], F32, name="h0_%d" % j, tag=tag, align_bytes=64)
+            for j, tag in enumerate(("h0_0", "w1_raw1_1"))
+        ]
+        sines(halves[0][:], 0, 0)
+        scatter(halves[0][:], 0, 0, BANK)
+        w1_q[1] = quantize_weight(w1_raw[1], W1_WIDTHS[1], "w1_1", "w1_1")
+        sines(halves[1][:], 0, BANK)
+        scatter(halves[1][:], 0, BANK, BANK)
+        sines_to_page(1)
+        for c in (2, 3):
+            t = 2 * (c - 2)
+            if c > 2:
                 sines_to_page(t)
                 sines_to_page(t + 1)
             whole_first_end(t)
@@ -231,14 +237,9 @@ def tile_list_garnet_bond_maximum_kernel(
             whole_second_end(t + 1)
         sines_to_page(4)
         w3_raw = [load_rows(w3, a, 0, N, "w3_raw%d" % a, ring, "staged", 3) for a in range(PASSES)]
-        w3_codes, w3_scales = quantize_weight(w3_raw, N, "w3", "w1_2")
+        w3_codes, w3_scales = quantize_weight(w3_raw, N, "w3", "w1_3")
         w2_codes = held.tile([P, PASSES, 2 * N], U8, name="w2_codes", align_bytes=64)
         nc.sync.dma_start(w2_codes[:].bitcast(I32), w2_words.rearrange("a p b -> p a b").bitcast(I32))
-        for q in range(4):
-            nc.sync.dma_start(
-                w2_plane[32 * q : 32 * q + 4].bitcast(I32),
-                w2_scales[:, 4 * q : 4 * q + 4, :].rearrange("a r n -> r a n").bitcast(I32),
-            )
         for t in range(PACK + 1, ROW_TILES - 1):
             sines_to_page(t)
         z0_bf = held.tile([P, M * PACK], BF16, name="z0_bf", align_bytes=64)
@@ -254,6 +255,12 @@ def tile_list_garnet_bond_maximum_kernel(
                     2,
                 )
         sines_to_page(ROW_TILES - 1)
+        w2_plane = w1_q[3][1][:].rearrange("p (a n) -> p a n", a=PASSES)
+        for q in range(4):
+            nc.sync.dma_start(
+                w2_plane[32 * q : 32 * q + 4].bitcast(I32),
+                w2_scales[:, 4 * q : 4 * q + 4, :].rearrange("a r n -> r a n").bitcast(I32),
+            )
         z0_codes = held.tile([P, M], U32, name="z0_codes", align_bytes=64)
         z0_scales = held.tile([P, M], U8, name="z0_scales", align_bytes=64)
         nc.vector.quantize_mx(out=z0_codes[:].bitcast(FP8X4), scales=z0_scales[:], in_=z0_bf[:])
@@ -265,12 +272,16 @@ def tile_list_garnet_bond_maximum_kernel(
         blocks = M // P
         last = blocks - 1
 
-        run_at = [
-            {sum(END1_BLOCKS[i // 2][:j]): n for j, n in enumerate(END1_BLOCKS[i // 2])} for i in range(PACK)
-        ]
+        run_at = [{sum(runs[:j]): n for j, n in enumerate(runs)} for runs in END1_BLOCKS]
         scaled = {}
+        bonds = {}
         rounded = {}
         sums = {}
+
+        def paced_tile(shape, dtype, name, parity, offset):
+            return paced.tile(
+                shape, dtype, name="%s%d" % (name, parity), offset=4096 * parity + offset, align_bytes=64
+            )
 
         def first_ends(c):
             for i in range(PACK):
@@ -281,101 +292,124 @@ def tile_list_garnet_bond_maximum_kernel(
                     for d in range(count):
                         ends1[c + d, i] = x[:, d * P : (d + 1) * P]
 
+        def plain_tiles(c):
+            return sorted((i for i in range(PACK) if run_at[i].get(c) != 1), key=lambda i: c + 1 not in run_at[i])
+
         def scale_ends(c):
-            scaled[c] = held.tile([P, PACK, P], F32, name="scaled", tag="paced%d" % (c % 2), align_bytes=64)
-            for i in sorted(range(PACK), key=lambda i: c + 1 not in run_at[i]):
-                if run_at[i].get(c) == 1:
+            tile = paced_tile([P, PACK, P], F32, "scaled", c % 2, 0)
+            for i in plain_tiles(c):
+                scaled[c, i] = tile[:, i, :]
+                nc.scalar.activation(scaled[c, i], ends1[c, i], COPY, scale=gain_cols[:, PACK + i : PACK + i + 1])
+
+        def fused_ends(c):
+            fused = [i for i in range(PACK) if run_at[i].get(c) == 1]
+            if fused:
+                tile = held.tile([P, PACK, P], F32, name="fused", tag="prod_%d" % plain_tiles(c)[0], align_bytes=64)
+                for i in fused:
+                    scaled[c, i] = tile[:, i, :]
                     nc.vector.tensor_tensor(
-                        scaled[c][:, i, :],
-                        pages[i][:].indirect(entries(end1_list, c * P, P)),
-                        gain_wide[:, i, :],
-                        MULT,
-                    )
-                else:
-                    nc.scalar.activation(
-                        scaled[c][:, i, :], ends1[c, i], COPY, scale=gain_cols[:, PACK + i : PACK + i + 1]
+                        scaled[c, i], pages[i][:].indirect(entries(end1_list, c * P, P)), gain_wide[:, i, :], MULT
                     )
 
         def second_ends(c):
-            m0 = c * P
-            bonds = ring.tile([P, PACK, P], F32, name="bonds", align_bytes=64)
+            bonds[c] = ring.tile([P, PACK, P], F32, name="bonds", align_bytes=64)
             for i in range(PACK):
-                second_end(bonds[:, i, :], scaled[c][:, i, :], PACK + i, m0, P)
+                second_end(bonds[c][:, i, :], scaled[c, i], PACK + i, c * P, P)
+
+        def round_block(c):
+            m0 = c * P
             if c == last - 1:
                 z_bf = held.tile([P, P * PACK], BF16, name="z_bf_late", tag="late0", align_bytes=64)
             else:
                 z_bf = ring.tile([P, P * PACK], BF16, name="z_bf", align_bytes=64)
-            tag = "paced%d" % (c % 2) if c < last else "zt_last"
             round_z(
                 z_bf[:],
                 an1[m0 // BANK][:, :, m0 % BANK : m0 % BANK + P],
-                [bonds[:, i, :] for i in range(PACK)],
+                [bonds[c][:, i, :] for i in range(PACK)],
                 P,
-                lambda: held.tile([P, K_PASS], BF16, name="zt_bf", tag=tag, align_bytes=64),
+                lambda: paced_tile([P, K_PASS], BF16, "zt_bf", c % 2 if c < last else 2, 1536),
                 2 if c == last else 1,
                 ((0, 1, 2), (3,)) if c == last else ((0, 1, 2, 3),),
             )
             rounded[c] = z_bf
 
+        banks = {}
+
+        def products(c, a, z_codes, z_scales):
+            y2, y3 = banks[c]
+            for y in (y2, y3):
+                for n in range(OUT_TILES):
+                    if y is y2:
+                        lhs = w2_codes[:, a, 2 * n * P : 2 * (n + 1) * P].bitcast(FP4X4)
+                        lhs_scale = w2_plane[:, a, n * P : (n + 1) * P]
+                    else:
+                        lhs = w3_codes[:, a * N + n * P : a * N + (n + 1) * P].bitcast(FP8X4)
+                        lhs_scale = w3_scales[:, a * N + n * P : a * N + (n + 1) * P]
+                    nc.tensor.matmul_mx(
+                        out=y[:, n, :],
+                        lhsT=lhs,
+                        lhsT_scale=lhs_scale,
+                        rhs=z_codes.bitcast(FP8X4),
+                        rhs_scale=z_scales,
+                        start=(a == 0 and n == 0),
+                        stop=(a == PASSES - 1 and n == OUT_TILES - 1),
+                    )
+
         def readouts(c):
-            m0, width = c * P, P
-            z_bf = rounded[c]
-            z_codes = ring.tile([P, width], U32, name="z_codes", align_bytes=64)
-            z_scales = ring.tile([P, width], U8, name="z_scales", align_bytes=64)
-            nc.vector.quantize_mx(out=z_codes[:].bitcast(FP8X4), scales=z_scales[:], in_=z_bf[:])
-            for b0 in range(0, width, P):
-                moving = [
-                    (z0_codes[:, m0 + b0 : m0 + b0 + P], z0_scales[:, m0 + b0 : m0 + b0 + P]),
-                    (z_codes[:, b0 : b0 + P], z_scales[:, b0 : b0 + P]),
-                ]
-                y2 = psum.tile([P, OUT_TILES, P], F32, name="y2", bufs=2)
-                y3 = psum.tile([P, OUT_TILES, P], F32, name="y3", bufs=3)
-                for a in range(PASSES):
-                    for y in (y2, y3):
-                        for n in range(OUT_TILES):
-                            if y is y2:
-                                lhs = w2_codes[:, a, 2 * n * P : 2 * (n + 1) * P].bitcast(FP4X4)
-                                lhs_scale = w2_plane[:, a, n * P : (n + 1) * P]
-                            else:
-                                lhs = w3_codes[:, a * N + n * P : a * N + (n + 1) * P].bitcast(FP8X4)
-                                lhs_scale = w3_scales[:, a * N + n * P : a * N + (n + 1) * P]
-                            nc.tensor.matmul_mx(
-                                out=y[:, n, :],
-                                lhsT=lhs,
-                                lhsT_scale=lhs_scale,
-                                rhs=moving[a][0].bitcast(FP8X4),
-                                rhs_scale=moving[a][1],
-                                start=(a == 0 and n == 0),
-                                stop=(a == PASSES - 1 and n == OUT_TILES - 1),
-                            )
-                if c == LATE[0]:
-                    y2_sb = held.tile([P, OUT_TILES, P], F32, name="y2_late", tag="late1", align_bytes=64)
-                else:
-                    y2_sb = ring.tile([P, OUT_TILES, P], F32, name="y2_sb", bufs=3)
-                nc.scalar.copy(y2_sb[:], y2[:])
-                sums[c] = (y2_sb, y3)
+            z_codes = ring.tile([P, P], U32, name="z_codes", align_bytes=64)
+            z_scales = ring.tile([P, P], U8, name="z_scales", align_bytes=64)
+            nc.vector.quantize_mx(out=z_codes[:].bitcast(FP8X4), scales=z_scales[:], in_=rounded[c][:])
+            y2 = psum.tile([P, OUT_TILES, P], F32, name="y2", bufs=2)
+            y3 = psum.tile([P, OUT_TILES, P], F32, name="y3", bufs=3)
+            banks[c] = (y2, y3)
+            products(c, 0, z0_codes[:, c * P : (c + 1) * P], z0_scales[:, c * P : (c + 1) * P])
+            products(c, 1, z_codes[:], z_scales[:])
+
+        def copy_y2(c):
+            y2, y3 = banks[c]
+            if c == last:
+                y2_sb = held.tile([P, OUT_TILES, P], F32, name="y2_last")
+            else:
+                y2_sb = paced_tile([P, OUT_TILES, P], F32, "y2_sb", (c + 1) % 2 if c + 1 < last else 2, 2048)
+            step = OUT_TILES // 2 if c == last else OUT_TILES
+            for n0 in range(0, OUT_TILES, step):
+                nc.scalar.copy(y2_sb[:, n0 : n0 + step], y2[:, n0 : n0 + step])
+            sums[c] = (y2_sb, y3)
 
         def store_maximum(c):
             y2_sb, y3 = sums[c]
-            if c in LATE:
-                best = held.tile([P, OUT_TILES, P], F32, name="best_late", tag="late%d" % LATE.index(c), align_bytes=64)
+            if c == LATE[0]:
+                best = held.tile([P, OUT_TILES, P], F32, name="best_late", tag="late0", align_bytes=64)
+            elif c == LATE[1]:
+                best = paced_tile([P, OUT_TILES, P], F32, "best_late", c % 2, 2048)
             else:
                 best = ring.tile([P, OUT_TILES, P], F32, name="best")
-            nc.vector.tensor_tensor(best[:], y3[:], y2_sb[:], MAX)
-            nc.sync.dma_start(out_view[:, :, c * P : (c + 1) * P], best[:])
+            step = OUT_TILES // 2 if c == last else OUT_TILES
+            for n0 in range(0, OUT_TILES, step):
+                rows = slice(n0, n0 + step)
+                nc.vector.tensor_tensor(best[:, rows], y3[:, rows], y2_sb[:, rows], MAX)
+                nc.sync.dma_start(out_view[:, rows, c * P : (c + 1) * P], best[:, rows])
 
         first_ends(0)
+        scale_ends(0)
         for c in range(blocks):
-            if c >= 3 and c - 3 not in LATE:
-                store_maximum(c - 3)
             if c >= 2:
                 readouts(c - 2)
-            scale_ends(c)
+            if c >= 3 and c - 3 not in LATE:
+                store_maximum(c - 3)
+            fused_ends(c)
             first_ends(c + 1)
             second_ends(c)
+            if c < last:
+                scale_ends(c + 1)
+            if c >= 2:
+                copy_y2(c - 2)
+            round_block(c)
         readouts(last - 1)
+        copy_y2(last - 1)
         for c in LATE:
             store_maximum(c)
         readouts(last)
+        copy_y2(last)
         store_maximum(last - 1)
         store_maximum(last)

@@ -161,7 +161,12 @@ def tile_list_garnet_bond_maximum_kernel(
             h = ring.tile([P, S], F32, name="h", bufs=4)
             for j0 in range(0, S, BANK):
                 sines(h[:, j0 : j0 + BANK], t, j0)
-            scatter(h[:], t, 0, S)
+            if t in (5, 6):
+                weighted = held.tile([P, S], F32, name="weighted%d" % t, tag="w1_raw3_%d" % (t - 5), align_bytes=64)
+                nc.vector.tensor_tensor(weighted[:], h[:], wgs_sb[:], MULT)
+                nc.vector.tensor_copy(pages[t % PAGES][:].indirect(site_list[:]), weighted[:])
+            else:
+                scatter(h[:], t, 0, S)
 
         def first_end(x1, t, m0, width):
             nc.vector.tensor_copy(x1, pages[t % PAGES][:].indirect(entries(end1_list, m0, width)))
@@ -337,7 +342,7 @@ def tile_list_garnet_bond_maximum_kernel(
 
         def products(c, a, z_codes, z_scales):
             y2, y3 = banks[c]
-            for y in (y2, y3):
+            for y in (y2, y3) if c >= last - 1 else (y3, y2):
                 for n in range(OUT_TILES):
                     if y is y2:
                         lhs = w2_codes[:, a, 2 * n * P : 2 * (n + 1) * P].bitcast(FP4X4)
@@ -382,8 +387,10 @@ def tile_list_garnet_bond_maximum_kernel(
                 best = held.tile([P, OUT_TILES, P], F32, name="best_late", tag="late0", align_bytes=64)
             elif c == LATE[1]:
                 best = paced_tile([P, OUT_TILES, P], F32, "best_late", c % 2, 2048)
+            elif c < LATE[0]:
+                best = ring.tile([P, OUT_TILES, P], F32, name="best", tag="h", bufs=4)
             else:
-                best = ring.tile([P, OUT_TILES, P], F32, name="best")
+                best = held.tile([P, OUT_TILES, P], F32, name="best%d" % c)
             step = OUT_TILES // 2 if c == last else OUT_TILES
             for n0 in range(0, OUT_TILES, step):
                 rows = slice(n0, n0 + step)

@@ -27,10 +27,25 @@ PASSES = 2
 BANK = 512
 ROW_TILES = H // P
 OUT_TILES = N // P
+BLOCKS = M // P
+LAST = BLOCKS - 1
+PAGES = PACK
+
 W1_WIDTHS = (128, 128, 256, 512)
-END1_BLOCKS = ((2, 2, 2, 2), (2, 2, 2, 1, 1), (3, 2, 2, 1), (3, 2, 2, 1))
-PAGES = 4
-LATE = (4, 5)
+
+END1_RUNS = ((2, 2, 2, 2), (2, 2, 2, 1, 1), (3, 2, 2, 1), (3, 2, 2, 1))
+FUSED_TILES = tuple(i for i in range(PACK) if 1 in END1_RUNS[i])
+
+LATE = (LAST - 3, LAST - 2)
+
+LAST_REGION = 2
+TILE_BYTES = PACK * P * 4
+SCALED_AT, Y2_AT = 0, TILE_BYTES
+ROUNDED_AT = TILE_BYTES - K_PASS
+
+H_BUFS = 4
+STAGED_BUFS = 3
+Y2_BANKS, Y3_BANKS = 2, 3
 
 
 def tile_list_garnet_bond_maximum_kernel(
@@ -41,7 +56,7 @@ def tile_list_garnet_bond_maximum_kernel(
         held = ctx.enter_context(tc.tile_pool(name="held", bufs=1))
         ring = ctx.enter_context(tc.tile_pool(name="ring", bufs=2))
         paced = ctx.enter_context(tc.tile_pool(name="paced", bufs=1))
-        psum = ctx.enter_context(tc.psum_pool(name="psum", bufs=2))
+        psum = ctx.enter_context(tc.psum_pool(name="psum", bufs=1))
 
         def load_list(name, dram):
             tile = held.tile([P, S // 16], U16, name=name)
@@ -82,12 +97,15 @@ def tile_list_garnet_bond_maximum_kernel(
                 tab_plane[32 * q : 32 * q + 4 * PASSES, :].bitcast(I32),
                 tab_scales[:, 4 * q : 4 * q + 4, :].bitcast(I32),
             )
-        w1_starts = [sum(W1_WIDTHS[:c]) for c in range(len(W1_WIDTHS))]
+        w1_starts = [sum(W1_WIDTHS[:piece]) for piece in range(len(W1_WIDTHS))]
         w1_raw = {}
 
-        def load_w1(c):
-            w1_raw[c] = [
-                load_rows(w1, a, w1_starts[c], W1_WIDTHS[c], "w1_raw%d_%d" % (c, a), held, "w1_raw%d_%d" % (c, a), 1)
+        def raw_tag(piece, a):
+            return "w1_raw%d_%d" % (piece, a)
+
+        def load_w1(piece):
+            w1_raw[piece] = [
+                load_rows(w1, a, w1_starts[piece], W1_WIDTHS[piece], raw_tag(piece, a), held, raw_tag(piece, a), 1)
                 for a in range(PASSES)
             ]
 
@@ -96,8 +114,8 @@ def tile_list_garnet_bond_maximum_kernel(
         site_list = load_list("site_list", offs2)
         wgs_sb = held.tile([P, S], F32, name="wgs_sb")
         nc.sync.dma_start(wgs_sb[:], wgs)
-        for c in range(1, len(W1_WIDTHS)):
-            load_w1(c)
+        for piece in range(1, len(W1_WIDTHS)):
+            load_w1(piece)
 
         identity = held.tile([P, P], F32, name="identity")
         make_identity(nc, identity[:])
@@ -109,7 +127,12 @@ def tile_list_garnet_bond_maximum_kernel(
         v_codes = [held.tile([P, S], U32, name="v_codes%d" % a, align_bytes=64) for a in range(PASSES)]
         nc.vector.tensor_copy(v_codes[0][:], tab[0][:].bitcast(U32).indirect(spin_list[:]))
         nc.vector.tensor_copy(v_scales[:], tab_plane[:].indirect(spin_list[:]))
-        w1_q = {0: quantize_weight(w1_raw[0], W1_WIDTHS[0], "w1_0", "w1_0")}
+        w1_q = {}
+
+        def quantize_w1(piece):
+            w1_q[piece] = quantize_weight(w1_raw[piece], W1_WIDTHS[piece], "w1_%d" % piece, "w1_%d" % piece)
+
+        quantize_w1(0)
         for j0 in range(0, S, BANK):
             nc.vector.tensor_copy(
                 v_codes[1][:, j0 : j0 + BANK], tab[1][:].bitcast(U32).indirect(entries(spin_list, j0, BANK))
@@ -120,26 +143,28 @@ def tile_list_garnet_bond_maximum_kernel(
 
         end1_list = load_list("end1_list", offs3)
         end2_list = load_list("end2_list", offs4)
+
         gain_rows = w1_raw[0][0][:, 0, :]
         nc.sync.dma_start(gain_rows[0:ROW_TILES, :], gain.rearrange("(t p) -> t p", p=P))
-        gain_psum = psum.tile([P, P], F32, name="gain_psum", tag="words", bufs=1)
+        gain_psum = psum.tile([P, P], F32, name="gain_psum", tag="words")
         nc.tensor.transpose(gain_psum[:], gain_rows, identity[:])
         gain_cols = held.tile([P, ROW_TILES], F32, name="gain_cols")
         nc.scalar.copy(gain_cols[:], gain_psum[:, 0:ROW_TILES])
-        gain_wide = held.tile([P, PACK, P], F32, name="gain_wide")
-        for i in range(PACK):
+        gain_wide = {}
+        for i in FUSED_TILES:
+            gain_wide[i] = held.tile([P, P], F32, name="gain_wide%d" % i)
             nc.scalar.activation(
-                gain_wide[:, i, :], identity[:], IDENTITY, bias=gain_cols[:, PACK + i : PACK + i + 1], scale=0.0
+                gain_wide[i][:], identity[:], IDENTITY, bias=gain_cols[:, PACK + i : PACK + i + 1], scale=0.0
             )
 
         def sines(h, t, j0):
-            c = max(i for i in range(len(W1_WIDTHS)) if w1_starts[i] <= t * P)
-            codes, scales = w1_q[c]
-            acc = psum.tile([P, BANK], F32, name="angles", tag="y3", bufs=3)
+            piece = max(x for x in range(len(W1_WIDTHS)) if w1_starts[x] <= t * P)
+            codes, scales = w1_q[piece]
+            angles = psum.tile([P, BANK], F32, name="angles", tag="y3", bufs=Y3_BANKS)
             for a in range(PASSES):
-                col = a * W1_WIDTHS[c] + t * P - w1_starts[c]
+                col = a * W1_WIDTHS[piece] + t * P - w1_starts[piece]
                 nc.tensor.matmul_mx(
-                    out=acc[:],
+                    out=angles[:],
                     lhsT=codes[:, col : col + P].bitcast(FP8X4),
                     lhsT_scale=scales[:, col : col + P],
                     rhs=v_codes[a][:, j0 : j0 + BANK].bitcast(FP8X4),
@@ -147,50 +172,42 @@ def tile_list_garnet_bond_maximum_kernel(
                     start=(a == 0),
                     stop=(a == PASSES - 1),
                 )
-            nc.scalar.activation(h, acc[:], SIN)
+            nc.scalar.activation(h, angles[:], SIN)
 
         def scatter(h, t, j0, width):
             nc.vector.tensor_tensor(
-                pages[t % PAGES][:].indirect(entries(site_list, j0, width)),
-                h,
-                wgs_sb[:, j0 : j0 + width],
-                MULT,
+                pages[t % PAGES][:].indirect(entries(site_list, j0, width)), h, wgs_sb[:, j0 : j0 + width], MULT
             )
 
         def sines_to_page(t):
-            h = ring.tile([P, S], F32, name="h", bufs=4)
+            h = ring.tile([P, S], F32, name="h", bufs=H_BUFS)
             for j0 in range(0, S, BANK):
                 sines(h[:, j0 : j0 + BANK], t, j0)
-            if t in (5, 6):
-                weighted = held.tile([P, S], F32, name="weighted%d" % t, tag="w1_raw3_%d" % (t - 5), align_bytes=64)
-                nc.vector.tensor_tensor(weighted[:], h[:], wgs_sb[:], MULT)
-                nc.vector.tensor_copy(pages[t % PAGES][:].indirect(site_list[:]), weighted[:])
-            else:
-                scatter(h[:], t, 0, S)
+            scatter(h[:], t, 0, S)
 
-        def first_end(x1, t, m0, width):
-            nc.vector.tensor_copy(x1, pages[t % PAGES][:].indirect(entries(end1_list, m0, width)))
-            nc.scalar.activation(x1, x1, COPY, scale=gain_cols[:, t : t + 1])
+        def first_end_of(t, m0, width):
+            return pages[t % PAGES][:].indirect(entries(end1_list, m0, width))
 
-        def second_end(prod, x1, t, m0, width):
-            nc.vector.tensor_tensor(prod, pages[t % PAGES][:].indirect(entries(end2_list, m0, width)), x1, MULT)
+        def second_end(bond, scaled_end, t, m0, width):
+            nc.vector.tensor_tensor(
+                bond, pages[t % PAGES][:].indirect(entries(end2_list, m0, width)), scaled_end, MULT
+            )
 
-        def load_aniso(a, m0, width):
-            an = ring.tile([P, PACK, width], F32, name="an", tag="staged", bufs=3, align_bytes=64)
+        def load_aniso(a, m0):
+            an = ring.tile([P, PACK, BANK], F32, name="an", tag="staged", bufs=STAGED_BUFS, align_bytes=64)
             nc.sync.dma_start(
-                an[:], aniso[a * K_PASS : (a + 1) * K_PASS, m0 : m0 + width].rearrange("(i p) m -> p i m", p=P)
+                an[:], aniso[a * K_PASS : (a + 1) * K_PASS, m0 : m0 + BANK].rearrange("(i p) m -> p i m", p=P)
             )
             return an
 
-        def round_z(z_bf, an, prod, width, rounded_tile, banks, groups=((0, 1, 2, 3),)):
-            blocks = width // P
-            words = psum.tile([P, blocks, 2, P], F32, name="words", tag="words", bufs=1)
-            for b in range(blocks):
+        def round_z(z_bf, an, bond, rounded_tile, groups):
+            words = None
+            for b, block_groups in enumerate(groups):
                 cols = slice(b * P, (b + 1) * P)
                 zt_bf = None
-                for g, tiles in enumerate(groups):
-                    zt = psum.tile([P, PACK, P], F32, name="zt", tag="zt%d" % ((b + g) % banks), bufs=1)
-                    terms = [(i, an[:, i, cols]) for i in tiles] + [(i, prod[i][:, cols]) for i in tiles]
+                for tiles, bank in block_groups:
+                    zt = psum.tile([P, PACK, P], F32, name="zt", tag=bank)
+                    terms = [(i, an[:, i, cols]) for i in tiles] + [(i, bond[i][:, cols]) for i in tiles]
                     for n, (i, term) in enumerate(terms):
                         nc.tensor.matmul(
                             zt[:, i, :], term, identity[:],
@@ -198,69 +215,71 @@ def tile_list_garnet_bond_maximum_kernel(
                         )
                     if zt_bf is None:
                         zt_bf = rounded_tile()
-                    words_of = slice(32 * tiles[0], 32 * (tiles[-1] + 1))
+                    p_range = slice(32 * tiles[0], 32 * (tiles[-1] + 1))
+                    sums_by_word = zt[:].rearrange("m i r -> m (i r)").rearrange("m (p u e) -> m u p e", u=2, e=2)
                     nc.scalar.copy(
-                        zt_bf[:].rearrange("m (u p e) -> m u p e", u=2, e=2)[:, :, words_of, :],
-                        zt[:].rearrange("m i r -> m (i r)").rearrange("m (p u e) -> m u p e", u=2, e=2)[:, :, words_of, :],
+                        zt_bf[:].rearrange("m (u p e) -> m u p e", u=2, e=2)[:, :, p_range, :],
+                        sums_by_word[:, :, p_range, :],
                     )
+                if words is None:
+                    words = psum.tile([P, len(groups), 2, P], F32, name="words")
                 for u in range(2):
                     nc.tensor.transpose(words[:, b, u, :], zt_bf[:].bitcast(F32)[:, u * P : (u + 1) * P], identity[:])
             nc.scalar.copy(
-                z_bf.bitcast(F32).rearrange("p (b m u) -> p b m u", b=blocks, u=2),
+                z_bf.bitcast(F32).rearrange("p (b m u) -> p b m u", b=len(groups), u=2),
                 words[:].rearrange("p b u m -> p b m u"),
             )
 
-        x1 = {}
-        prod = [held.tile([P, M], F32, name="prod_%d" % i, align_bytes=64) for i in range(PACK)]
+        whole_end = {}
+        whole_bond = [held.tile([P, M], F32, name="bond_%d" % i, align_bytes=64) for i in range(PACK)]
 
-        def whole_first_end(t):
-            x1[t] = held.tile([P, M], F32, name="x1_%d" % t, tag="w1_raw%d_%d" % (2 + t // 2, t % 2), align_bytes=64)
-            first_end(x1[t][:], t, 0, M)
-
-        def whole_second_end(t):
-            second_end(prod[t][:], x1[t][:], t, 0, M)
+        def whole_first_end(t, piece):
+            whole_end[t] = held.tile([P, M], F32, name="end_%d" % t, tag=raw_tag(piece, t % 2), align_bytes=64)
+            nc.vector.tensor_copy(whole_end[t][:], first_end_of(t, 0, M))
+            nc.scalar.activation(whole_end[t][:], whole_end[t][:], COPY, scale=gain_cols[:, t : t + 1])
 
         halves = [
             held.tile([P, BANK], F32, name="h0_%d" % j, tag=tag, align_bytes=64)
-            for j, tag in enumerate(("h0_0", "w1_raw1_1"))
+            for j, tag in enumerate(("h0_0", raw_tag(1, 1)))
         ]
         sines(halves[0][:], 0, 0)
         scatter(halves[0][:], 0, 0, BANK)
-        w1_q[1] = quantize_weight(w1_raw[1], W1_WIDTHS[1], "w1_1", "w1_1")
+        quantize_w1(1)
         sines(halves[1][:], 0, BANK)
         scatter(halves[1][:], 0, BANK, BANK)
         sines_to_page(1)
-        for c in (2, 3):
-            t = 2 * (c - 2)
-            if c > 2:
+        for t in range(0, PACK, 2):
+            piece = 2 + t // 2
+            if t > 0:
                 sines_to_page(t)
                 sines_to_page(t + 1)
-            whole_first_end(t)
-            w1_q[c] = quantize_weight(w1_raw[c], W1_WIDTHS[c], "w1_%d" % c, "w1_%d" % c)
-            whole_first_end(t + 1)
-            whole_second_end(t)
-            whole_second_end(t + 1)
-        sines_to_page(4)
-        w3_raw = [load_rows(w3, a, 0, N, "w3_raw%d" % a, ring, "staged", 3) for a in range(PASSES)]
-        w3_codes, w3_scales = quantize_weight(w3_raw, N, "w3", "w1_3")
+            whole_first_end(t, piece)
+            quantize_w1(piece)
+            whole_first_end(t + 1, piece)
+            for tile_t in (t, t + 1):
+                second_end(whole_bond[tile_t][:], whole_end[tile_t][:], tile_t, 0, M)
+
+        widest = len(W1_WIDTHS) - 1
+        sines_to_page(PACK)
+        w3_raw = [load_rows(w3, a, 0, N, "w3_raw%d" % a, ring, "staged", STAGED_BUFS) for a in range(PASSES)]
+        w3_codes, w3_scales = quantize_weight(w3_raw, N, "w3", "w1_%d" % widest)
         w2_codes = held.tile([P, PASSES, 2 * N], U8, name="w2_codes", align_bytes=64)
         nc.sync.dma_start(w2_codes[:].bitcast(I32), w2_words.rearrange("a p b -> p a b").bitcast(I32))
         for t in range(PACK + 1, ROW_TILES - 1):
             sines_to_page(t)
         z0_bf = held.tile([P, M * PACK], BF16, name="z0_bf", align_bytes=64)
         for m0 in range(0, M, BANK):
-            an = load_aniso(0, m0, BANK)
+            an0 = load_aniso(0, m0)
             for d in range(0, BANK, 2 * P):
                 round_z(
                     z0_bf[:, (m0 + d) * PACK : (m0 + d + 2 * P) * PACK],
-                    an[:, :, d : d + 2 * P],
-                    [x[:, m0 + d : m0 + d + 2 * P] for x in prod],
-                    2 * P,
+                    an0[:, :, d : d + 2 * P],
+                    [x[:, m0 + d : m0 + d + 2 * P] for x in whole_bond],
                     lambda: ring.tile([P, K_PASS], BF16, name="zt_bf", bufs=3),
-                    2,
+                    [[((0, 1, 2, 3), "zt%d" % b)] for b in range(2)],
                 )
         sines_to_page(ROW_TILES - 1)
-        w2_plane = w1_q[3][1][:].rearrange("p (a n) -> p a n", a=PASSES)
+        w2_plane = w1_q[widest][1][:].rearrange("p (a n) -> p a n", a=PASSES)
         for q in range(4):
             nc.sync.dma_start(
                 w2_plane[32 * q : 32 * q + 4].bitcast(I32),
@@ -271,78 +290,69 @@ def tile_list_garnet_bond_maximum_kernel(
         nc.vector.quantize_mx(out=z0_codes[:].bitcast(FP8X4), scales=z0_scales[:], in_=z0_bf[:])
 
         out_view = out.rearrange("(t p) m -> p t m", p=P)
-        an1 = [load_aniso(1, m0, BANK) for m0 in range(0, M, BANK)]
-        ends1 = {}
+        an1 = [load_aniso(1, m0) for m0 in range(0, M, BANK)]
+        run_at = [{sum(runs[:j]): n for j, n in enumerate(runs)} for runs in END1_RUNS]
+        plain_end, scaled_end, bonds, z_rounded, y_banks, y_pairs = {}, {}, {}, {}, {}, {}
 
-        blocks = M // P
-        last = blocks - 1
+        def region_of(c):
+            return c % 2 if c < LAST else LAST_REGION
 
-        run_at = [{sum(runs[:j]): n for j, n in enumerate(runs)} for runs in END1_BLOCKS]
-        scaled = {}
-        bonds = {}
-        rounded = {}
-        sums = {}
-
-        def paced_tile(shape, dtype, name, parity, offset):
+        def paced_tile(shape, dtype, name, region, offset):
             return paced.tile(
-                shape, dtype, name="%s%d" % (name, parity), offset=4096 * parity + offset, align_bytes=64
+                shape, dtype, name="%s%d" % (name, region), offset=2 * TILE_BYTES * region + offset, align_bytes=64
             )
 
         def first_ends(c):
             for i in range(PACK):
                 count = run_at[i].get(c, 0)
                 if count > 1:
-                    x = held.tile([P, count * P], F32, name="ends", tag="prod_%d" % i, align_bytes=64)
-                    nc.vector.tensor_copy(x[:], pages[i][:].indirect(entries(end1_list, c * P, count * P)))
+                    run = held.tile([P, count * P], F32, name="run", tag="bond_%d" % i, align_bytes=64)
+                    nc.vector.tensor_copy(run[:], first_end_of(PACK + i, c * P, count * P))
                     for d in range(count):
-                        ends1[c + d, i] = x[:, d * P : (d + 1) * P]
+                        plain_end[c + d, i] = run[:, d * P : (d + 1) * P]
 
         def plain_tiles(c):
             return sorted((i for i in range(PACK) if run_at[i].get(c) != 1), key=lambda i: c + 1 not in run_at[i])
 
         def scale_ends(c):
-            tile = paced_tile([P, PACK, P], F32, "scaled", c % 2, 0)
+            tile = paced_tile([P, PACK, P], F32, "scaled", c % 2, SCALED_AT)
             for i in plain_tiles(c):
-                scaled[c, i] = tile[:, i, :]
-                nc.scalar.activation(scaled[c, i], ends1[c, i], COPY, scale=gain_cols[:, PACK + i : PACK + i + 1])
+                scaled_end[c, i] = tile[:, i, :]
+                nc.scalar.activation(
+                    scaled_end[c, i], plain_end[c, i], COPY, scale=gain_cols[:, PACK + i : PACK + i + 1]
+                )
 
         def fused_ends(c):
             fused = [i for i in range(PACK) if run_at[i].get(c) == 1]
             if fused:
-                tile = held.tile([P, PACK, P], F32, name="fused", tag="prod_%d" % plain_tiles(c)[0], align_bytes=64)
+                tile = held.tile([P, PACK, P], F32, name="fused", tag="bond_%d" % plain_tiles(c)[0], align_bytes=64)
                 for i in fused:
-                    scaled[c, i] = tile[:, i, :]
-                    nc.vector.tensor_tensor(
-                        scaled[c, i], pages[i][:].indirect(entries(end1_list, c * P, P)), gain_wide[:, i, :], MULT
-                    )
+                    scaled_end[c, i] = tile[:, i, :]
+                    nc.vector.tensor_tensor(scaled_end[c, i], first_end_of(PACK + i, c * P, P), gain_wide[i][:], MULT)
 
         def second_ends(c):
             bonds[c] = ring.tile([P, PACK, P], F32, name="bonds", align_bytes=64)
             for i in range(PACK):
-                second_end(bonds[c][:, i, :], scaled[c, i], PACK + i, c * P, P)
+                second_end(bonds[c][:, i, :], scaled_end[c, i], PACK + i, c * P, P)
 
         def round_block(c):
             m0 = c * P
-            if c == last - 1:
-                z_bf = held.tile([P, P * PACK], BF16, name="z_bf_late", tag="late0", align_bytes=64)
+            groups = [((0, 1, 2), "zt0"), ((3,), "zt1")] if c == LAST else [((0, 1, 2, 3), "zt0")]
+            if c == LAST - 1:
+                z_rounded[c] = held.tile([P, K_PASS], BF16, name="z_bf_late", align_bytes=64)
             else:
-                z_bf = ring.tile([P, P * PACK], BF16, name="z_bf", align_bytes=64)
+                z_rounded[c] = ring.tile([P, K_PASS], BF16, name="z_bf", align_bytes=64)
             round_z(
-                z_bf[:],
+                z_rounded[c][:],
                 an1[m0 // BANK][:, :, m0 % BANK : m0 % BANK + P],
                 [bonds[c][:, i, :] for i in range(PACK)],
-                P,
-                lambda: paced_tile([P, K_PASS], BF16, "zt_bf", c % 2 if c < last else 2, 1536),
-                2 if c == last else 1,
-                ((0, 1, 2), (3,)) if c == last else ((0, 1, 2, 3),),
+                lambda: paced_tile([P, K_PASS], BF16, "zt_bf", region_of(c), ROUNDED_AT),
+                [groups],
             )
-            rounded[c] = z_bf
-
-        banks = {}
 
         def products(c, a, z_codes, z_scales):
-            y2, y3 = banks[c]
-            for y in (y2, y3) if c >= last - 1 else (y3, y2):
+            y2, y3 = y_banks[c]
+            for y in (y2, y3) if c >= LAST - 1 else (y3, y2):
                 for n in range(OUT_TILES):
                     if y is y2:
                         lhs = w2_codes[:, a, 2 * n * P : 2 * (n + 1) * P].bitcast(FP4X4)
@@ -363,43 +373,44 @@ def tile_list_garnet_bond_maximum_kernel(
         def readouts(c):
             z_codes = ring.tile([P, P], U32, name="z_codes", align_bytes=64)
             z_scales = ring.tile([P, P], U8, name="z_scales", align_bytes=64)
-            nc.vector.quantize_mx(out=z_codes[:].bitcast(FP8X4), scales=z_scales[:], in_=rounded[c][:])
-            y2 = psum.tile([P, OUT_TILES, P], F32, name="y2", bufs=2)
-            y3 = psum.tile([P, OUT_TILES, P], F32, name="y3", bufs=3)
-            banks[c] = (y2, y3)
+            nc.vector.quantize_mx(out=z_codes[:].bitcast(FP8X4), scales=z_scales[:], in_=z_rounded[c][:])
+            y2 = psum.tile([P, OUT_TILES, P], F32, name="y2", bufs=Y2_BANKS)
+            y3 = psum.tile([P, OUT_TILES, P], F32, name="y3", bufs=Y3_BANKS)
+            y_banks[c] = (y2, y3)
             products(c, 0, z0_codes[:, c * P : (c + 1) * P], z0_scales[:, c * P : (c + 1) * P])
             products(c, 1, z_codes[:], z_scales[:])
 
+        def out_parts(c):
+            step = OUT_TILES // 2 if c == LAST else OUT_TILES
+            return [slice(n0, n0 + step) for n0 in range(0, OUT_TILES, step)]
+
         def copy_y2(c):
-            y2, y3 = banks[c]
-            if c == last:
+            y2, y3 = y_banks[c]
+            if c == LAST:
                 y2_sb = held.tile([P, OUT_TILES, P], F32, name="y2_last")
             else:
-                y2_sb = paced_tile([P, OUT_TILES, P], F32, "y2_sb", (c + 1) % 2 if c + 1 < last else 2, 2048)
-            step = OUT_TILES // 2 if c == last else OUT_TILES
-            for n0 in range(0, OUT_TILES, step):
-                nc.scalar.copy(y2_sb[:, n0 : n0 + step], y2[:, n0 : n0 + step])
-            sums[c] = (y2_sb, y3)
+                y2_sb = paced_tile([P, OUT_TILES, P], F32, "y2_sb", region_of(c + 1), Y2_AT)
+            for rows in out_parts(c):
+                nc.scalar.copy(y2_sb[:, rows], y2[:, rows])
+            y_pairs[c] = (y2_sb, y3)
 
         def store_maximum(c):
-            y2_sb, y3 = sums[c]
+            y2_sb, y3 = y_pairs[c]
             if c == LATE[0]:
-                best = held.tile([P, OUT_TILES, P], F32, name="best_late", tag="late0", align_bytes=64)
+                best = held.tile([P, OUT_TILES, P], F32, name="best_late", tag="z_bf_late", align_bytes=64)
             elif c == LATE[1]:
-                best = paced_tile([P, OUT_TILES, P], F32, "best_late", c % 2, 2048)
+                best = paced_tile([P, OUT_TILES, P], F32, "best_late", region_of(LATE[0] + 1), Y2_AT)
             elif c < LATE[0]:
-                best = ring.tile([P, OUT_TILES, P], F32, name="best", tag="h", bufs=4)
+                best = ring.tile([P, OUT_TILES, P], F32, name="best", tag="h", bufs=H_BUFS)
             else:
                 best = held.tile([P, OUT_TILES, P], F32, name="best%d" % c)
-            step = OUT_TILES // 2 if c == last else OUT_TILES
-            for n0 in range(0, OUT_TILES, step):
-                rows = slice(n0, n0 + step)
+            for rows in out_parts(c):
                 nc.vector.tensor_tensor(best[:, rows], y3[:, rows], y2_sb[:, rows], MAX)
                 nc.sync.dma_start(out_view[:, rows, c * P : (c + 1) * P], best[:, rows])
 
         first_ends(0)
         scale_ends(0)
-        for c in range(blocks):
+        for c in range(BLOCKS):
             if c >= 2:
                 readouts(c - 2)
             if c >= 3 and c - 3 not in LATE:
@@ -407,16 +418,16 @@ def tile_list_garnet_bond_maximum_kernel(
             fused_ends(c)
             first_ends(c + 1)
             second_ends(c)
-            if c < last:
+            if c < LAST:
                 scale_ends(c + 1)
             if c >= 2:
                 copy_y2(c - 2)
             round_block(c)
-        readouts(last - 1)
-        copy_y2(last - 1)
+        readouts(LAST - 1)
+        copy_y2(LAST - 1)
         for c in LATE:
             store_maximum(c)
-        readouts(last)
-        copy_y2(last)
-        store_maximum(last - 1)
-        store_maximum(last)
+        readouts(LAST)
+        copy_y2(LAST)
+        store_maximum(LAST - 1)
+        store_maximum(LAST)

@@ -43,6 +43,8 @@ TILE_BYTES = PACK * P * 4
 SCALED_AT, Y2_AT = 0, TILE_BYTES
 ROUNDED_AT = TILE_BYTES - K_PASS
 
+HEAD_PAGES = 2
+FIRST = 256
 H_BUFS = 4
 STAGED_BUFS = 3
 Y2_BANKS, Y3_BANKS = 2, 3
@@ -119,7 +121,7 @@ def tile_list_garnet_bond_maximum_kernel(
 
         identity = held.tile([P, P], F32, name="identity")
         make_identity(nc, identity[:])
-        pages = [held.tile([P, T2], F32, name="page%d" % t) for t in range(PAGES - 1)]
+        pages = [held.tile([P, T2], F32, name="page%d" % t) for t in range(HEAD_PAGES)]
         for page in pages:
             nc.vector.memset(page[:].bitcast(I32), 0)
 
@@ -133,13 +135,14 @@ def tile_list_garnet_bond_maximum_kernel(
             w1_q[piece] = quantize_weight(w1_raw[piece], W1_WIDTHS[piece], "w1_%d" % piece, "w1_%d" % piece)
 
         quantize_w1(0)
-        for j0 in range(0, S, BANK):
+        for j0, width in ((0, FIRST), (FIRST, S - FIRST)):
             nc.vector.tensor_copy(
-                v_codes[1][:, j0 : j0 + BANK], tab[1][:].bitcast(U32).indirect(entries(spin_list, j0, BANK))
+                v_codes[1][:, j0 : j0 + width], tab[1][:].bitcast(U32).indirect(entries(spin_list, j0, width))
             )
 
-        pages.append(held.tile([P, T2], F32, name="page_last", tag="tab1"))
-        nc.vector.memset(pages[-1][:].bitcast(I32), 0)
+        def zero_page_beside_scatter(tag):
+            pages.append(held.tile([P, T2], F32, name="page_late", tag=tag, align_bytes=64))
+            nc.gpsimd.memset(pages[-1][:].bitcast(I32), 0)
 
         end1_list = load_list("end1_list", offs3)
         end2_list = load_list("end2_list", offs4)
@@ -157,18 +160,18 @@ def tile_list_garnet_bond_maximum_kernel(
                 gain_wide[i][:], identity[:], IDENTITY, bias=gain_cols[:, PACK + i : PACK + i + 1], scale=0.0
             )
 
-        def sines(h, t, j0):
+        def sines(h, t, j0, width=BANK):
             piece = max(x for x in range(len(W1_WIDTHS)) if w1_starts[x] <= t * P)
             codes, scales = w1_q[piece]
-            angles = psum.tile([P, BANK], F32, name="angles", tag="y3", bufs=Y3_BANKS)
+            angles = psum.tile([P, width], F32, name="angles", tag="y3", bufs=Y3_BANKS)
             for a in range(PASSES):
                 col = a * W1_WIDTHS[piece] + t * P - w1_starts[piece]
                 nc.tensor.matmul_mx(
                     out=angles[:],
                     lhsT=codes[:, col : col + P].bitcast(FP8X4),
                     lhsT_scale=scales[:, col : col + P],
-                    rhs=v_codes[a][:, j0 : j0 + BANK].bitcast(FP8X4),
-                    rhs_scale=v_scales[4 * a :, j0 : j0 + BANK],
+                    rhs=v_codes[a][:, j0 : j0 + width].bitcast(FP8X4),
+                    rhs_scale=v_scales[4 * a :, j0 : j0 + width],
                     start=(a == 0),
                     stop=(a == PASSES - 1),
                 )
@@ -239,14 +242,17 @@ def tile_list_garnet_bond_maximum_kernel(
             nc.scalar.activation(whole_end[t][:], whole_end[t][:], COPY, scale=gain_cols[:, t : t + 1])
 
         halves = [
-            held.tile([P, BANK], F32, name="h0_%d" % j, tag=tag, align_bytes=64)
-            for j, tag in enumerate(("h0_0", raw_tag(1, 1)))
+            held.tile([P, width], F32, name=tag + "_h", tag=tag, align_bytes=64)
+            for width, tag in ((FIRST, "h0_0"), (S - FIRST, raw_tag(1, 1)))
         ]
-        sines(halves[0][:], 0, 0)
-        scatter(halves[0][:], 0, 0, BANK)
+        sines(halves[0][:], 0, 0, FIRST)
+        scatter(halves[0][:], 0, 0, FIRST)
         quantize_w1(1)
-        sines(halves[1][:], 0, BANK)
-        scatter(halves[1][:], 0, BANK, BANK)
+        zero_page_beside_scatter("w1_1")
+        sines(halves[1][:, 0:FIRST], 0, FIRST, FIRST)
+        sines(halves[1][:, FIRST:], 0, BANK)
+        scatter(halves[1][:], 0, FIRST, S - FIRST)
+        zero_page_beside_scatter(raw_tag(1, 1))
         sines_to_page(1)
         for t in range(0, PACK, 2):
             piece = 2 + t // 2

@@ -32,22 +32,24 @@ LAST = BLOCKS - 1
 PAGES = PACK
 
 W1_WIDTHS = (128, 128, 256, 512)
-
-END1_RUNS = ((2, 2, 2, 2), (2, 2, 2, 1, 1), (3, 2, 2, 1), (3, 2, 2, 1))
-FUSED_TILES = tuple(i for i in range(PACK) if 1 in END1_RUNS[i])
-
-LATE = (LAST - 3, LAST - 2)
-
-LAST_REGION = 2
-TILE_BYTES = PACK * P * 4
-SCALED_AT, Y2_AT = 0, TILE_BYTES
-ROUNDED_AT = TILE_BYTES - K_PASS
-
-HEAD_PAGES = 2
 FIRST = 256
-H_BUFS = 4
+HALF = M // 2
+KIB = 1024
+PAGE_BYTES = T2 * 4
+HEAD_PAGES = 2
+
+PAGE_AT = {t: (t - HEAD_PAGES) * PAGE_BYTES for t in range(HEAD_PAGES, ROW_TILES)}
+ROUNDED_W1_AT = {1: PAGE_AT[2], 2: PAGE_AT[4] - 2 * KIB, 3: PAGE_AT[6] - 4 * KIB}
+RAW_W1_AT = {(0, 0): PAGE_AT[2] + 2 * KIB, (0, 1): PAGE_AT[2] + 4 * KIB, (2, 0): PAGE_AT[3], (3, 1): PAGE_AT[7]}
+V_CODES_AT = PAGE_AT[7] + PAGE_BYTES + 2 * KIB
+END_AT = (V_CODES_AT + 4 * KIB, V_CODES_AT + 2 * KIB, V_CODES_AT)
+AFTER_BA_AT = V_CODES_AT + 12 * KIB
+ROUNDED_BA_AT = AFTER_BA_AT + 8 * KIB - KIB // 2
+PLAIN_D4_AT = ROUNDED_BA_AT + KIB
+LAST_AT = V_CODES_AT + 15 * KIB
+ROUNDED_BB_AT = PLAIN_D4_AT + 2 * KIB + KIB // 2
 STAGED_BUFS = 3
-Y2_BANKS, Y3_BANKS = 2, 3
+BOND_BUFS = 3
 
 
 def tile_list_garnet_bond_maximum_kernel(
@@ -57,7 +59,7 @@ def tile_list_garnet_bond_maximum_kernel(
     with ExitStack() as ctx:
         held = ctx.enter_context(tc.tile_pool(name="held", bufs=1))
         ring = ctx.enter_context(tc.tile_pool(name="ring", bufs=2))
-        paced = ctx.enter_context(tc.tile_pool(name="paced", bufs=1))
+        laid = ctx.enter_context(tc.tile_pool(name="laid", bufs=1))
         psum = ctx.enter_context(tc.psum_pool(name="psum", bufs=1))
 
         def load_list(name, dram):
@@ -68,31 +70,40 @@ def tile_list_garnet_bond_maximum_kernel(
         def entries(tile, start, count):
             return tile[:, start // 16 : (start + count) // 16]
 
-        def load_rows(w, a, c0, width, name, pool, tag, bufs):
-            raw = pool.tile([P, PACK, width], F32, name=name, tag=tag, bufs=bufs, align_bytes=64)
+        def laid_tile(shape, dtype, name, offset):
+            return laid.tile(shape, dtype, name=name, offset=offset, align_bytes=64)
+
+        def held_tile(shape, dtype, name, tag=None):
+            return held.tile(shape, dtype, name=name, tag=tag or name, align_bytes=64)
+
+        def load_rows(raw, w, a, c0, width):
             nc.sync.dma_start(
                 raw[:], w[a * K_PASS : (a + 1) * K_PASS, c0 : c0 + width].rearrange("(p i) c -> p i c", i=PACK)
             )
             return raw
 
-        def quantize_weight(raws, width, name, tag):
-            grouped = held.tile([P, PASSES, width, PACK], BF16, name=name + "_bf16", tag=tag, align_bytes=64)
+        def quantize(bf16_values, name, codes_at=None):
+            width = bf16_values.shape[1] // PACK
+            if codes_at is None:
+                codes = held_tile([P, width], U32, name + "_codes")
+            else:
+                codes = laid_tile([P, width], U32, name + "_codes", codes_at)
+            scales = held_tile([P, width], U8, name + "_scales")
+            nc.vector.quantize_mx(out=codes[:].bitcast(FP8X4), scales=scales[:], in_=bf16_values)
+            return codes, scales
+
+        def quantize_weight(raws, grouped, name):
             for a in range(PASSES):
                 nc.scalar.copy(
                     grouped[:, a].rearrange("p (c q) i -> p c i q", q=4),
                     raws[a][:].rearrange("p i (c q) -> p c i q", q=4),
                 )
-            codes = held.tile([P, PASSES * width], U32, name=name + "_codes", align_bytes=64)
-            scales = held.tile([P, PASSES * width], U8, name=name + "_scales", align_bytes=64)
-            nc.vector.quantize_mx(
-                out=codes[:].bitcast(FP8X4), scales=scales[:], in_=grouped[:].rearrange("p a c i -> p (a c i)")
-            )
-            return codes, scales
+            return quantize(grouped[:].rearrange("p a c i -> p (a c i)"), name)
 
         tab_plane = held.tile([P, T], U8, name="tab_plane")
         nc.vector.memset(tab_plane[:].bitcast(I32), 0)
         spin_list = load_list("spin_list", offs)
-        tab = [held.tile([P, T], I32, name="tab%d" % a) for a in range(PASSES)]
+        tab = [held_tile([P, T], I32, "tab%d" % a) for a in range(PASSES)]
         nc.sync.dma_start(tab[0][:], tab_words[0].rearrange("p t i -> p (t i)").bitcast(I32))
         for q in range(4):
             nc.sync.dma_start(
@@ -102,37 +113,47 @@ def tile_list_garnet_bond_maximum_kernel(
         w1_starts = [sum(W1_WIDTHS[:piece]) for piece in range(len(W1_WIDTHS))]
         w1_raw = {}
 
-        def raw_tag(piece, a):
-            return "w1_raw%d_%d" % (piece, a)
-
         def load_w1(piece):
-            w1_raw[piece] = [
-                load_rows(w1, a, w1_starts[piece], W1_WIDTHS[piece], raw_tag(piece, a), held, raw_tag(piece, a), 1)
-                for a in range(PASSES)
-            ]
+            w1_raw[piece] = []
+            for a in range(PASSES):
+                shape, name = [P, PACK, W1_WIDTHS[piece]], "w1_raw%d_%d" % (piece, a)
+                if (piece, a) in RAW_W1_AT:
+                    raw = laid_tile(shape, F32, name, RAW_W1_AT[piece, a])
+                else:
+                    raw = held_tile(shape, F32, name)
+                w1_raw[piece].append(load_rows(raw, w1, a, w1_starts[piece], W1_WIDTHS[piece]))
 
         load_w1(0)
         nc.sync.dma_start(tab[1][:], tab_words[1].rearrange("p t i -> p (t i)").bitcast(I32))
         site_list = load_list("site_list", offs2)
-        wgs_sb = held.tile([P, S], F32, name="wgs_sb")
+        wgs_sb = held_tile([P, S], F32, "wgs_sb")
         nc.sync.dma_start(wgs_sb[:], wgs)
         for piece in range(1, len(W1_WIDTHS)):
             load_w1(piece)
 
         identity = held.tile([P, P], F32, name="identity")
         make_identity(nc, identity[:])
-        pages = [held.tile([P, T2], F32, name="page%d" % t) for t in range(HEAD_PAGES)]
-        for page in pages:
-            nc.vector.memset(page[:].bitcast(I32), 0)
+        pages = {t: held.tile([P, T2], F32, name="page%d" % t) for t in range(HEAD_PAGES)}
+        for t in range(HEAD_PAGES):
+            nc.vector.memset(pages[t][:].bitcast(I32), 0)
 
-        v_scales = held.tile([P, S], U8, name="v_scales", align_bytes=64)
-        v_codes = [held.tile([P, S], U32, name="v_codes%d" % a, align_bytes=64) for a in range(PASSES)]
+        def zero_page(t):
+            pages[t] = laid_tile([P, T2], F32, "page%d" % t, PAGE_AT[t])
+            nc.gpsimd.memset(pages[t][:].bitcast(I32), 0)
+
+        v_scales = held_tile([P, S], U8, "v_scales")
+        v_codes = [laid_tile([P, S], U32, "v_codes%d" % a, V_CODES_AT + a * 4 * KIB) for a in range(PASSES)]
         nc.vector.tensor_copy(v_codes[0][:], tab[0][:].bitcast(U32).indirect(spin_list[:]))
         nc.vector.tensor_copy(v_scales[:], tab_plane[:].indirect(spin_list[:]))
         w1_q = {}
 
         def quantize_w1(piece):
-            w1_q[piece] = quantize_weight(w1_raw[piece], W1_WIDTHS[piece], "w1_%d" % piece, "w1_%d" % piece)
+            shape, name = [P, PASSES, W1_WIDTHS[piece], PACK], "w1_%d" % piece
+            if piece in ROUNDED_W1_AT:
+                grouped = laid_tile(shape, BF16, name + "_bf16", ROUNDED_W1_AT[piece])
+            else:
+                grouped = held_tile(shape, BF16, name + "_bf16")
+            w1_q[piece] = quantize_weight(w1_raw[piece], grouped, name)
 
         quantize_w1(0)
         for j0, width in ((0, FIRST), (FIRST, S - FIRST)):
@@ -140,30 +161,13 @@ def tile_list_garnet_bond_maximum_kernel(
                 v_codes[1][:, j0 : j0 + width], tab[1][:].bitcast(U32).indirect(entries(spin_list, j0, width))
             )
 
-        def zero_page_beside_scatter(tag):
-            pages.append(held.tile([P, T2], F32, name="page_late", tag=tag, align_bytes=64))
-            nc.gpsimd.memset(pages[-1][:].bitcast(I32), 0)
+        angle_banks = ["y0", "y1", "y2", "y3"]
 
-        end1_list = load_list("end1_list", offs3)
-        end2_list = load_list("end2_list", offs4)
-
-        gain_rows = w1_raw[0][0][:, 0, :]
-        nc.sync.dma_start(gain_rows[0:ROW_TILES, :], gain.rearrange("(t p) -> t p", p=P))
-        gain_psum = psum.tile([P, P], F32, name="gain_psum", tag="words")
-        nc.tensor.transpose(gain_psum[:], gain_rows, identity[:])
-        gain_cols = held.tile([P, ROW_TILES], F32, name="gain_cols")
-        nc.scalar.copy(gain_cols[:], gain_psum[:, 0:ROW_TILES])
-        gain_wide = {}
-        for i in FUSED_TILES:
-            gain_wide[i] = held.tile([P, P], F32, name="gain_wide%d" % i)
-            nc.scalar.activation(
-                gain_wide[i][:], identity[:], IDENTITY, bias=gain_cols[:, PACK + i : PACK + i + 1], scale=0.0
-            )
-
-        def sines(h, t, j0, width=BANK):
+        def sines(h, t, j0, width):
             piece = max(x for x in range(len(W1_WIDTHS)) if w1_starts[x] <= t * P)
             codes, scales = w1_q[piece]
-            angles = psum.tile([P, width], F32, name="angles", tag="y3", bufs=Y3_BANKS)
+            angle_banks.append(angle_banks.pop(0))
+            angles = psum.tile([P, width], F32, name="angles", tag=angle_banks[-1])
             for a in range(PASSES):
                 col = a * W1_WIDTHS[piece] + t * P - w1_starts[piece]
                 nc.tensor.matmul_mx(
@@ -179,261 +183,314 @@ def tile_list_garnet_bond_maximum_kernel(
 
         def scatter(h, t, j0, width):
             nc.vector.tensor_tensor(
-                pages[t % PAGES][:].indirect(entries(site_list, j0, width)), h, wgs_sb[:, j0 : j0 + width], MULT
+                pages[t][:].indirect(entries(site_list, j0, width)), h, wgs_sb[:, j0 : j0 + width], MULT
             )
 
-        def sines_to_page(t):
-            h = ring.tile([P, S], F32, name="h", bufs=H_BUFS)
+        def sines_to_page(t, h):
             for j0 in range(0, S, BANK):
-                sines(h[:, j0 : j0 + BANK], t, j0)
+                sines(h[:, j0 : j0 + BANK], t, j0, BANK)
             scatter(h[:], t, 0, S)
 
-        def first_end_of(t, m0, width):
-            return pages[t % PAGES][:].indirect(entries(end1_list, m0, width))
-
-        def second_end(bond, scaled_end, t, m0, width):
-            nc.vector.tensor_tensor(
-                bond, pages[t % PAGES][:].indirect(entries(end2_list, m0, width)), scaled_end, MULT
-            )
-
-        def load_aniso(a, m0):
-            an = ring.tile([P, PACK, BANK], F32, name="an", tag="staged", bufs=STAGED_BUFS, align_bytes=64)
-            nc.sync.dma_start(
-                an[:], aniso[a * K_PASS : (a + 1) * K_PASS, m0 : m0 + BANK].rearrange("(i p) m -> p i m", p=P)
-            )
-            return an
-
-        def round_z(z_bf, an, bond, rounded_tile, groups):
-            words = None
-            for b, block_groups in enumerate(groups):
-                cols = slice(b * P, (b + 1) * P)
-                zt_bf = None
-                for tiles, bank in block_groups:
-                    zt = psum.tile([P, PACK, P], F32, name="zt", tag=bank)
-                    terms = [(i, an[:, i, cols]) for i in tiles] + [(i, bond[i][:, cols]) for i in tiles]
-                    for n, (i, term) in enumerate(terms):
-                        nc.tensor.matmul(
-                            zt[:, i, :], term, identity[:],
-                            start=(n == 0), stop=(n == len(terms) - 1), is_transpose=True,
-                        )
-                    if zt_bf is None:
-                        zt_bf = rounded_tile()
-                    p_range = slice(32 * tiles[0], 32 * (tiles[-1] + 1))
-                    sums_by_word = zt[:].rearrange("m i r -> m (i r)").rearrange("m (p u e) -> m u p e", u=2, e=2)
-                    nc.scalar.copy(
-                        zt_bf[:].rearrange("m (u p e) -> m u p e", u=2, e=2)[:, :, p_range, :],
-                        sums_by_word[:, :, p_range, :],
-                    )
-                if words is None:
-                    words = psum.tile([P, len(groups), 2, P], F32, name="words")
-                for u in range(2):
-                    nc.tensor.transpose(words[:, b, u, :], zt_bf[:].bitcast(F32)[:, u * P : (u + 1) * P], identity[:])
-            nc.scalar.copy(
-                z_bf.bitcast(F32).rearrange("p (b m u) -> p b m u", b=len(groups), u=2),
-                words[:].rearrange("p b u m -> p b m u"),
-            )
-
-        whole_end = {}
-        whole_bond = [held.tile([P, M], F32, name="bond_%d" % i, align_bytes=64) for i in range(PACK)]
-
-        def whole_first_end(t, piece):
-            whole_end[t] = held.tile([P, M], F32, name="end_%d" % t, tag=raw_tag(piece, t % 2), align_bytes=64)
-            nc.vector.tensor_copy(whole_end[t][:], first_end_of(t, 0, M))
-            nc.scalar.activation(whole_end[t][:], whole_end[t][:], COPY, scale=gain_cols[:, t : t + 1])
-
-        halves = [
-            held.tile([P, width], F32, name=tag + "_h", tag=tag, align_bytes=64)
-            for width, tag in ((FIRST, "h0_0"), (S - FIRST, raw_tag(1, 1)))
-        ]
-        sines(halves[0][:], 0, 0, FIRST)
-        scatter(halves[0][:], 0, 0, FIRST)
+        h_first = held_tile([P, FIRST], F32, "h_first")
+        sines(h_first[:], 0, 0, FIRST)
+        scatter(h_first[:], 0, 0, FIRST)
         quantize_w1(1)
-        zero_page_beside_scatter("w1_1")
-        sines(halves[1][:, 0:FIRST], 0, FIRST, FIRST)
-        sines(halves[1][:, FIRST:], 0, BANK)
-        scatter(halves[1][:], 0, FIRST, S - FIRST)
-        zero_page_beside_scatter(raw_tag(1, 1))
-        sines_to_page(1)
-        for t in range(0, PACK, 2):
-            piece = 2 + t // 2
-            if t > 0:
-                sines_to_page(t)
-                sines_to_page(t + 1)
-            whole_first_end(t, piece)
-            quantize_w1(piece)
-            whole_first_end(t + 1, piece)
-            for tile_t in (t, t + 1):
-                second_end(whole_bond[tile_t][:], whole_end[tile_t][:], tile_t, 0, M)
+        zero_page(2)
+        h_rest = held_tile([P, S - FIRST], F32, "h_rest", "w1_raw1_1")
+        sines(h_rest[:, 0:FIRST], 0, FIRST, FIRST)
+        sines(h_rest[:, FIRST:], 0, BANK, BANK)
+        scatter(h_rest[:], 0, FIRST, S - FIRST)
+        quantize_w1(2)
+        zero_page(3)
+        zero_page(4)
+        sines_to_page(1, held_tile([P, S], F32, "h1", "w1_raw2_1"))
+        quantize_w1(3)
+        zero_page(5)
+        zero_page(6)
+        sines_to_page(2, laid_tile([P, S], F32, "h2", PAGE_AT[7]))
+        zero_page(7)
+        for t in range(3, ROW_TILES):
+            sines_to_page(t, held_tile([P, S], F32, "h%d" % t, "w1_raw1_1" if t % 2 else "w1_raw2_1"))
 
-        widest = len(W1_WIDTHS) - 1
-        sines_to_page(PACK)
-        w3_raw = [load_rows(w3, a, 0, N, "w3_raw%d" % a, ring, "staged", STAGED_BUFS) for a in range(PASSES)]
-        w3_codes, w3_scales = quantize_weight(w3_raw, N, "w3", "w1_%d" % widest)
-        w2_codes = held.tile([P, PASSES, 2 * N], U8, name="w2_codes", align_bytes=64)
+        end1_list = load_list("end1_list", offs3)
+        end2_list = load_list("end2_list", offs4)
+        gain_rows = w1_raw[1][0][:, 0, :]
+        nc.sync.dma_start(gain_rows[0:ROW_TILES, :], gain.rearrange("(t p) -> t p", p=P))
+        gain_psum = psum.tile([P, P], F32, name="gain_psum", tag="w0")
+        nc.tensor.transpose(gain_psum[:], gain_rows, identity[:])
+        gain_cols = held.tile([P, ROW_TILES], F32, name="gain_cols")
+        nc.scalar.copy(gain_cols[:], gain_psum[:, 0:ROW_TILES])
+
+        def staged(name):
+            return ring.tile([P, PACK, BANK], F32, name=name, tag="staged", bufs=STAGED_BUFS, align_bytes=64)
+
+        w3_raw = [load_rows(staged("w3_raw"), w3, a, 0, N) for a in range(PASSES)]
+        w3_codes, w3_scales = quantize_weight(
+            w3_raw, held_tile([P, PASSES, N, PACK], BF16, "w3_bf16", "w1_raw3_0"), "w3"
+        )
+        gain_wide = [held_tile([P, PACK, HALF], F32, "gain_wide%d" % a, "tab%d" % a) for a in range(PASSES)]
+        for t in range(ROW_TILES):
+            nc.scalar.activation(
+                gain_wide[t // PACK][:, t % PACK, :], wgs_sb[:, 0:HALF], IDENTITY,
+                bias=gain_cols[:, t : t + 1], scale=0.0,
+            )
+        w2_codes = held_tile([P, PASSES, 2 * N], U8, "w2_codes")
         nc.sync.dma_start(w2_codes[:].bitcast(I32), w2_words.rearrange("a p b -> p a b").bitcast(I32))
-        for t in range(PACK + 1, ROW_TILES - 1):
-            sines_to_page(t)
-        z0_bf = held.tile([P, M * PACK], BF16, name="z0_bf", align_bytes=64)
-        for m0 in range(0, M, BANK):
-            an0 = load_aniso(0, m0)
-            for d in range(0, BANK, 2 * P):
-                round_z(
-                    z0_bf[:, (m0 + d) * PACK : (m0 + d + 2 * P) * PACK],
-                    an0[:, :, d : d + 2 * P],
-                    [x[:, m0 + d : m0 + d + 2 * P] for x in whole_bond],
-                    lambda: ring.tile([P, K_PASS], BF16, name="zt_bf", bufs=3),
-                    [[((0, 1, 2, 3), "zt%d" % b)] for b in range(2)],
-                )
-        sines_to_page(ROW_TILES - 1)
-        w2_plane = w1_q[widest][1][:].rearrange("p (a n) -> p a n", a=PASSES)
+        w2_plane = w1_q[3][1][:].rearrange("p (a n) -> p a n", a=PASSES)
         for q in range(4):
             nc.sync.dma_start(
                 w2_plane[32 * q : 32 * q + 4].bitcast(I32),
                 w2_scales[:, 4 * q : 4 * q + 4, :].rearrange("a r n -> r a n").bitcast(I32),
             )
-        z0_codes = held.tile([P, M], U32, name="z0_codes", align_bytes=64)
-        z0_scales = held.tile([P, M], U8, name="z0_scales", align_bytes=64)
-        nc.vector.quantize_mx(out=z0_codes[:].bitcast(FP8X4), scales=z0_scales[:], in_=z0_bf[:])
-
-        out_view = out.rearrange("(t p) m -> p t m", p=P)
-        an1 = [load_aniso(1, m0) for m0 in range(0, M, BANK)]
-        run_at = [{sum(runs[:j]): n for j, n in enumerate(runs)} for runs in END1_RUNS]
-        plain_end, scaled_end, bonds, z_rounded, y_banks, y_pairs = {}, {}, {}, {}, {}, {}
-
-        def region_of(c):
-            return c % 2 if c < LAST else LAST_REGION
-
-        def paced_tile(shape, dtype, name, region, offset):
-            return paced.tile(
-                shape, dtype, name="%s%d" % (name, region), offset=2 * TILE_BYTES * region + offset, align_bytes=64
-            )
-
-        def first_ends(c):
-            for i in range(PACK):
-                count = run_at[i].get(c, 0)
-                if count > 1:
-                    run = held.tile([P, count * P], F32, name="run", tag="bond_%d" % i, align_bytes=64)
-                    nc.vector.tensor_copy(run[:], first_end_of(PACK + i, c * P, count * P))
-                    for d in range(count):
-                        plain_end[c + d, i] = run[:, d * P : (d + 1) * P]
-
-        def plain_tiles(c):
-            return sorted((i for i in range(PACK) if run_at[i].get(c) != 1), key=lambda i: c + 1 not in run_at[i])
-
-        def scale_ends(c):
-            tile = paced_tile([P, PACK, P], F32, "scaled", c % 2, SCALED_AT)
-            for i in plain_tiles(c):
-                scaled_end[c, i] = tile[:, i, :]
-                nc.scalar.activation(
-                    scaled_end[c, i], plain_end[c, i], COPY, scale=gain_cols[:, PACK + i : PACK + i + 1]
+        an = {}
+        for m0 in (0, HALF):
+            for a in range(PASSES):
+                an[a, m0] = staged("an")
+                nc.sync.dma_start(
+                    an[a, m0][:],
+                    aniso[a * K_PASS : (a + 1) * K_PASS, m0 : m0 + HALF].rearrange("(i p) m -> p i m", p=P),
                 )
 
-        def fused_ends(c):
-            fused = [i for i in range(PACK) if run_at[i].get(c) == 1]
-            if fused:
-                tile = held.tile([P, PACK, P], F32, name="fused", tag="bond_%d" % plain_tiles(c)[0], align_bytes=64)
-                for i in fused:
-                    scaled_end[c, i] = tile[:, i, :]
-                    nc.vector.tensor_tensor(scaled_end[c, i], first_end_of(PACK + i, c * P, P), gain_wide[i][:], MULT)
-
-        def second_ends(c):
-            bonds[c] = ring.tile([P, PACK, P], F32, name="bonds", align_bytes=64)
-            for i in range(PACK):
-                second_end(bonds[c][:, i, :], scaled_end[c, i], PACK + i, c * P, P)
-
-        def round_block(c):
-            m0 = c * P
-            groups = [((0, 1, 2), "zt0"), ((3,), "zt1")] if c == LAST else [((0, 1, 2, 3), "zt0")]
-            if c == LAST - 1:
-                z_rounded[c] = held.tile([P, K_PASS], BF16, name="z_bf_late", align_bytes=64)
-            else:
-                z_rounded[c] = ring.tile([P, K_PASS], BF16, name="z_bf", align_bytes=64)
-            round_z(
-                z_rounded[c][:],
-                an1[m0 // BANK][:, :, m0 % BANK : m0 % BANK + P],
-                [bonds[c][:, i, :] for i in range(PACK)],
-                lambda: paced_tile([P, K_PASS], BF16, "zt_bf", region_of(c), ROUNDED_AT),
-                [groups],
+        def first_end(end, t, m0, width):
+            nc.vector.tensor_tensor(
+                end, pages[t][:].indirect(entries(end1_list, m0, width)),
+                gain_wide[t // PACK][:, t % PACK, 0:width], MULT,
             )
 
-        def products(c, a, z_codes, z_scales):
-            y2, y3 = y_banks[c]
-            for y in (y2, y3) if c >= LAST - 1 else (y3, y2):
-                for n in range(OUT_TILES):
-                    if y is y2:
-                        lhs = w2_codes[:, a, 2 * n * P : 2 * (n + 1) * P].bitcast(FP4X4)
-                        lhs_scale = w2_plane[:, a, n * P : (n + 1) * P]
-                    else:
-                        lhs = w3_codes[:, a * N + n * P : a * N + (n + 1) * P].bitcast(FP8X4)
-                        lhs_scale = w3_scales[:, a * N + n * P : a * N + (n + 1) * P]
-                    nc.tensor.matmul_mx(
-                        out=y[:, n, :],
-                        lhsT=lhs,
-                        lhsT_scale=lhs_scale,
-                        rhs=z_codes.bitcast(FP8X4),
-                        rhs_scale=z_scales,
-                        start=(a == 0 and n == 0),
-                        stop=(a == PASSES - 1 and n == OUT_TILES - 1),
+        def plain_first_end(end, t, m0, width):
+            nc.vector.tensor_copy(end, pages[t][:].indirect(entries(end1_list, m0, width)))
+
+        def scale_end(scaled, end, t):
+            nc.scalar.activation(scaled, end, COPY, scale=gain_cols[:, t : t + 1])
+
+        def second_end(bond, end, t, m0, width):
+            nc.vector.tensor_tensor(bond, pages[t][:].indirect(entries(end2_list, m0, width)), end, MULT)
+
+        def sum_and_round(rounded, bank, tiles, bonds, m0, blocks):
+            a, count = tiles[0] // PACK, len(tiles)
+            zt = psum.tile([P, blocks, count, P], F32, name="zt", tag=bank)
+            aniso_half = an[a, m0 // HALF * HALF]
+            terms = []
+            for b in range(blocks):
+                c0 = m0 % HALF + b * P
+                terms.extend((b, j, aniso_half[:, t % PACK, c0 : c0 + P]) for j, t in enumerate(tiles))
+            for j in range(count):
+                terms.extend((b, j, bonds[j][:, b * P : (b + 1) * P]) for b in range(blocks))
+            for n, (b, j, term) in enumerate(terms):
+                nc.tensor.matmul(
+                    zt[:, b, j, :], term, identity[:], start=(n == 0), stop=(n == len(terms) - 1), is_transpose=True
+                )
+            p0 = 32 * (tiles[0] % PACK)
+            nc.scalar.copy(
+                rounded[:].rearrange("m b (u p e) -> m b u p e", u=2, e=2)[:, :, :, p0 : p0 + 32 * count, :],
+                zt[:].rearrange("m b j r -> m b (j r)").rearrange("m b (p u e) -> m b u p e", u=2, e=2),
+            )
+
+        def to_words(rounded, blocks, banks):
+            z_bf = ring.tile([P, blocks * K_PASS], BF16, name="z_bf", align_bytes=64)
+            for b0 in range(0, blocks, 2):
+                count = min(2, blocks - b0)
+                words = psum.tile([P, count, 2, P], F32, name="words", tag=banks[b0 // 2])
+                for b in range(count):
+                    for u in range(2):
+                        nc.tensor.transpose(
+                            words[:, b, u, :], rounded[:, b0 + b, :].bitcast(F32)[:, u * P : (u + 1) * P], identity[:]
+                        )
+                nc.scalar.copy(
+                    z_bf[:, b0 * K_PASS : (b0 + count) * K_PASS].bitcast(F32).rearrange(
+                        "p (b m u) -> p b m u", b=count, u=2
+                    ),
+                    words[:].rearrange("p b u m -> p b m u"),
+                )
+            return z_bf
+
+        def product_pass(y, which, a, n, z, c0, width, start, stop):
+            codes, scales = z
+            if which == 2:
+                lhs = w2_codes[:, a, 2 * n * P : 2 * (n + 1) * P].bitcast(FP4X4)
+                lhs_scale = w2_plane[:, a, n * P : (n + 1) * P]
+            else:
+                lhs = w3_codes[:, a * N + n * P : a * N + (n + 1) * P].bitcast(FP8X4)
+                lhs_scale = w3_scales[:, a * N + n * P : a * N + (n + 1) * P]
+            nc.tensor.matmul_mx(
+                out=y, lhsT=lhs, lhsT_scale=lhs_scale, rhs=codes[:, c0 : c0 + width].bitcast(FP8X4),
+                rhs_scale=scales[:, c0 : c0 + width], start=start, stop=stop,
+            )
+
+        out_view = out.rearrange("(t p) m -> p t m", p=P)
+
+        def maximum(best, y3, y2, rows, m0, width):
+            nc.vector.tensor_tensor(best, y3, y2, MAX)
+            nc.sync.dma_start(out_view[:, rows, m0 : m0 + width], best)
+
+        ends, bonds = {}, {}
+
+        def end_slot(slot, shape):
+            return laid_tile(shape, F32, "end%d" % slot, END_AT[slot])
+
+        def ring_bond():
+            return ring.tile([P, HALF], F32, name="bond", bufs=BOND_BUFS, align_bytes=64)
+
+        rounded_a = [held_tile([P, PACK, K_PASS], BF16, "rounded_a%d" % a) for a in range(PASSES)]
+        z_a = {}
+        y_a = {}
+
+        def half_products(n, a):
+            if a == 0:
+                y_a[n] = [psum.tile([P, HALF], F32, name="y_a", tag="y%d" % (2 * (n % 2) + j)) for j in range(2)]
+            for j in range(2):
+                product_pass(y_a[n][j][:], 2 + j, a, n, z_a[a], 0, HALF, a == 0, a == PASSES - 1)
+
+        def first_a(t):
+            ends[t] = end_slot(t % 3, [P, HALF])
+            first_end(ends[t][:], t, 0, HALF)
+
+        def second_a(t):
+            if t == 5:
+                bonds["late"] = held_tile([P, 3, HALF], F32, "bonds_a567", "rounded_a0")
+            bond = bonds["late"][:, t - 5, :] if t >= 5 else ring_bond()[:]
+            second_end(bond, ends[t][:], t, 0, HALF)
+            sum_and_round(rounded_a[t // PACK], "z%d" % (t % 2), [t], [bond], 0, PACK)
+
+        first_a(0)
+        for t in range(ROW_TILES - 1):
+            first_a(t + 1)
+            second_a(t)
+            if t == PACK - 1:
+                z_a[0] = quantize(to_words(rounded_a[0], PACK, ("w0", "w1"))[:], "z_a0")
+                half_products(0, 0)
+                half_products(1, 0)
+        QUARTER = HALF // 2
+        M_D = HALF + QUARTER
+        ends_b03 = laid_tile([P, 2, HALF], F32, "ends_b03", END_AT[2] - 2 * KIB)
+        first_end(ends_b03[:, 0, :], 0, HALF, HALF)
+        second_a(ROW_TILES - 1)
+        z_bf_a1 = to_words(rounded_a[1], PACK, ("w0", "w1"))
+
+        plain_b1 = end_slot(0, [P, HALF])
+        plain_first_end(plain_b1[:], 1, HALF, HALF)
+        end_b2 = end_slot(1, [P, HALF])
+        first_end(end_b2[:], 2, HALF, HALF)
+        first_end(ends_b03[:, 1, :], 3, HALF, HALF)
+        scaled_b1 = held_tile([P, HALF], F32, "scaled_b1", "rounded_a1")
+        scale_end(scaled_b1[:], plain_b1[:], 1)
+        ends_b = [ends_b03[:, 0, :], scaled_b1[:], end_b2[:], ends_b03[:, 1, :]]
+        z_a[1] = quantize(z_bf_a1[:], "z_a1")
+
+        def pair_unit(rounded, banks, a, unit_ends, unit_bonds, m0):
+            for i in range(PACK):
+                second_end(unit_bonds[i], unit_ends[i], PACK * a + i, m0, QUARTER)
+                if i % 2:
+                    tiles = [PACK * a + i - 1, PACK * a + i]
+                    sum_and_round(rounded, banks[i // 2], tiles, unit_bonds[i - 1 : i + 1], m0, 2)
+
+        after_z1 = laid_tile([P, 8, QUARTER], F32, "after_z1", END_AT[0])
+        rounded_ba = laid_tile([P, 2, K_PASS], BF16, "rounded_ba", ROUNDED_BA_AT)
+        pair_unit(rounded_ba, ("z1", "z0"), 0, [x[:, 0:QUARTER] for x in ends_b], [after_z1[:, i, :] for i in range(PACK)], HALF)
+        z_bf_ba = to_words(rounded_ba, 2, ("w0",))
+        parks = [
+            held_tile([P, 2, HALF], F32, "park0", "w1_raw2_1"),
+            held_tile([P, 2, HALF], F32, "park1", "w1_raw1_1"),
+            held_tile([P, 4, HALF], F32, "park2", "w1_raw3_0"),
+        ]
+        parked = [parks[0][:], parks[1][:], parks[2][:, 0:2], parks[2][:, 2:4]]
+        for n in range(OUT_TILES):
+            if n >= 2:
+                half_products(n, 0)
+            half_products(n, 1)
+            for j in range(2):
+                nc.scalar.copy(parked[n][:, j, :], y_a[n][j][:])
+
+        ends_c = [after_z1[:, PACK + i, :] for i in range(PACK)]
+        for i in range(PACK):
+            first_end(ends_c[i], PACK + i, HALF, QUARTER)
+        bonds_c45 = held_tile([P, 2, QUARTER], F32, "bonds_c45")
+        after_ba = laid_tile([P, 6, QUARTER], F32, "after_ba", AFTER_BA_AT + 2 * KIB)
+        bonds_c = [bonds_c45[:, 0, :], bonds_c45[:, 1, :], after_ba[:, 0, :], after_ba[:, 1, :]]
+        rounded_c = held_tile([P, 2, K_PASS], BF16, "rounded_c", "rounded_a0")
+        z_ba = quantize(z_bf_ba[:], "z_ba")
+        pair_unit(rounded_c, ("z1", "z0"), 1, ends_c, bonds_c, HALF)
+        z_bf_c = to_words(rounded_c, 2, ("w1",))
+        y_c = {}
+
+        def pair_products(j, a, z):
+            if a == 0:
+                y_c[j] = [psum.tile([P, 2, QUARTER], F32, name="y_c", tag="y%d" % (2 * j + k)) for k in range(2)]
+            for d in range(2):
+                for b in range(2):
+                    product_pass(
+                        y_c[j][0][:, d, b * P : (b + 1) * P], 2, a, 2 * j + d, z, b * P, P,
+                        a == 0 and d == 0 and b == 0, a == 1 and d == 1 and b == 1,
                     )
+            for d in range(2):
+                product_pass(y_c[j][1][:, d, :], 3, a, 2 * j + d, z, 0, QUARTER, a == 0 and d == 0, a == 1 and d == 1)
 
-        def readouts(c):
-            z_codes = ring.tile([P, P], U32, name="z_codes", align_bytes=64)
-            z_scales = ring.tile([P, P], U8, name="z_scales", align_bytes=64)
-            nc.vector.quantize_mx(out=z_codes[:].bitcast(FP8X4), scales=z_scales[:], in_=z_rounded[c][:])
-            y2 = psum.tile([P, OUT_TILES, P], F32, name="y2", bufs=Y2_BANKS)
-            y3 = psum.tile([P, OUT_TILES, P], F32, name="y3", bufs=Y3_BANKS)
-            y_banks[c] = (y2, y3)
-            products(c, 0, z0_codes[:, c * P : (c + 1) * P], z0_scales[:, c * P : (c + 1) * P])
-            products(c, 1, z_codes[:], z_scales[:])
+        for j in range(2):
+            pair_products(j, 0, z_ba)
 
-        def out_parts(c):
-            step = OUT_TILES // 2 if c == LAST else OUT_TILES
-            return [slice(n0, n0 + step) for n0 in range(0, OUT_TILES, step)]
+        rounded_bb = laid_tile([P, 2, K_PASS], BF16, "rounded_bb", ROUNDED_BB_AT)
+        pair_unit(rounded_bb, ("z0", "z1"), 0, [x[:, QUARTER:] for x in ends_b], [after_ba[:, 2 + i, :] for i in range(PACK)], M_D)
+        z_bf_bb = to_words(rounded_bb, 2, ("w0",))
+        plain_d4 = laid_tile([P, QUARTER], F32, "plain_d4", PLAIN_D4_AT)
+        plain_first_end(plain_d4[:], 4, M_D, QUARTER)
+        after_c = held_tile([P, 3, QUARTER], F32, "after_c", "rounded_a0")
+        scaled_d4 = after_c[:, 0, :]
+        scale_end(scaled_d4, plain_d4[:], 4)
+        best0 = after_c[:, 1:3, :].rearrange("p (o a) m -> p o (a m)", o=1)
+        maximum(best0, parked[0][:, 1:2, :], parked[0][:, 0:1, :], slice(0, 1), 0, HALF)
+        z_c = quantize(z_bf_c[:], "z_c", ROUNDED_BB_AT)
+        plain_d5 = laid_tile([P, QUARTER], F32, "plain_d5", PLAIN_D4_AT - KIB // 2)
+        plain_first_end(plain_d5[:], 5, M_D, QUARTER)
+        scaled_d5 = laid_tile([P, QUARTER], F32, "scaled_d5", ROUNDED_BB_AT + KIB)
+        scale_end(scaled_d5[:], plain_d5[:], 5)
+        park_c = held_tile([P, 3, 2, QUARTER], F32, "park_c", "wgs_sb")
+        for j in range(2):
+            pair_products(j, 1, z_c)
+            nc.scalar.copy(park_c[:, j], y_c[j][0][:])
+            if j == 0:
+                nc.scalar.copy(park_c[:, 2], y_c[0][1][:])
+        ends_d67 = laid_tile([P, 2, QUARTER], F32, "ends_d67", PLAIN_D4_AT + KIB // 2)
+        for t in (6, 7):
+            first_end(ends_d67[:, t - 6, :], t, M_D, QUARTER)
+        ends_d = [scaled_d4, scaled_d5[:], ends_d67[:, 0, :], ends_d67[:, 1, :]]
+        z_bb = quantize(z_bf_bb[:], "z_bb")
+        y_d = [
+            [psum.tile([P, OUT_TILES, P], F32, name="y_d", tag=tag) for tag in tags]
+            for tags in (("y0", "w1"), ("y2", "y1"))
+        ]
 
-        def copy_y2(c):
-            y2, y3 = y_banks[c]
-            if c == LAST:
-                y2_sb = held.tile([P, OUT_TILES, P], F32, name="y2_last")
+        def block_products(b, a, z, c0, order):
+            for k in order:
+                for n in range(OUT_TILES):
+                    product_pass(y_d[b][k][:, n, :], 2 + k, a, n, z, c0, P, a == 0 and n == 0, a == 1 and n == 3)
+
+        for b in range(2):
+            block_products(b, 0, z_bb, b * P, (1, 0))
+        last = laid_tile([P, 3, HALF], F32, "last", LAST_AT)
+        rounded_d = [held_tile([P, 1, K_PASS], BF16, "rounded_d0", "rounded_a1"), held_tile([P, 1, K_PASS], BF16, "rounded_d1")]
+        z_bf_d = []
+        for b in range(2):
+            bonds_d = [last[:, b, i * P : (i + 1) * P] for i in range(PACK)]
+            for i in range(PACK):
+                second_end(bonds_d[i], ends_d[i][:, b * P : (b + 1) * P], 4 + i, M_D + b * P, P)
+            if b == 0:
+                sum_and_round(rounded_d[0], "z1", [4, 5, 6, 7], bonds_d, M_D, 1)
             else:
-                y2_sb = paced_tile([P, OUT_TILES, P], F32, "y2_sb", region_of(c + 1), Y2_AT)
-            for rows in out_parts(c):
-                nc.scalar.copy(y2_sb[:, rows], y2[:, rows])
-            y_pairs[c] = (y2_sb, y3)
-
-        def store_maximum(c):
-            y2_sb, y3 = y_pairs[c]
-            if c == LATE[0]:
-                best = held.tile([P, OUT_TILES, P], F32, name="best_late", tag="z_bf_late", align_bytes=64)
-            elif c == LATE[1]:
-                best = paced_tile([P, OUT_TILES, P], F32, "best_late", region_of(LATE[0] + 1), Y2_AT)
-            elif c < LATE[0]:
-                best = ring.tile([P, OUT_TILES, P], F32, name="best", tag="h", bufs=H_BUFS)
-            else:
-                best = held.tile([P, OUT_TILES, P], F32, name="best%d" % c)
-            for rows in out_parts(c):
-                nc.vector.tensor_tensor(best[:, rows], y3[:, rows], y2_sb[:, rows], MAX)
-                nc.sync.dma_start(out_view[:, rows, c * P : (c + 1) * P], best[:, rows])
-
-        first_ends(0)
-        scale_ends(0)
-        for c in range(BLOCKS):
-            if c >= 2:
-                readouts(c - 2)
-            if c >= 3 and c - 3 not in LATE:
-                store_maximum(c - 3)
-            fused_ends(c)
-            first_ends(c + 1)
-            second_ends(c)
-            if c < LAST:
-                scale_ends(c + 1)
-            if c >= 2:
-                copy_y2(c - 2)
-            round_block(c)
-        readouts(LAST - 1)
-        copy_y2(LAST - 1)
-        for c in LATE:
-            store_maximum(c)
-        readouts(LAST)
-        copy_y2(LAST)
-        store_maximum(LAST - 1)
-        store_maximum(LAST)
+                sum_and_round(rounded_d[1], "z0", [4, 5, 6], bonds_d[0:3], M_D + P, 1)
+                sum_and_round(rounded_d[1], "z1", [7], bonds_d[3:4], M_D + P, 1)
+            z_bf_d.append(to_words(rounded_d[b], 1, ("w0",)))
+        park_d = held_tile([P, 2, OUT_TILES, P], F32, "park_d", "w1_3_codes")
+        parts = ([slice(0, 4)], [slice(0, 2), slice(2, 4)])
+        for b in range(2):
+            block_products(b, 1, quantize(z_bf_d[b][:], "z_d%d" % b), 0, (0, 1))
+            for rows in parts[b]:
+                nc.scalar.copy(park_d[:, b, rows], y_d[b][0][:, rows])
+        for rows in parts[1]:
+            maximum(park_d[:, 1, rows], y_d[1][1][:, rows], park_d[:, 1, rows], rows, M_D + P, P)
+        maximum(park_d[:, 0], y_d[0][1][:], park_d[:, 0], slice(0, 4), M_D, P)
+        later = held_tile([P, 4, HALF], F32, "later", "rounded_a1")
+        for n in range(1, OUT_TILES):
+            maximum(last[:, 2:3, :] if n == 1 else later[:, n - 2 : n - 1, :], parked[n][:, 1:2, :], parked[n][:, 0:1, :], slice(n, n + 1), 0, HALF)
+        for j in range(2):
+            best = later[:, 2 + j, :].rearrange("p (d m) -> p d m", d=2)
+            maximum(best, y_c[1][1][:] if j else park_c[:, 2], park_c[:, j], slice(2 * j, 2 * j + 2), HALF, QUARTER)

@@ -41,13 +41,11 @@ HEAD_PAGES = 2
 PAGE_AT = {t: (t - HEAD_PAGES) * PAGE_BYTES for t in range(HEAD_PAGES, ROW_TILES)}
 ROUNDED_W1_AT = {1: PAGE_AT[2], 2: PAGE_AT[4] - 2 * KIB, 3: PAGE_AT[6] - 4 * KIB}
 RAW_W1_AT = {(0, 0): PAGE_AT[2] + 2 * KIB, (0, 1): PAGE_AT[2] + 4 * KIB, (2, 0): PAGE_AT[3], (3, 1): PAGE_AT[7]}
-V_CODES_AT = PAGE_AT[7] + PAGE_BYTES + 2 * KIB
-END_AT = (V_CODES_AT + 4 * KIB, V_CODES_AT + 2 * KIB, V_CODES_AT)
-AFTER_BA_AT = V_CODES_AT + 12 * KIB
-ROUNDED_BA_AT = AFTER_BA_AT + 8 * KIB - KIB // 2
-PLAIN_D4_AT = ROUNDED_BA_AT + KIB
-LAST_AT = V_CODES_AT + 15 * KIB
-ROUNDED_BB_AT = PLAIN_D4_AT + 2 * KIB + KIB // 2
+V_CODES_AT = PAGE_AT[7] + PAGE_BYTES
+PAIR = 2 * P
+PAIRS = M // PAIR
+UNITS = 2 * PAIRS - 1
+IN_PHASE = {4: (0, 0)}
 STAGED_BUFS = 3
 BOND_BUFS = 3
 
@@ -228,10 +226,10 @@ def tile_list_garnet_bond_maximum_kernel(
         w3_codes, w3_scales = quantize_weight(
             w3_raw, held_tile([P, PASSES, N, PACK], BF16, "w3_bf16", "w1_raw3_0"), "w3"
         )
-        gain_wide = [held_tile([P, PACK, HALF], F32, "gain_wide%d" % a, "tab%d" % a) for a in range(PASSES)]
+        gain_wide = held_tile([P, ROW_TILES, PAIR], F32, "gain_wide", "tab0")
         for t in range(ROW_TILES):
             nc.scalar.activation(
-                gain_wide[t // PACK][:, t % PACK, :], wgs_sb[:, 0:HALF], IDENTITY,
+                gain_wide[:, t, :], wgs_sb[:, 0:PAIR], IDENTITY,
                 bias=gain_cols[:, t : t + 1], scale=0.0,
             )
         w2_codes = held_tile([P, PASSES, 2 * N], U8, "w2_codes")
@@ -254,7 +252,7 @@ def tile_list_garnet_bond_maximum_kernel(
         def first_end(end, t, m0, width):
             nc.vector.tensor_tensor(
                 end, pages[t][:].indirect(entries(end1_list, m0, width)),
-                gain_wide[t // PACK][:, t % PACK, 0:width], MULT,
+                gain_wide[:, t, 0:width], MULT,
             )
 
         def plain_first_end(end, t, m0, width):
@@ -287,7 +285,7 @@ def tile_list_garnet_bond_maximum_kernel(
             )
 
         def to_words(rounded, blocks, banks):
-            z_bf = ring.tile([P, blocks * K_PASS], BF16, name="z_bf", align_bytes=64)
+            z_bf = ring.tile([P, blocks * K_PASS], BF16, name="z_bf", bufs=3, align_bytes=64)
             for b0 in range(0, blocks, 2):
                 count = min(2, blocks - b0)
                 words = psum.tile([P, count, 2, P], F32, name="words", tag=banks[b0 // 2])
@@ -323,162 +321,101 @@ def tile_list_garnet_bond_maximum_kernel(
             nc.vector.tensor_tensor(best, y3, y2, MAX)
             nc.sync.dma_start(out_view[:, rows, m0 : m0 + width], best)
 
-        ends, bonds = {}, {}
+        z, z_bf, rounded, y, parked = {}, {}, {}, {}, {}
+        park_tags = ("w1_raw3_0", "tab1", "park2")
 
-        def end_slot(slot, shape):
-            return laid_tile(shape, F32, "end%d" % slot, END_AT[slot])
-
-        def ring_bond():
-            return ring.tile([P, HALF], F32, name="bond", bufs=BOND_BUFS, align_bytes=64)
-
-        rounded_a = [held_tile([P, PACK, K_PASS], BF16, "rounded_a%d" % a) for a in range(PASSES)]
-        z_a = {}
-        y_a = {}
-
-        def half_products(n, a):
+        def pair_products(j, a):
             if a == 0:
-                y_a[n] = [psum.tile([P, HALF], F32, name="y_a", tag="y%d" % (2 * (n % 2) + j)) for j in range(2)]
-            for j in range(2):
-                product_pass(y_a[n][j][:], 2 + j, a, n, z_a[a], 0, HALF, a == 0, a == PASSES - 1)
+                y[j] = [psum.tile([P, 2, PAIR], F32, name="y", tag="y%d" % k) for k in range(4)]
+                parked[j] = held_tile([P, 4, 2, PAIR], F32, "parked%d" % j, park_tags[j])
+            for half in range(2):
+                y2, y3 = y[j][2 * half], y[j][2 * half + 1]
+                for d in range(2):
+                    for c0 in (0, P):
+                        first, final = d == 0 and c0 == 0, d == 1 and c0 == P
+                        product_pass(
+                            y2[:, d, c0 : c0 + P], 2, a, 2 * half + d, z[2 * j + a], c0, P,
+                            a == 0 and first, a == 1 and final,
+                        )
+                for d in range(2):
+                    product_pass(y3[:, d, :], 3, a, 2 * half + d, z[2 * j + a], 0, PAIR, a == 0 and d == 0, a == 1 and d == 1)
+                if a == 1:
+                    nc.scalar.copy(parked[j][:, 2 * half], y2[:])
+                    if (j, half) != (PAIRS - 2, 1):
+                        nc.scalar.copy(parked[j][:, 2 * half + 1], y3[:])
 
-        def first_a(t):
-            ends[t] = end_slot(t % 3, [P, HALF])
-            first_end(ends[t][:], t, 0, HALF)
+        def pair_maximum(best, j, half):
+            y3 = y[j][3][:] if (j, half) == (PAIRS - 2, 1) else parked[j][:, 2 * half + 1]
+            maximum(best, y3, parked[j][:, 2 * half], slice(2 * half, 2 * half + 2), j * PAIR, PAIR)
 
-        def second_a(t):
-            if t == 5:
-                bonds["late"] = held_tile([P, 3, HALF], F32, "bonds_a567", "rounded_a0")
-            bond = bonds["late"][:, t - 5, :] if t >= 5 else ring_bond()[:]
-            second_end(bond, ends[t][:], t, 0, HALF)
-            sum_and_round(rounded_a[t // PACK], "z%d" % (t % 2), [t], [bond], 0, PACK)
+        def finish_unit(k):
+            z[k] = quantize(z_bf[k][:], "z%d" % k)
+            if k < UNITS - 1:
+                pair_products(k // 2, k % 2)
 
-        first_a(0)
-        for t in range(ROW_TILES - 1):
-            first_a(t + 1)
-            second_a(t)
-            if t == PACK - 1:
-                z_a[0] = quantize(to_words(rounded_a[0], PACK, ("w0", "w1"))[:], "z_a0")
-                half_products(0, 0)
-                half_products(1, 0)
-        QUARTER = HALF // 2
-        M_D = HALF + QUARTER
-        ends_b03 = laid_tile([P, 2, HALF], F32, "ends_b03", END_AT[2] - 2 * KIB)
-        first_end(ends_b03[:, 0, :], 0, HALF, HALF)
-        second_a(ROW_TILES - 1)
-        z_bf_a1 = to_words(rounded_a[1], PACK, ("w0", "w1"))
+        def new_ends():
+            three = laid_tile([P, 3, PAIR], F32, "ends_three", V_CODES_AT + 4 * KIB)
+            one = laid_tile([P, PAIR], F32, "ends_one", V_CODES_AT + 7 * KIB)
+            return [three[:, 0, :], three[:, 1, :], three[:, 2, :], one[:]]
 
-        plain_b1 = end_slot(0, [P, HALF])
-        plain_first_end(plain_b1[:], 1, HALF, HALF)
-        end_b2 = end_slot(1, [P, HALF])
-        first_end(end_b2[:], 2, HALF, HALF)
-        first_end(ends_b03[:, 1, :], 3, HALF, HALF)
-        scaled_b1 = held_tile([P, HALF], F32, "scaled_b1", "rounded_a1")
-        scale_end(scaled_b1[:], plain_b1[:], 1)
-        ends_b = [ends_b03[:, 0, :], scaled_b1[:], end_b2[:], ends_b03[:, 1, :]]
-        z_a[1] = quantize(z_bf_a1[:], "z_a1")
-
-        def pair_unit(rounded, banks, a, unit_ends, unit_bonds, m0):
+        for k in range(UNITS):
+            a, m0 = k % 2, k // 2 * PAIR
+            ends = new_ends()
+            first_end(ends[0], PACK * a, m0, PAIR)
+            if k >= 2:
+                finish_unit(k - 2)
+            for i in range(1, PACK):
+                first_end(ends[i], PACK * a + i, m0, PAIR)
+            early = ring.tile([P, 2, PAIR], F32, name="early_bonds", align_bytes=64)
+            late = held_tile([P, 4, PAIR], F32, "late_bonds", "rounded%d" % ((k - 1) % 3))
+            bonds = [early[:, 0, :], early[:, 1, :], late[:, 0, :], late[:, 1, :]]
+            rounded[k] = held_tile([P, 2, K_PASS], BF16, "rounded", "rounded%d" % (k % 3))
             for i in range(PACK):
-                second_end(unit_bonds[i], unit_ends[i], PACK * a + i, m0, QUARTER)
+                if i == 2 and k in IN_PHASE:
+                    pair_maximum(late[:, 2:4, :], *IN_PHASE[k])
+                second_end(bonds[i], ends[i], PACK * a + i, m0, PAIR)
                 if i % 2:
                     tiles = [PACK * a + i - 1, PACK * a + i]
-                    sum_and_round(rounded, banks[i // 2], tiles, unit_bonds[i - 1 : i + 1], m0, 2)
+                    sum_and_round(rounded[k], "z%d" % ((k + i // 2) % 2), tiles, bonds[i - 1 : i + 1], m0, 2)
+            z_bf[k] = to_words(rounded[k], 2, ("w0",))
 
-        after_z1 = laid_tile([P, 8, QUARTER], F32, "after_z1", END_AT[0])
-        rounded_ba = laid_tile([P, 2, K_PASS], BF16, "rounded_ba", ROUNDED_BA_AT)
-        pair_unit(rounded_ba, ("z1", "z0"), 0, [x[:, 0:QUARTER] for x in ends_b], [after_z1[:, i, :] for i in range(PACK)], HALF)
-        z_bf_ba = to_words(rounded_ba, 2, ("w0",))
-        parks = [
-            held_tile([P, 2, HALF], F32, "park0", "w1_raw2_1"),
-            held_tile([P, 2, HALF], F32, "park1", "w1_raw1_1"),
-            held_tile([P, 4, HALF], F32, "park2", "w1_raw3_0"),
-        ]
-        parked = [parks[0][:], parks[1][:], parks[2][:, 0:2], parks[2][:, 2:4]]
-        for n in range(OUT_TILES):
-            if n >= 2:
-                half_products(n, 0)
-            half_products(n, 1)
-            for j in range(2):
-                nc.scalar.copy(parked[n][:, j, :], y_a[n][j][:])
-
-        ends_c = [after_z1[:, PACK + i, :] for i in range(PACK)]
+        M_D = M - PAIR
+        three = laid_tile([P, 3, PAIR], F32, "ends_three", V_CODES_AT + 4 * KIB)
+        plain = laid_tile([P, PAIR], F32, "ends_one", V_CODES_AT + 7 * KIB)
+        first_end(three[:, 0, :], 4, M_D, PAIR)
+        finish_unit(UNITS - 2)
+        plain_first_end(plain[:], 7, M_D, PAIR)
+        scaled = [held_tile([P, P], F32, "scaled6"), held_tile([P, P], F32, "scaled7", "rounded%d" % ((UNITS - 1) % 3))]
+        scale_end(scaled[0][:], plain[:, 0:P], 7)
+        for i in (1, 2):
+            first_end(three[:, i, :], 4 + i, M_D, PAIR)
+        rounded_d = [held_tile([P, 1, K_PASS], BF16, "rounded_d%d" % b) for b in range(2)]
+        bonds6 = held_tile([P, PACK, P], F32, "bonds6")
         for i in range(PACK):
-            first_end(ends_c[i], PACK + i, HALF, QUARTER)
-        bonds_c45 = held_tile([P, 2, QUARTER], F32, "bonds_c45")
-        after_ba = laid_tile([P, 6, QUARTER], F32, "after_ba", AFTER_BA_AT + 2 * KIB)
-        bonds_c = [bonds_c45[:, 0, :], bonds_c45[:, 1, :], after_ba[:, 0, :], after_ba[:, 1, :]]
-        rounded_c = held_tile([P, 2, K_PASS], BF16, "rounded_c", "rounded_a0")
-        z_ba = quantize(z_bf_ba[:], "z_ba")
-        pair_unit(rounded_c, ("z1", "z0"), 1, ends_c, bonds_c, HALF)
-        z_bf_c = to_words(rounded_c, 2, ("w1",))
-        y_c = {}
-
-        def pair_products(j, a, z):
-            if a == 0:
-                y_c[j] = [psum.tile([P, 2, QUARTER], F32, name="y_c", tag="y%d" % (2 * j + k)) for k in range(2)]
-            for d in range(2):
-                for b in range(2):
-                    product_pass(
-                        y_c[j][0][:, d, b * P : (b + 1) * P], 2, a, 2 * j + d, z, b * P, P,
-                        a == 0 and d == 0 and b == 0, a == 1 and d == 1 and b == 1,
-                    )
-            for d in range(2):
-                product_pass(y_c[j][1][:, d, :], 3, a, 2 * j + d, z, 0, QUARTER, a == 0 and d == 0, a == 1 and d == 1)
-
-        for j in range(2):
-            pair_products(j, 0, z_ba)
-
-        rounded_bb = laid_tile([P, 2, K_PASS], BF16, "rounded_bb", ROUNDED_BB_AT)
-        pair_unit(rounded_bb, ("z0", "z1"), 0, [x[:, QUARTER:] for x in ends_b], [after_ba[:, 2 + i, :] for i in range(PACK)], M_D)
-        z_bf_bb = to_words(rounded_bb, 2, ("w0",))
-        plain_d4 = laid_tile([P, QUARTER], F32, "plain_d4", PLAIN_D4_AT)
-        plain_first_end(plain_d4[:], 4, M_D, QUARTER)
-        after_c = held_tile([P, 3, QUARTER], F32, "after_c", "rounded_a0")
-        scaled_d4 = after_c[:, 0, :]
-        scale_end(scaled_d4, plain_d4[:], 4)
-        best0 = after_c[:, 1:3, :].rearrange("p (o a) m -> p o (a m)", o=1)
-        maximum(best0, parked[0][:, 1:2, :], parked[0][:, 0:1, :], slice(0, 1), 0, HALF)
-        z_c = quantize(z_bf_c[:], "z_c", ROUNDED_BB_AT)
-        plain_d5 = laid_tile([P, QUARTER], F32, "plain_d5", PLAIN_D4_AT - KIB // 2)
-        plain_first_end(plain_d5[:], 5, M_D, QUARTER)
-        scaled_d5 = laid_tile([P, QUARTER], F32, "scaled_d5", ROUNDED_BB_AT + KIB)
-        scale_end(scaled_d5[:], plain_d5[:], 5)
-        park_c = held_tile([P, 3, 2, QUARTER], F32, "park_c", "wgs_sb")
-        for j in range(2):
-            pair_products(j, 1, z_c)
-            nc.scalar.copy(park_c[:, j], y_c[j][0][:])
-            if j == 0:
-                nc.scalar.copy(park_c[:, 2], y_c[0][1][:])
-        ends_d67 = laid_tile([P, 2, QUARTER], F32, "ends_d67", PLAIN_D4_AT + KIB // 2)
-        for t in (6, 7):
-            first_end(ends_d67[:, t - 6, :], t, M_D, QUARTER)
-        ends_d = [scaled_d4, scaled_d5[:], ends_d67[:, 0, :], ends_d67[:, 1, :]]
-        z_bb = quantize(z_bf_bb[:], "z_bb")
+            second_end(bonds6[:, i, :], three[:, i, 0:P] if i < 3 else scaled[0][:], 4 + i, M_D, P)
+        sum_and_round(rounded_d[0], "z1", [4, 5, 6, 7], [bonds6[:, i, :] for i in range(PACK)], M_D, 1)
+        z_bf_d = [to_words(rounded_d[0], 1, ("w0",))]
+        scale_end(scaled[1][:], plain[:, P:], 7)
+        finish_unit(UNITS - 1)
         y_d = [
             [psum.tile([P, OUT_TILES, P], F32, name="y_d", tag=tag) for tag in tags]
             for tags in (("y0", "w1"), ("y2", "y1"))
         ]
 
-        def block_products(b, a, z, c0, order):
+        def block_products(b, a, z_block, c0, order):
             for k in order:
                 for n in range(OUT_TILES):
-                    product_pass(y_d[b][k][:, n, :], 2 + k, a, n, z, c0, P, a == 0 and n == 0, a == 1 and n == 3)
+                    product_pass(y_d[b][k][:, n, :], 2 + k, a, n, z_block, c0, P, a == 0 and n == 0, a == 1 and n == 3)
 
-        for b in range(2):
-            block_products(b, 0, z_bb, b * P, (1, 0))
-        last = laid_tile([P, 3, HALF], F32, "last", LAST_AT)
-        rounded_d = [held_tile([P, 1, K_PASS], BF16, "rounded_d0", "rounded_a1"), held_tile([P, 1, K_PASS], BF16, "rounded_d1")]
-        z_bf_d = []
-        for b in range(2):
-            bonds_d = [last[:, b, i * P : (i + 1) * P] for i in range(PACK)]
-            for i in range(PACK):
-                second_end(bonds_d[i], ends_d[i][:, b * P : (b + 1) * P], 4 + i, M_D + b * P, P)
-            if b == 0:
-                sum_and_round(rounded_d[0], "z1", [4, 5, 6, 7], bonds_d, M_D, 1)
-            else:
-                sum_and_round(rounded_d[1], "z0", [4, 5, 6], bonds_d[0:3], M_D + P, 1)
-                sum_and_round(rounded_d[1], "z1", [7], bonds_d[3:4], M_D + P, 1)
-            z_bf_d.append(to_words(rounded_d[b], 1, ("w0",)))
+        block_products(0, 0, z[UNITS - 1], 0, (1, 0))
+        last = laid_tile([P, 2, HALF], F32, "last", V_CODES_AT + 7 * KIB)
+        bonds7 = [last[:, 0, i * P : (i + 1) * P] for i in range(PACK)]
+        for i in range(PACK):
+            second_end(bonds7[i], three[:, i, P:] if i < 3 else scaled[1][:], 4 + i, M_D + P, P)
+        sum_and_round(rounded_d[1], "z0", [4, 5, 6], bonds7[0:3], M_D + P, 1)
+        sum_and_round(rounded_d[1], "z1", [7], bonds7[3:4], M_D + P, 1)
+        z_bf_d.append(to_words(rounded_d[1], 1, ("w0",)))
+        block_products(1, 0, z[UNITS - 1], P, (1, 0))
         park_d = held_tile([P, 2, OUT_TILES, P], F32, "park_d", "w1_3_codes")
         parts = ([slice(0, 4)], [slice(0, 2), slice(2, 4)])
         for b in range(2):
@@ -488,9 +425,8 @@ def tile_list_garnet_bond_maximum_kernel(
         for rows in parts[1]:
             maximum(park_d[:, 1, rows], y_d[1][1][:, rows], park_d[:, 1, rows], rows, M_D + P, P)
         maximum(park_d[:, 0], y_d[0][1][:], park_d[:, 0], slice(0, 4), M_D, P)
-        later = held_tile([P, 4, HALF], F32, "later", "rounded_a1")
-        for n in range(1, OUT_TILES):
-            maximum(last[:, 2:3, :] if n == 1 else later[:, n - 2 : n - 1, :], parked[n][:, 1:2, :], parked[n][:, 0:1, :], slice(n, n + 1), 0, HALF)
-        for j in range(2):
-            best = later[:, 2 + j, :].rearrange("p (d m) -> p d m", d=2)
-            maximum(best, y_c[1][1][:] if j else park_c[:, 2], park_c[:, j], slice(2 * j, 2 * j + 2), HALF, QUARTER)
+        left = [(j, half) for j in range(PAIRS - 1) for half in range(2) if (j, half) not in IN_PHASE.values()]
+        pair_maximum(last[:, 1, :].rearrange("p (d m) -> p d m", d=2), *left[0])
+        later = held_tile([P, len(left) - 1, 2, PAIR], F32, "later", "rounded_d0")
+        for n, (j, half) in enumerate(left[1:]):
+            pair_maximum(later[:, n], j, half)

@@ -36,16 +36,19 @@ FIRST = 256
 HALF = M // 2
 KIB = 1024
 PAGE_BYTES = T2 * 4
-HEAD_PAGES = 2
+HEAD_PAGES = 1
 
 PAGE_AT = {t: (t - HEAD_PAGES) * PAGE_BYTES for t in range(HEAD_PAGES, ROW_TILES)}
-ROUNDED_W1_AT = {1: PAGE_AT[2], 2: PAGE_AT[4] - 2 * KIB, 3: PAGE_AT[6] - 4 * KIB}
-RAW_W1_AT = {(0, 0): PAGE_AT[2] + 2 * KIB, (0, 1): PAGE_AT[2] + 4 * KIB, (2, 0): PAGE_AT[3], (3, 1): PAGE_AT[7]}
+ROUNDED_W1_AT = {1: PAGE_AT[1], 2: PAGE_AT[3] - 2 * KIB, 3: PAGE_AT[5] - 4 * KIB}
+RAW_W1_AT = {
+    (0, 0): PAGE_AT[1] + 2 * KIB, (0, 1): PAGE_AT[1] + 4 * KIB, (2, 0): PAGE_AT[2], (3, 1): PAGE_AT[7] - 4 * KIB,
+}
 V_CODES_AT = PAGE_AT[7] + PAGE_BYTES
 PAIR = 2 * P
 PAIRS = M // PAIR
-UNITS = 2 * PAIRS - 1
-IN_PHASE = {4: (0, 0)}
+UNITS = ((0, 0, 2 * PAIR), (1, 0, PAIR), (1, PAIR, PAIR), (0, 2 * PAIR, PAIR), (1, 2 * PAIR, PAIR), (0, 3 * PAIR, PAIR))
+FINAL = len(UNITS) - 1
+PRODUCTS_AFTER = (((0, 0),), ((0, 1), (1, 0)), ((1, 1),), ((2, 0),), ((2, 1),), ())
 STAGED_BUFS = 3
 BOND_BUFS = 3
 
@@ -162,6 +165,9 @@ def tile_list_garnet_bond_maximum_kernel(
         angle_banks = ["y0", "y1", "y2", "y3"]
 
         def sines(h, t, j0, width):
+            nc.scalar.activation(h, angles_of(t, j0, width)[:], SIN)
+
+        def angles_of(t, j0, width):
             piece = max(x for x in range(len(W1_WIDTHS)) if w1_starts[x] <= t * P)
             codes, scales = w1_q[piece]
             angle_banks.append(angle_banks.pop(0))
@@ -177,7 +183,7 @@ def tile_list_garnet_bond_maximum_kernel(
                     start=(a == 0),
                     stop=(a == PASSES - 1),
                 )
-            nc.scalar.activation(h, angles[:], SIN)
+            return angles
 
         def scatter(h, t, j0, width):
             nc.vector.tensor_tensor(
@@ -193,22 +199,37 @@ def tile_list_garnet_bond_maximum_kernel(
         sines(h_first[:], 0, 0, FIRST)
         scatter(h_first[:], 0, 0, FIRST)
         quantize_w1(1)
-        zero_page(2)
+        zero_page(1)
         h_rest = held_tile([P, S - FIRST], F32, "h_rest", "w1_raw1_1")
         sines(h_rest[:, 0:FIRST], 0, FIRST, FIRST)
         sines(h_rest[:, FIRST:], 0, BANK, BANK)
         scatter(h_rest[:], 0, FIRST, S - FIRST)
         quantize_w1(2)
+        zero_page(2)
         zero_page(3)
-        zero_page(4)
         sines_to_page(1, held_tile([P, S], F32, "h1", "w1_raw2_1"))
         quantize_w1(3)
         zero_page(5)
-        zero_page(6)
-        sines_to_page(2, laid_tile([P, S], F32, "h2", PAGE_AT[7]))
+        zero_page(4)
+        sines_to_page(2, laid_tile([P, S], F32, "h2", PAGE_AT[7] - 2 * KIB))
         zero_page(7)
+        zero_page(6)
+        held_angles = []
         for t in range(3, ROW_TILES):
-            sines_to_page(t, held_tile([P, S], F32, "h%d" % t, "w1_raw1_1" if t % 2 else "w1_raw2_1"))
+            if t == ROW_TILES - 2:
+                h = laid_tile([P, S], F32, "h%d" % t, V_CODES_AT + 4 * KIB)
+                for j0 in range(0, S, BANK):
+                    held_angles.append(angles_of(t, j0, BANK))
+                for j0 in range(0, S, BANK):
+                    held_angles.append(angles_of(t + 1, j0, BANK))
+            else:
+                h = held_tile([P, S], F32, "h%d" % t, "w1_raw1_1" if t % 2 else "w1_raw2_1")
+            if t >= ROW_TILES - 2:
+                for j0 in range(0, S, BANK):
+                    nc.scalar.activation(h[:, j0 : j0 + BANK], held_angles.pop(0)[:], SIN)
+                scatter(h[:], t, 0, S)
+            else:
+                sines_to_page(t, h)
 
         end1_list = load_list("end1_list", offs3)
         end2_list = load_list("end2_list", offs4)
@@ -226,10 +247,10 @@ def tile_list_garnet_bond_maximum_kernel(
         w3_codes, w3_scales = quantize_weight(
             w3_raw, held_tile([P, PASSES, N, PACK], BF16, "w3_bf16", "w1_raw3_0"), "w3"
         )
-        gain_wide = held_tile([P, ROW_TILES, PAIR], F32, "gain_wide", "tab0")
+        gain_wide = [held_tile([P, PACK, HALF if a == 0 else PAIR], F32, "gain_wide%d" % a, "tab0" if a == 0 else None) for a in range(PASSES)]
         for t in range(ROW_TILES):
             nc.scalar.activation(
-                gain_wide[:, t, :], wgs_sb[:, 0:PAIR], IDENTITY,
+                gain_wide[t // PACK][:, t % PACK, :], wgs_sb[:, 0 : HALF if t < PACK else PAIR], IDENTITY,
                 bias=gain_cols[:, t : t + 1], scale=0.0,
             )
         w2_codes = held_tile([P, PASSES, 2 * N], U8, "w2_codes")
@@ -252,7 +273,7 @@ def tile_list_garnet_bond_maximum_kernel(
         def first_end(end, t, m0, width):
             nc.vector.tensor_tensor(
                 end, pages[t][:].indirect(entries(end1_list, m0, width)),
-                gain_wide[:, t, 0:width], MULT,
+                gain_wide[t // PACK][:, t % PACK, 0:width], MULT,
             )
 
         def plain_first_end(end, t, m0, width):
@@ -328,17 +349,19 @@ def tile_list_garnet_bond_maximum_kernel(
             if a == 0:
                 y[j] = [psum.tile([P, 2, PAIR], F32, name="y", tag="y%d" % k) for k in range(4)]
                 parked[j] = held_tile([P, 4, 2, PAIR], F32, "parked%d" % j, park_tags[j])
+            k = max(x for x, (ua, um, uw) in enumerate(UNITS) if ua == a and um <= j * PAIR)
+            z_unit, z0 = z[k], j * PAIR - UNITS[k][1]
             for half in range(2):
                 y2, y3 = y[j][2 * half], y[j][2 * half + 1]
                 for d in range(2):
                     for c0 in (0, P):
                         first, final = d == 0 and c0 == 0, d == 1 and c0 == P
                         product_pass(
-                            y2[:, d, c0 : c0 + P], 2, a, 2 * half + d, z[2 * j + a], c0, P,
+                            y2[:, d, c0 : c0 + P], 2, a, 2 * half + d, z_unit, z0 + c0, P,
                             a == 0 and first, a == 1 and final,
                         )
                 for d in range(2):
-                    product_pass(y3[:, d, :], 3, a, 2 * half + d, z[2 * j + a], 0, PAIR, a == 0 and d == 0, a == 1 and d == 1)
+                    product_pass(y3[:, d, :], 3, a, 2 * half + d, z_unit, z0, PAIR, a == 0 and d == 0, a == 1 and d == 1)
                 if a == 1:
                     nc.scalar.copy(parked[j][:, 2 * half], y2[:])
                     if (j, half) != (PAIRS - 2, 1):
@@ -350,53 +373,54 @@ def tile_list_garnet_bond_maximum_kernel(
 
         def finish_unit(k):
             z[k] = quantize(z_bf[k][:], "z%d" % k)
-            if k < UNITS - 1:
-                pair_products(k // 2, k % 2)
+            for j, a in PRODUCTS_AFTER[k]:
+                pair_products(j, a)
 
-        def new_ends():
-            three = laid_tile([P, 3, PAIR], F32, "ends_three", V_CODES_AT + 4 * KIB)
-            one = laid_tile([P, PAIR], F32, "ends_one", V_CODES_AT + 7 * KIB)
+        def new_ends(width):
+            three = laid_tile([P, 3, width], F32, "ends_three", V_CODES_AT)
+            one = laid_tile([P, width], F32, "ends_one", V_CODES_AT + 6 * KIB)
             return [three[:, 0, :], three[:, 1, :], three[:, 2, :], one[:]]
 
-        for k in range(UNITS):
-            a, m0 = k % 2, k // 2 * PAIR
-            ends = new_ends()
-            first_end(ends[0], PACK * a, m0, PAIR)
-            if k >= 2:
-                finish_unit(k - 2)
-            for i in range(1, PACK):
-                first_end(ends[i], PACK * a + i, m0, PAIR)
-            early = ring.tile([P, 2, PAIR], F32, name="early_bonds", align_bytes=64)
-            late = held_tile([P, 4, PAIR], F32, "late_bonds", "rounded%d" % ((k - 1) % 3))
+        for k, (a, m0, width) in enumerate(UNITS):
+            blocks = width // P
+            group = PACK // blocks
+            ends = new_ends(width)
+            for n, i in enumerate((2, 0, 1, 3)):
+                first_end(ends[i], PACK * a + i, m0, width)
+                if n == 0 and k >= 2:
+                    finish_unit(k - 2)
+            early = ring.tile([P, 2, width], F32, name="early_bonds", align_bytes=64)
+            late = held_tile([P, 2, width], F32, "late_bonds", "rounded%d" % ((k - 1) % 2))
             bonds = [early[:, 0, :], early[:, 1, :], late[:, 0, :], late[:, 1, :]]
-            rounded[k] = held_tile([P, 2, K_PASS], BF16, "rounded", "rounded%d" % (k % 3))
+            rounded[k] = held_tile([P, blocks, K_PASS], BF16, "rounded", "rounded%d" % (k % 2))
             for i in range(PACK):
-                if i == 2 and k in IN_PHASE:
-                    pair_maximum(late[:, 2:4, :], *IN_PHASE[k])
-                second_end(bonds[i], ends[i], PACK * a + i, m0, PAIR)
-                if i % 2:
-                    tiles = [PACK * a + i - 1, PACK * a + i]
-                    sum_and_round(rounded[k], "z%d" % ((k + i // 2) % 2), tiles, bonds[i - 1 : i + 1], m0, 2)
-            z_bf[k] = to_words(rounded[k], 2, ("w0",))
+                second_end(bonds[i], ends[i], PACK * a + i, m0, width)
+                if (i + 1) % group == 0:
+                    tiles = [PACK * a + x for x in range(i + 1 - group, i + 1)]
+                    bank = "z%d" % ((k + i // group) % 2)
+                    sum_and_round(rounded[k], bank, tiles, bonds[i + 1 - group : i + 1], m0, blocks)
+            z_bf[k] = to_words(rounded[k], blocks, ("w0", "w1"))
 
         M_D = M - PAIR
-        three = laid_tile([P, 3, PAIR], F32, "ends_three", V_CODES_AT + 4 * KIB)
-        plain = laid_tile([P, PAIR], F32, "ends_one", V_CODES_AT + 7 * KIB)
+        three = laid_tile([P, 3, PAIR], F32, "ends_three", V_CODES_AT)
+        plain = laid_tile([P, PAIR], F32, "ends_one", V_CODES_AT + 6 * KIB)
         first_end(three[:, 0, :], 4, M_D, PAIR)
-        finish_unit(UNITS - 2)
+        finish_unit(FINAL - 1)
         plain_first_end(plain[:], 7, M_D, PAIR)
-        scaled = [held_tile([P, P], F32, "scaled6"), held_tile([P, P], F32, "scaled7", "rounded%d" % ((UNITS - 1) % 3))]
+        scaled = [held_tile([P, P], F32, "scaled6"), held_tile([P, P], F32, "scaled7", "rounded%d" % (FINAL % 2))]
         scale_end(scaled[0][:], plain[:, 0:P], 7)
         for i in (1, 2):
             first_end(three[:, i, :], 4 + i, M_D, PAIR)
+        best_in_phase = held_tile([P, 2, PAIR], F32, "best_in_phase", "rounded%d" % ((FINAL - 1) % 2))
+        pair_maximum(best_in_phase[:], 0, 0)
         rounded_d = [held_tile([P, 1, K_PASS], BF16, "rounded_d%d" % b) for b in range(2)]
         bonds6 = held_tile([P, PACK, P], F32, "bonds6")
         for i in range(PACK):
             second_end(bonds6[:, i, :], three[:, i, 0:P] if i < 3 else scaled[0][:], 4 + i, M_D, P)
-        sum_and_round(rounded_d[0], "z1", [4, 5, 6, 7], [bonds6[:, i, :] for i in range(PACK)], M_D, 1)
+        sum_and_round(rounded_d[0], "z0", [4, 5, 6, 7], [bonds6[:, i, :] for i in range(PACK)], M_D, 1)
         z_bf_d = [to_words(rounded_d[0], 1, ("w0",))]
         scale_end(scaled[1][:], plain[:, P:], 7)
-        finish_unit(UNITS - 1)
+        finish_unit(FINAL)
         y_d = [
             [psum.tile([P, OUT_TILES, P], F32, name="y_d", tag=tag) for tag in tags]
             for tags in (("y0", "w1"), ("y2", "y1"))
@@ -407,15 +431,15 @@ def tile_list_garnet_bond_maximum_kernel(
                 for n in range(OUT_TILES):
                     product_pass(y_d[b][k][:, n, :], 2 + k, a, n, z_block, c0, P, a == 0 and n == 0, a == 1 and n == 3)
 
-        block_products(0, 0, z[UNITS - 1], 0, (1, 0))
-        last = laid_tile([P, 2, HALF], F32, "last", V_CODES_AT + 7 * KIB)
+        block_products(0, 0, z[FINAL], 0, (1, 0))
+        last = laid_tile([P, 2, HALF], F32, "last", V_CODES_AT + 6 * KIB)
         bonds7 = [last[:, 0, i * P : (i + 1) * P] for i in range(PACK)]
         for i in range(PACK):
             second_end(bonds7[i], three[:, i, P:] if i < 3 else scaled[1][:], 4 + i, M_D + P, P)
-        sum_and_round(rounded_d[1], "z0", [4, 5, 6], bonds7[0:3], M_D + P, 1)
-        sum_and_round(rounded_d[1], "z1", [7], bonds7[3:4], M_D + P, 1)
+        sum_and_round(rounded_d[1], "z1", [4, 5, 6], bonds7[0:3], M_D + P, 1)
+        sum_and_round(rounded_d[1], "z0", [7], bonds7[3:4], M_D + P, 1)
         z_bf_d.append(to_words(rounded_d[1], 1, ("w0",)))
-        block_products(1, 0, z[UNITS - 1], P, (1, 0))
+        block_products(1, 0, z[FINAL], P, (1, 0))
         park_d = held_tile([P, 2, OUT_TILES, P], F32, "park_d", "w1_3_codes")
         parts = ([slice(0, 4)], [slice(0, 2), slice(2, 4)])
         for b in range(2):
@@ -425,7 +449,7 @@ def tile_list_garnet_bond_maximum_kernel(
         for rows in parts[1]:
             maximum(park_d[:, 1, rows], y_d[1][1][:, rows], park_d[:, 1, rows], rows, M_D + P, P)
         maximum(park_d[:, 0], y_d[0][1][:], park_d[:, 0], slice(0, 4), M_D, P)
-        left = [(j, half) for j in range(PAIRS - 1) for half in range(2) if (j, half) not in IN_PHASE.values()]
+        left = [(j, half) for j in range(PAIRS - 1) for half in range(2) if (j, half) != (0, 0)]
         pair_maximum(last[:, 1, :].rearrange("p (d m) -> p d m", d=2), *left[0])
         later = held_tile([P, len(left) - 1, 2, PAIR], F32, "later", "rounded_d0")
         for n, (j, half) in enumerate(left[1:]):

@@ -103,9 +103,9 @@ def tile_list_garnet_bond_maximum_kernel(
 
         tab_plane = held.tile([P, T], U8, name="tab_plane")
         nc.vector.memset(tab_plane[:].bitcast(I32), 0)
-        spin_list = load_list("spin_list", offs)
         tab = [held_tile([P, T], I32, "tab%d" % a) for a in range(PASSES)]
         nc.sync.dma_start(tab[0][:], tab_words[0].rearrange("p t i -> p (t i)").bitcast(I32))
+        spin_list = load_list("spin_list", offs)
         for q in range(4):
             nc.sync.dma_start(
                 tab_plane[32 * q : 32 * q + 4 * PASSES, :].bitcast(I32),
@@ -390,10 +390,12 @@ def tile_list_garnet_bond_maximum_kernel(
                 if n == 0 and k >= 2:
                     finish_unit(k - 2)
             early = ring.tile([P, 2, width], F32, name="early_bonds", align_bytes=64)
-            late = held_tile([P, 2, width], F32, "late_bonds", "rounded%d" % ((k - 1) % 2))
+            late = held_tile([P, 4 if k == FINAL - 1 else 2, width], F32, "late_bonds", "rounded%d" % ((k - 1) % 3))
             bonds = [early[:, 0, :], early[:, 1, :], late[:, 0, :], late[:, 1, :]]
-            rounded[k] = held_tile([P, blocks, K_PASS], BF16, "rounded", "rounded%d" % (k % 2))
+            rounded[k] = held_tile([P, blocks, K_PASS], BF16, "rounded", "rounded%d" % (k % 3))
             for i in range(PACK):
+                if i == 2 and k == FINAL - 1:
+                    pair_maximum(late[:, 2:4, :], 0, 1)
                 second_end(bonds[i], ends[i], PACK * a + i, m0, width)
                 if (i + 1) % group == 0:
                     tiles = [PACK * a + x for x in range(i + 1 - group, i + 1)]
@@ -407,11 +409,11 @@ def tile_list_garnet_bond_maximum_kernel(
         first_end(three[:, 0, :], 4, M_D, PAIR)
         finish_unit(FINAL - 1)
         plain_first_end(plain[:], 7, M_D, PAIR)
-        scaled = [held_tile([P, P], F32, "scaled6"), held_tile([P, P], F32, "scaled7", "rounded%d" % (FINAL % 2))]
+        scaled = [held_tile([P, P], F32, "scaled6"), held_tile([P, P], F32, "scaled7", "rounded%d" % (FINAL % 3))]
         scale_end(scaled[0][:], plain[:, 0:P], 7)
         for i in (1, 2):
             first_end(three[:, i, :], 4 + i, M_D, PAIR)
-        best_in_phase = held_tile([P, 2, PAIR], F32, "best_in_phase", "rounded%d" % ((FINAL - 1) % 2))
+        best_in_phase = held_tile([P, 2, PAIR], F32, "best_in_phase", "rounded%d" % ((FINAL - 1) % 3))
         pair_maximum(best_in_phase[:], 0, 0)
         rounded_d = [held_tile([P, 1, K_PASS], BF16, "rounded_d%d" % b) for b in range(2)]
         bonds6 = held_tile([P, PACK, P], F32, "bonds6")
@@ -449,7 +451,7 @@ def tile_list_garnet_bond_maximum_kernel(
         for rows in parts[1]:
             maximum(park_d[:, 1, rows], y_d[1][1][:, rows], park_d[:, 1, rows], rows, M_D + P, P)
         maximum(park_d[:, 0], y_d[0][1][:], park_d[:, 0], slice(0, 4), M_D, P)
-        left = [(j, half) for j in range(PAIRS - 1) for half in range(2) if (j, half) != (0, 0)]
+        left = [(j, half) for j in range(PAIRS - 1) for half in range(2) if j != 0]
         pair_maximum(last[:, 1, :].rearrange("p (d m) -> p d m", d=2), *left[0])
         later = held_tile([P, len(left) - 1, 2, PAIR], F32, "later", "rounded_d0")
         for n, (j, half) in enumerate(left[1:]):

@@ -49,7 +49,7 @@ PAIRS = M // PAIR
 UNITS = ((0, 0, 2 * PAIR), (1, 0, PAIR), (1, PAIR, PAIR), (0, 2 * PAIR, PAIR), (1, 2 * PAIR, PAIR), (0, 3 * PAIR, PAIR))
 FINAL = len(UNITS) - 1
 PRODUCTS_AFTER = (((0, 0),), ((0, 1), (1, 0)), ((1, 1),), ((2, 0),), ((2, 1),), ())
-STAGED_BUFS = 3
+STAGED_BUFS = 2
 BOND_BUFS = 3
 
 
@@ -128,8 +128,10 @@ def tile_list_garnet_bond_maximum_kernel(
         nc.sync.dma_start(tab[1][:], tab_words[1].rearrange("p t i -> p (t i)").bitcast(I32))
         site_list = load_list("site_list", offs2)
         wgs_sb = held_tile([P, S], F32, "wgs_sb")
-        nc.sync.dma_start(wgs_sb[:], wgs)
-        for piece in range(1, len(W1_WIDTHS)):
+        nc.sync.dma_start(wgs_sb[:, 0:FIRST], wgs[:, 0:FIRST])
+        load_w1(1)
+        nc.sync.dma_start(wgs_sb[:, FIRST:], wgs[:, FIRST:])
+        for piece in range(2, len(W1_WIDTHS)):
             load_w1(piece)
 
         identity = held.tile([P, P], F32, name="identity")
@@ -261,14 +263,12 @@ def tile_list_garnet_bond_maximum_kernel(
                 w2_plane[32 * q : 32 * q + 4].bitcast(I32),
                 w2_scales[:, 4 * q : 4 * q + 4, :].rearrange("a r n -> r a n").bitcast(I32),
             )
-        an = {}
+        an_low = held_tile([P, PACK, M], F32, "an_low")
+        nc.sync.dma_start(an_low[:], aniso[0:K_PASS, :].rearrange("(i p) m -> p i m", p=P))
+        an = {(0, m0): an_low[:, :, m0 : m0 + HALF] for m0 in (0, HALF)}
         for m0 in (0, HALF):
-            for a in range(PASSES):
-                an[a, m0] = staged("an")
-                nc.sync.dma_start(
-                    an[a, m0][:],
-                    aniso[a * K_PASS : (a + 1) * K_PASS, m0 : m0 + HALF].rearrange("(i p) m -> p i m", p=P),
-                )
+            an[1, m0] = staged("an")
+            nc.sync.dma_start(an[1, m0][:], aniso[K_PASS:, m0 : m0 + HALF].rearrange("(i p) m -> p i m", p=P))
 
         def first_end(end, t, m0, width):
             nc.vector.tensor_tensor(

from contextlib import ExitStack

import concourse.mybir as mybir
from concourse.masks import make_identity

K, H, N, T, S, T2, M = 1024, 1024, 512, 2048, 1024, 2048, 1024
FLOPS = 2 * K * H * S + 2 * 2 * H * N * M

F32 = mybir.dt.float32
BF16 = mybir.dt.bfloat16
I32 = mybir.dt.int32
U32 = mybir.dt.uint32
U16 = mybir.dt.uint16
U8 = mybir.dt.uint8
FP8X4 = mybir.dt.float8_e4m3fn_x4
FP4X4 = mybir.dt.float4_e2m1fn_x4
MULT = mybir.AluOpType.mult
MAX = mybir.AluOpType.max
COPY = mybir.ActivationFunctionType.Copy
IDENTITY = mybir.ActivationFunctionType.Identity
SIN = mybir.ActivationFunctionType.Sin

P = 128
PACK = 4
K_PASS = P * PACK
PASSES = 2
BANK = 512
ROW_TILES = H // P
OUT_TILES = N // P
BLOCKS = M // P
LAST = BLOCKS - 1
PAGES = PACK

W1_WIDTHS = (128, 128, 256, 512)
FIRST = 256
HALF = M // 2
KIB = 1024
PAGE_BYTES = T2 * 4
HEAD_PAGES = 1

PAGE_AT = {t: (t - HEAD_PAGES) * PAGE_BYTES for t in range(HEAD_PAGES, ROW_TILES)}
ROUNDED_W1_AT = {1: PAGE_AT[1], 2: PAGE_AT[3] - 2 * KIB, 3: PAGE_AT[5] - 4 * KIB}
RAW_W1_AT = {
    (0, 0): PAGE_AT[1] + 2 * KIB, (0, 1): PAGE_AT[1] + 4 * KIB, (2, 0): PAGE_AT[2], (3, 1): PAGE_AT[7] - 4 * KIB,
}
V_CODES_AT = PAGE_AT[7] + PAGE_BYTES
PAIR = 2 * P
PAIRS = M // PAIR
UNITS = ((0, 0, 2 * PAIR), (1, 0, PAIR), (1, PAIR, PAIR), (0, 2 * PAIR, PAIR), (1, 2 * PAIR, PAIR), (0, 3 * PAIR, PAIR))
FINAL = len(UNITS) - 1
PRODUCTS_AFTER = (((0, 0),), ((0, 1), (1, 0)), ((1, 1),), ((2, 0),), ((2, 1),), ())
STAGED_BUFS = 2
BOND_BUFS = 3


def tile_list_garnet_bond_maximum_kernel(
    tc, tab_words, tab_scales, offs, offs2, offs3, offs4, w1, wgs, gain, aniso, w2_words, w2_scales, w3, out
):
    nc = tc.nc
    with ExitStack() as ctx:
        held = ctx.enter_context(tc.tile_pool(name="held", bufs=1))
        ring = ctx.enter_context(tc.tile_pool(name="ring", bufs=2))
        laid = ctx.enter_context(tc.tile_pool(name="laid", bufs=1))
        psum = ctx.enter_context(tc.psum_pool(name="psum", bufs=1))

        def load_list(name, dram):
            tile = held.tile([P, S // 16], U16, name=name)
            nc.sync.dma_start(tile[:], dram)
            return tile

        def entries(tile, start, count):
            return tile[:, start // 16 : (start + count) // 16]

        def laid_tile(shape, dtype, name, offset):
            return laid.tile(shape, dtype, name=name, offset=offset, align_bytes=64)

        def held_tile(shape, dtype, name, tag=None):
            return held.tile(shape, dtype, name=name, tag=tag or name, align_bytes=64)

        def load_rows(raw, w, a, c0, width):
            nc.sync.dma_start(
                raw[:], w[a * K_PASS : (a + 1) * K_PASS, c0 : c0 + width].rearrange("(p i) c -> p i c", i=PACK)
            )
            return raw

        def quantize(bf16_values, name, codes_at=None):
            width = bf16_values.shape[1] // PACK
            if codes_at is None:
                codes = held_tile([P, width], U32, name + "_codes")
            else:
                codes = laid_tile([P, width], U32, name + "_codes", codes_at)
            scales = held_tile([P, width], U8, name + "_scales")
            nc.vector.quantize_mx(out=codes[:].bitcast(FP8X4), scales=scales[:], in_=bf16_values)
            return codes, scales

        def quantize_weight(raws, grouped, name):
            for a in range(PASSES):
                nc.scalar.copy(
                    grouped[:, a].rearrange("p (c q) i -> p c i q", q=4),
                    raws[a][:].rearrange("p i (c q) -> p c i q", q=4),
                )
            return quantize(grouped[:].rearrange("p a c i -> p (a c i)"), name)

        tab_plane = held.tile([P, T], U8, name="tab_plane")
        nc.vector.memset(tab_plane[:].bitcast(I32), 0)
        tab = [held_tile([P, T], I32, "tab%d" % a) for a in range(PASSES)]
        nc.sync.dma_start(tab[0][:], tab_words[0].rearrange("p t i -> p (t i)").bitcast(I32))
        spin_list = load_list("spin_list", offs)
        for q in range(4):
            nc.sync.dma_start(
                tab_plane[32 * q : 32 * q + 4 * PASSES, :].bitcast(I32),
                tab_scales[:, 4 * q : 4 * q + 4, :].bitcast(I32),
            )
        w1_starts = [sum(W1_WIDTHS[:piece]) for piece in range(len(W1_WIDTHS))]
        w1_raw = {}

        def load_w1(piece):
            w1_raw[piece] = []
            for a in range(PASSES):
                shape, name = [P, PACK, W1_WIDTHS[piece]], "w1_raw%d_%d" % (piece, a)
                if (piece, a) in RAW_W1_AT:
                    raw = laid_tile(shape, F32, name, RAW_W1_AT[piece, a])
                else:
                    raw = held_tile(shape, F32, name)
                w1_raw[piece].append(load_rows(raw, w1, a, w1_starts[piece], W1_WIDTHS[piece]))

        load_w1(0)
        nc.sync.dma_start(tab[1][:], tab_words[1].rearrange("p t i -> p (t i)").bitcast(I32))
        site_list = load_list("site_list", offs2)
        wgs_sb = held_tile([P, S], F32, "wgs_sb")
        nc.sync.dma_start(wgs_sb[:, 0:FIRST], wgs[:, 0:FIRST])
        load_w1(1)
        nc.sync.dma_start(wgs_sb[:, FIRST:], wgs[:, FIRST:])
        for piece in range(2, len(W1_WIDTHS)):
            load_w1(piece)

        identity = held.tile([P, P], F32, name="identity")
        make_identity(nc, identity[:])
        pages = {t: held.tile([P, T2], F32, name="page%d" % t) for t in range(HEAD_PAGES)}
        for t in range(HEAD_PAGES):
            nc.vector.memset(pages[t][:].bitcast(I32), 0)

        def zero_page(t):
            pages[t] = laid_tile([P, T2], F32, "page%d" % t, PAGE_AT[t])
            nc.gpsimd.memset(pages[t][:].bitcast(I32), 0)

        v_scales = held_tile([P, S], U8, "v_scales")
        v_codes = [laid_tile([P, S], U32, "v_codes%d" % a, V_CODES_AT + a * 4 * KIB) for a in range(PASSES)]
        nc.vector.tensor_copy(v_codes[0][:], tab[0][:].bitcast(U32).indirect(spin_list[:]))
        nc.vector.tensor_copy(v_scales[:], tab_plane[:].indirect(spin_list[:]))
        w1_q = {}

        def quantize_w1(piece):
            shape, name = [P, PASSES, W1_WIDTHS[piece], PACK], "w1_%d" % piece
            if piece in ROUNDED_W1_AT:
                grouped = laid_tile(shape, BF16, name + "_bf16", ROUNDED_W1_AT[piece])
            else:
                grouped = held_tile(shape, BF16, name + "_bf16")
            w1_q[piece] = quantize_weight(w1_raw[piece], grouped, name)

        quantize_w1(0)
        for j0, width in ((0, FIRST), (FIRST, S - FIRST)):
            nc.vector.tensor_copy(
                v_codes[1][:, j0 : j0 + width], tab[1][:].bitcast(U32).indirect(entries(spin_list, j0, width))
            )

        angle_banks = ["y0", "y1", "y2", "y3"]

        def sines(h, t, j0, width):
            nc.scalar.activation(h, angles_of(t, j0, width)[:], SIN)

        def angles_of(t, j0, width):
            piece = max(x for x in range(len(W1_WIDTHS)) if w1_starts[x] <= t * P)
            codes, scales = w1_q[piece]
            angle_banks.append(angle_banks.pop(0))
            angles = psum.tile([P, width], F32, name="angles", tag=angle_banks[-1])
            for a in range(PASSES):
                col = a * W1_WIDTHS[piece] + t * P - w1_starts[piece]
                nc.tensor.matmul_mx(
                    out=angles[:],
                    lhsT=codes[:, col : col + P].bitcast(FP8X4),
                    lhsT_scale=scales[:, col : col + P],
                    rhs=v_codes[a][:, j0 : j0 + width].bitcast(FP8X4),
                    rhs_scale=v_scales[4 * a :, j0 : j0 + width],
                    start=(a == 0),
                    stop=(a == PASSES - 1),
                )
            return angles

        def scatter(h, t, j0, width):
            nc.vector.tensor_tensor(
                pages[t][:].indirect(entries(site_list, j0, width)), h, wgs_sb[:, j0 : j0 + width], MULT
            )

        def sines_to_page(t, h):
            for j0 in range(0, S, BANK):
                sines(h[:, j0 : j0 + BANK], t, j0, BANK)
            scatter(h[:], t, 0, S)

        h_first = held_tile([P, FIRST], F32, "h_first")
        sines(h_first[:], 0, 0, FIRST)
        scatter(h_first[:], 0, 0, FIRST)
        quantize_w1(1)
        zero_page(1)
        h_rest = held_tile([P, S - FIRST], F32, "h_rest", "w1_raw1_1")
        sines(h_rest[:, 0:FIRST], 0, FIRST, FIRST)
        sines(h_rest[:, FIRST:], 0, BANK, BANK)
        scatter(h_rest[:], 0, FIRST, S - FIRST)
        quantize_w1(2)
        zero_page(2)
        zero_page(3)
        sines_to_page(1, held_tile([P, S], F32, "h1", "w1_raw2_1"))
        quantize_w1(3)
        zero_page(5)
        zero_page(4)
        sines_to_page(2, laid_tile([P, S], F32, "h2", PAGE_AT[7] - 2 * KIB))
        zero_page(7)
        zero_page(6)
        held_angles = []
        for t in range(3, ROW_TILES):
            if t == ROW_TILES - 2:
                h = laid_tile([P, S], F32, "h%d" % t, V_CODES_AT + 4 * KIB)
                for j0 in range(0, S, BANK):
                    held_angles.append(angles_of(t, j0, BANK))
                for j0 in range(0, S, BANK):
                    held_angles.append(angles_of(t + 1, j0, BANK))
            else:
                h = held_tile([P, S], F32, "h%d" % t, "w1_raw1_1" if t % 2 else "w1_raw2_1")
            if t >= ROW_TILES - 2:
                for j0 in range(0, S, BANK):
                    nc.scalar.activation(h[:, j0 : j0 + BANK], held_angles.pop(0)[:], SIN)
                scatter(h[:], t, 0, S)
            else:
                sines_to_page(t, h)

        end1_list = load_list("end1_list", offs3)
        end2_list = load_list("end2_list", offs4)
        gain_rows = w1_raw[1][0][:, 0, :]
        nc.sync.dma_start(gain_rows[0:ROW_TILES, :], gain.rearrange("(t p) -> t p", p=P))
        gain_psum = psum.tile([P, P], F32, name="gain_psum", tag="w0")
        nc.tensor.transpose(gain_psum[:], gain_rows, identity[:])
        gain_cols = held.tile([P, ROW_TILES], F32, name="gain_cols")
        nc.scalar.copy(gain_cols[:], gain_psum[:, 0:ROW_TILES])

        def staged(name):
            return ring.tile([P, PACK, BANK], F32, name=name, tag="staged", bufs=STAGED_BUFS, align_bytes=64)

        w3_raw = [load_rows(staged("w3_raw"), w3, a, 0, N) for a in range(PASSES)]
        w3_codes, w3_scales = quantize_weight(
            w3_raw, held_tile([P, PASSES, N, PACK], BF16, "w3_bf16", "w1_raw3_0"), "w3"
        )
        gain_wide = [held_tile([P, PACK, HALF if a == 0 else PAIR], F32, "gain_wide%d" % a, "tab0" if a == 0 else None) for a in range(PASSES)]
        for t in range(ROW_TILES):
            nc.scalar.activation(
                gain_wide[t // PACK][:, t % PACK, :], wgs_sb[:, 0 : HALF if t < PACK else PAIR], IDENTITY,
                bias=gain_cols[:, t : t + 1], scale=0.0,
            )
        w2_codes = held_tile([P, PASSES, 2 * N], U8, "w2_codes")
        nc.sync.dma_start(w2_codes[:].bitcast(I32), w2_words.rearrange("a p b -> p a b").bitcast(I32))
        w2_plane = w1_q[3][1][:].rearrange("p (a n) -> p a n", a=PASSES)
        for q in range(4):
            nc.sync.dma_start(
                w2_plane[32 * q : 32 * q + 4].bitcast(I32),
                w2_scales[:, 4 * q : 4 * q + 4, :].rearrange("a r n -> r a n").bitcast(I32),
            )
        an_low = held_tile([P, PACK, M], F32, "an_low")
        nc.sync.dma_start(an_low[:], aniso[0:K_PASS, :].rearrange("(i p) m -> p i m", p=P))
        an = {(0, m0): an_low[:, :, m0 : m0 + HALF] for m0 in (0, HALF)}
        for m0 in (0, HALF):
            an[1, m0] = staged("an")
            nc.sync.dma_start(an[1, m0][:], aniso[K_PASS:, m0 : m0 + HALF].rearrange("(i p) m -> p i m", p=P))

        def first_end(end, t, m0, width):
            nc.vector.tensor_tensor(
                end, pages[t][:].indirect(entries(end1_list, m0, width)),
                gain_wide[t // PACK][:, t % PACK, 0:width], MULT,
            )

        def plain_first_end(end, t, m0, width):
            nc.vector.tensor_copy(end, pages[t][:].indirect(entries(end1_list, m0, width)))

        def scale_end(scaled, end, t):
            nc.scalar.activation(scaled, end, COPY, scale=gain_cols[:, t : t + 1])

        def second_end(bond, end, t, m0, width):
            nc.vector.tensor_tensor(bond, pages[t][:].indirect(entries(end2_list, m0, width)), end, MULT)

        def sum_and_round(rounded, bank, tiles, bonds, m0, blocks):
            a, count = tiles[0] // PACK, len(tiles)
            zt = psum.tile([P, blocks, count, P], F32, name="zt", tag=bank)
            aniso_half = an[a, m0 // HALF * HALF]
            terms = []
            for b in range(blocks):
                c0 = m0 % HALF + b * P
                terms.extend((b, j, aniso_half[:, t % PACK, c0 : c0 + P]) for j, t in enumerate(tiles))
            for j in range(count):
                terms.extend((b, j, bonds[j][:, b * P : (b + 1) * P]) for b in range(blocks))
            for n, (b, j, term) in enumerate(terms):
                nc.tensor.matmul(
                    zt[:, b, j, :], term, identity[:], start=(n == 0), stop=(n == len(terms) - 1), is_transpose=True
                )
            p0 = 32 * (tiles[0] % PACK)
            nc.scalar.copy(
                rounded[:].rearrange("m b (u p e) -> m b u p e", u=2, e=2)[:, :, :, p0 : p0 + 32 * count, :],
                zt[:].rearrange("m b j r -> m b (j r)").rearrange("m b (p u e) -> m b u p e", u=2, e=2),
            )

        def to_words(rounded, blocks, banks):
            z_bf = ring.tile([P, blocks * K_PASS], BF16, name="z_bf", bufs=3, align_bytes=64)
            for b0 in range(0, blocks, 2):
                count = min(2, blocks - b0)
                words = psum.tile([P, count, 2, P], F32, name="words", tag=banks[b0 // 2])
                for b in range(count):
                    for u in range(2):
                        nc.tensor.transpose(
                            words[:, b, u, :], rounded[:, b0 + b, :].bitcast(F32)[:, u * P : (u + 1) * P], identity[:]
                        )
                nc.scalar.copy(
                    z_bf[:, b0 * K_PASS : (b0 + count) * K_PASS].bitcast(F32).rearrange(
                        "p (b m u) -> p b m u", b=count, u=2
                    ),
                    words[:].rearrange("p b u m -> p b m u"),
                )
            return z_bf

        def product_pass(y, which, a, n, z, c0, width, start, stop):
            codes, scales = z
            if which == 2:
                lhs = w2_codes[:, a, 2 * n * P : 2 * (n + 1) * P].bitcast(FP4X4)
                lhs_scale = w2_plane[:, a, n * P : (n + 1) * P]
            else:
                lhs = w3_codes[:, a * N + n * P : a * N + (n + 1) * P].bitcast(FP8X4)
                lhs_scale = w3_scales[:, a * N + n * P : a * N + (n + 1) * P]
            nc.tensor.matmul_mx(
                out=y, lhsT=lhs, lhsT_scale=lhs_scale, rhs=codes[:, c0 : c0 + width].bitcast(FP8X4),
                rhs_scale=scales[:, c0 : c0 + width], start=start, stop=stop,
            )

        out_view = out.rearrange("(t p) m -> p t m", p=P)

        def maximum(best, y3, y2, rows, m0, width):
            nc.vector.tensor_tensor(best, y3, y2, MAX)
            nc.sync.dma_start(out_view[:, rows, m0 : m0 + width], best)

        z, z_bf, rounded, y, parked = {}, {}, {}, {}, {}
        park_tags = ("w1_raw3_0", "tab1", "park2")

        def pair_products(j, a):
            if a == 0:
                y[j] = [psum.tile([P, 2, PAIR], F32, name="y", tag="y%d" % k) for k in range(4)]
                parked[j] = held_tile([P, 4, 2, PAIR], F32, "parked%d" % j, park_tags[j])
            k = max(x for x, (ua, um, uw) in enumerate(UNITS) if ua == a and um <= j * PAIR)
            z_unit, z0 = z[k], j * PAIR - UNITS[k][1]
            for half in range(2):
                y2, y3 = y[j][2 * half], y[j][2 * half + 1]
                for d in range(2):
                    for c0 in (0, P):
                        first, final = d == 0 and c0 == 0, d == 1 and c0 == P
                        product_pass(
                            y2[:, d, c0 : c0 + P], 2, a, 2 * half + d, z_unit, z0 + c0, P,
                            a == 0 and first, a == 1 and final,
                        )
                for d in range(2):
                    product_pass(y3[:, d, :], 3, a, 2 * half + d, z_unit, z0, PAIR, a == 0 and d == 0, a == 1 and d == 1)
                if a == 1:
                    nc.scalar.copy(parked[j][:, 2 * half], y2[:])
                    if (j, half) != (PAIRS - 2, 1):
                        nc.scalar.copy(parked[j][:, 2 * half + 1], y3[:])

        def pair_maximum(best, j, half):
            y3 = y[j][3][:] if (j, half) == (PAIRS - 2, 1) else parked[j][:, 2 * half + 1]
            maximum(best, y3, parked[j][:, 2 * half], slice(2 * half, 2 * half + 2), j * PAIR, PAIR)

        def finish_unit(k):
            z[k] = quantize(z_bf[k][:], "z%d" % k)
            for j, a in PRODUCTS_AFTER[k]:
                pair_products(j, a)

        def new_ends(width):
            three = laid_tile([P, 3, width], F32, "ends_three", V_CODES_AT)
            one = laid_tile([P, width], F32, "ends_one", V_CODES_AT + 6 * KIB)
            return [three[:, 0, :], three[:, 1, :], three[:, 2, :], one[:]]

        for k, (a, m0, width) in enumerate(UNITS):
            blocks = width // P
            group = PACK // blocks
            ends = new_ends(width)
            for n, i in enumerate((2, 0, 1, 3)):
                first_end(ends[i], PACK * a + i, m0, width)
                if n == 0 and k >= 2:
                    finish_unit(k - 2)
            early = ring.tile([P, 2, width], F32, name="early_bonds", align_bytes=64)
            late = held_tile([P, 4 if k == FINAL - 1 else 2, width], F32, "late_bonds", "rounded%d" % ((k - 1) % 3))
            bonds = [early[:, 0, :], early[:, 1, :], late[:, 0, :], late[:, 1, :]]
            rounded[k] = held_tile([P, blocks, K_PASS], BF16, "rounded", "rounded%d" % (k % 3))
            for i in range(PACK):
                if i == 2 and k == FINAL - 1:
                    pair_maximum(late[:, 2:4, :], 0, 1)
                second_end(bonds[i], ends[i], PACK * a + i, m0, width)
                if (i + 1) % group == 0:
                    tiles = [PACK * a + x for x in range(i + 1 - group, i + 1)]
                    bank = "z%d" % ((k + i // group) % 2)
                    sum_and_round(rounded[k], bank, tiles, bonds[i + 1 - group : i + 1], m0, blocks)
            z_bf[k] = to_words(rounded[k], blocks, ("w0", "w1"))

        M_D = M - PAIR
        three = laid_tile([P, 3, PAIR], F32, "ends_three", V_CODES_AT)
        plain = laid_tile([P, PAIR], F32, "ends_one", V_CODES_AT + 6 * KIB)
        first_end(three[:, 0, :], 4, M_D, PAIR)
        finish_unit(FINAL - 1)
        plain_first_end(plain[:], 7, M_D, PAIR)
        scaled = [held_tile([P, P], F32, "scaled6"), held_tile([P, P], F32, "scaled7", "rounded%d" % (FINAL % 3))]
        scale_end(scaled[0][:], plain[:, 0:P], 7)
        for i in (1, 2):
            first_end(three[:, i, :], 4 + i, M_D, PAIR)
        best_in_phase = held_tile([P, 2, PAIR], F32, "best_in_phase", "rounded%d" % ((FINAL - 1) % 3))
        pair_maximum(best_in_phase[:], 0, 0)
        rounded_d = [held_tile([P, 1, K_PASS], BF16, "rounded_d%d" % b) for b in range(2)]
        bonds6 = held_tile([P, PACK, P], F32, "bonds6")
        for i in range(PACK):
            second_end(bonds6[:, i, :], three[:, i, 0:P] if i < 3 else scaled[0][:], 4 + i, M_D, P)
        sum_and_round(rounded_d[0], "z0", [4, 5, 6, 7], [bonds6[:, i, :] for i in range(PACK)], M_D, 1)
        z_bf_d = [to_words(rounded_d[0], 1, ("w0",))]
        scale_end(scaled[1][:], plain[:, P:], 7)
        finish_unit(FINAL)
        y_d = [
            [psum.tile([P, OUT_TILES, P], F32, name="y_d", tag=tag) for tag in tags]
            for tags in (("y0", "w1"), ("y2", "y1"))
        ]

        def block_products(b, a, z_block, c0, order):
            for k in order:
                for n in range(OUT_TILES):
                    product_pass(y_d[b][k][:, n, :], 2 + k, a, n, z_block, c0, P, a == 0 and n == 0, a == 1 and n == 3)

        block_products(0, 0, z[FINAL], 0, (1, 0))
        last = laid_tile([P, 2, HALF], F32, "last", V_CODES_AT + 6 * KIB)
        bonds7 = [last[:, 0, i * P : (i + 1) * P] for i in range(PACK)]
        for i in range(PACK):
            second_end(bonds7[i], three[:, i, P:] if i < 3 else scaled[1][:], 4 + i, M_D + P, P)
        sum_and_round(rounded_d[1], "z1", [4, 5, 6], bonds7[0:3], M_D + P, 1)
        sum_and_round(rounded_d[1], "z0", [7], bonds7[3:4], M_D + P, 1)
        z_bf_d.append(to_words(rounded_d[1], 1, ("w0",)))
        block_products(1, 0, z[FINAL], P, (1, 0))
        park_d = held_tile([P, 2, OUT_TILES, P], F32, "park_d", "w1_3_codes")
        parts = ([slice(0, 4)], [slice(0, 2), slice(2, 4)])
        for b in range(2):
            block_products(b, 1, quantize(z_bf_d[b][:], "z_d%d" % b), 0, (0, 1))
            for rows in parts[b]:
                nc.scalar.copy(park_d[:, b, rows], y_d[b][0][:, rows])
        for rows in parts[1]:
            maximum(park_d[:, 1, rows], y_d[1][1][:, rows], park_d[:, 1, rows], rows, M_D + P, P)
        maximum(park_d[:, 0], y_d[0][1][:], park_d[:, 0], slice(0, 4), M_D, P)
        left = [(j, half) for j in range(PAIRS - 1) for half in range(2) if j != 0]
        pair_maximum(last[:, 1, :].rearrange("p (d m) -> p d m", d=2), *left[0])
        later = held_tile([P, len(left) - 1, 2, PAIR], F32, "later", "rounded_d0")
        for n, (j, half) in enumerate(left[1:]):
            pair_maximum(later[:, n], j, half)
